import numpy as np, ml_dtypes
CORES = [3,7,11,15,131,135,139,143]
N = 8
import mx_ref
BF = ml_dtypes.bfloat16
def gcols(t, e):
    v = np.concatenate([t.reshape(8, 16, -1, 4), np.zeros((8, 16, 1, 4), BF)], axis=2)
    return np.ascontiguousarray(np.stack([v[g][:, e[g]] for g in range(8)])).reshape(128, -1)
def tile(rs):
    return np.stack(rs, axis=2).reshape(128, -1).astype(BF)
def pick(q, e):
    c = np.concatenate([q[0].reshape(128, -1, 4), np.zeros((128, 1, 4), np.uint8)], axis=1); s = np.concatenate([q[1], np.ones((16, 1), np.uint8)], axis=1)
    return (np.ascontiguousarray(c[:, e].reshape(128, -1)), np.ascontiguousarray(s[:, e]))
def join(*qs):
    return (np.concatenate([q[0] for q in qs], axis=1), np.concatenate([q[1] for q in qs], axis=1))
def put(q, e, v):
    c, s = q[0].reshape(128, -1, 4).copy(), q[1].copy(); c[:, e] = v[0].reshape(128, -1, 4); s[:, e] = v[1]
    return (c.reshape(128, -1), s)
def pk(c, s):
    return (np.ascontiguousarray(c), mx_ref.live(s))
def emit(q):
    return q[0], q[1]
def packed(v, rng):
    q = [mx_ref.quantize(np.ascontiguousarray(v[r])) for r in range(N)]
    return np.stack([a for a, b in q]), np.stack([mx_ref.plane(b, rng) for a, b in q])
def values_of_codes():
    e, c = np.zeros((128, 128, 4), np.float32), np.zeros((128, 2, 4), np.uint8)
    e[np.arange(128), np.arange(128), 0] = 1
    c[:127, :, 0] = np.arange(256).reshape(2, 128).T[:127]
    return mx_ref.matmul(mx_ref.quantize(e.reshape(128, 512).astype(BF)), (c.reshape(128, 8), np.full((16, 2), 127, np.uint8))).T.reshape(-1).astype(np.float64)
CODE_VALUE, SCALE_VALUE = values_of_codes(), 2.0 ** (np.arange(256) - 127.0)
def decode(q):
    return (CODE_VALUE[q[0]].reshape(16, 8, -1, 4) * SCALE_VALUE[q[1]][:, None, :, None] + 0.0).reshape(128, -1).astype(np.float32)
def f(rng, *shape):
    return mx_ref.flush((rng.standard_normal(shape, dtype=np.float32) * np.exp2(rng.integers(-2, 3, shape[:-1] + (1,)))).astype(BF))
def wide(rng, *shape, cols=0):
    v = rng.standard_normal(shape, dtype=np.float32) * np.exp2(rng.integers(-12, 13, shape)).astype(np.float32)
    if cols: v *= np.repeat(np.exp2(rng.integers(-cols, cols + 1, shape[:-2] + (1, shape[-1] // 4))) * (rng.random(shape[:-2] + (1, shape[-1] // 4)) > 0.0625), 4, axis=-1).astype(np.float32)
    return mx_ref.flush(v.astype(BF))
C, K, R = 320, 44, 3
H = C // 2
STEP = [1, 2, 4]
def partner(r, t):
    return r ^ STEP[t]
def chains(sl, sr, f):
    a = np.flatnonzero(np.concatenate([[0], f[:-1]]) == 0)
    b = np.flatnonzero(f == 0)
    at = np.stack([a, b], axis=1).reshape(-1)
    o = np.argsort(-(np.stack([sl[a], sr[b]], axis=1).reshape(-1) + np.float32(0.0)), kind="stable")
    own = np.arange(len(a))
    near = [[k - 1 if k > 0 and f[k - 1] else -1, k + 1 if f[k] else -1] for k in range(C)]
    for i in range(K):
        d, e = int(o[2 * i]), int(o[2 * i + 1])
        if own[d // 2] != own[e // 2]:
            own[own == own[e // 2]] = own[d // 2]
            near[at[d]][d % 2], near[at[e]][e % 2] = int(at[e]), int(at[d])
    ways, seen = [], set()
    for k in range(C):
        if min(near[k]) < 0 and k not in seen:
            way, came = [k], -1
            while True:
                on = [j for j in near[way[-1]] if j >= 0 and j != came]
                if not on: break
                came = way[-1]
                way.append(on[0])
            seen.update((way[0], way[-1]))
            ways.append(way)
    ways.sort(key=min)
    return np.concatenate(ways), np.concatenate([[1] * (len(way) - 1) + [0] for way in ways])
def numbers_of(rng):
    return {"x": np.array(f(rng, N, 128, 4 * C)), "u": np.array(f(rng, N, 128, 512)), "v": np.array(f(rng, N, 128, 512))}
def weights(rng, w):
    c, p = packed(w, rng)
    return {"wc": c, "ws": p}
def layer(rng):
    w = np.array(f(rng, N, 128, 2048)).reshape(N, 8, 16, 4, 8, 16, 4)
    w[:, :, :, :, :, 8:] = 0
    w[:, :, :, :, :, 0] = 0
    return weights(rng, w.reshape(N, 128, 2048))
def signs(rng):
    k = np.stack([rng.permutation(8) % 4 for r in range(N)])
    return np.stack([k % 2, k // 2], axis=2) * 2.0 - 1.0
def digits(s):
    b = ((s[..., None] >> np.arange(8)) & 1) * np.exp2(np.arange(8.0))
    return b.reshape(N, 8, C, 2, 4).transpose(0, 1, 3, 2, 4)
def own_part(u, k):
    k = k.astype(np.float32).astype(BF)
    u = u.reshape(N, 8, 16, 128, 4)
    u[:, :, :, ::16] = 0
    u[:, :, :, 1::16] = 0
    for g in range(8):
        for s in range(2):
            u[:, g, 0, 16 * g + s, s] = k
            u[:, g, 8 + 2 * s:10 + 2 * s, 16 * g + s] = k[:, None, None]
    return u.reshape(N, 128, 512)
def setup_inputs(rng):
    return {**numbers_of(rng), **weights(rng, f(rng, N, 128, 2048))}
def setup_inputs_ties(rng):
    d = numbers_of(rng)
    e = rng.permutation(N)
    x = d["x"].reshape(N, 8, 16, C, 4)
    for r in range(N):
        k = np.zeros(C, int) if r == e[0] else rng.permutation(C) % 3
        a = x[r][:, :8, :3].copy()
        a[:, :, 2] = 0
        x[r][:, :8] = a[:, :, k]
    x[e[1]] = 0
    u = d["u"].reshape(N, 8, 16, 128, 4)
    u[:, :, 8:, ::16] = 0
    u[:, :, 8:, 1::16] = 0
    w = np.array(f(rng, N, 128, 2048)).reshape(N, 8, 16, 4, 8, 16, 4)
    w[:, :, 8:, :, :, :8] = 0
    return {"x": x.reshape(N, 128, 4 * C), "u": u.reshape(N, 128, 512), "v": d["v"], **weights(rng, w.reshape(N, 128, 2048))}
def setup_inputs_near(rng):
    d = numbers_of(rng)
    x = d["x"].astype(np.float32).reshape(N, 8, 16, C, 4)
    c = np.arange(C)
    x[:, :, 0] = 0
    x[:, :, 0, :, :2] = signs(rng)[:, :, None]
    x[:, :, 8:10] = digits(np.tile(C // 2 - 1 - (C - 1 - c) // 3, (N, 8, 1))) * 2.0 ** -23
    x[:, :, 10:12] = digits((c // 2 + rng.integers(0, C // 2, (N, 8, 1))) % (C // 2)) * 2.0 ** -23
    x[:, :, 12:] = rng.integers(4, 8, (N, 8, 4, C, 4)) * rng.choice([-1.0, 1.0], (N, 8, 4, C, 4)) * 2.0 ** -20
    k = np.where(rng.permutation(N) < N // 2, 2.0 ** -30, 1.0)
    return {"x": x.reshape(N, 128, 4 * C).astype(BF), "u": own_part(d["u"], k), "v": d["v"], **layer(rng)}
def setup_inputs_loops(rng):
    d = numbers_of(rng)
    s = np.zeros((N, 8, C, 2), int)
    q = int(rng.integers(8))
    for r in range(N):
        kind = np.insert(rng.permutation(7) % 5, q, 5)
        for g in range(8):
            if g == q:
                if r & STEP[1]:
                    s[r, g, H + 1:H + 3 * K - 2, 0] = 3
                    s[r, g, H:H + 3 * K - 3, 1] = 3
                    s[r, g, H, 0] = 2
                    s[r, g, H + 3 * K - 2, 0] = 1
                else:
                    s[r, g, 3:2 * K + 3, 0] = 3
                    s[r, g, 2:2 * K + 2, 1] = 3
                    s[r, g, 2, 0] = 2
                    s[r, g, 2 * K + 2, 1] = 2
                    s[r, g, 0] = (2, 1)
                continue
            left, e, free = K, [], rng.permutation(C)
            while left:
                n, closed = ((K, 1), (K, 0), (int(rng.integers(1, 4)), 1), (int(rng.integers(1, 8)), int(rng.integers(2))), (1, 1))[kind[g]]
                n = min(n, left)
                m = n + 1 - closed
                c, free = free[:m], free[m:]
                side = rng.integers(0, 2, m)
                e += [(c[j], side[j], c[(j + 1) % m], 1 - side[(j + 1) % m]) for j in range(n)]
                left -= n
            e = np.array(e)
            i = K - rng.permutation(K)
            s[r, g, e[:, 0], e[:, 1]] = i
            s[r, g, e[:, 2], e[:, 3]] = i
    tiny = rng.permutation(N) < N // 2
    size = np.where(tiny[:, None] | (np.arange(8) == q), 2.0 ** -27, 2.0 ** -4)[:, :, None, None, None]
    x = d["x"].astype(np.float32).reshape(N, 8, 16, C, 4)
    x[:, :, 0] = 0
    x[:, :, 8:10] = digits(s[..., 0]) * size
    x[:, :, 10:12] = digits(s[..., 1]) * size
    x[:, :, 12:] = rng.integers(4, 8, (N, 8, 4, C, 4)) * rng.choice([-1.0, 1.0], (N, 8, 4, C, 4)) * size
    return {"x": x.reshape(N, 128, 4 * C).astype(BF), "u": own_part(d["u"], np.where(tiny, 2.0 ** -30, 1.0)), "v": d["v"], **layer(rng)}
def setup_inputs_huge(rng):
    d = numbers_of(rng)
    x = 2.0 ** 30 * (0.45 + 0.15 * rng.random((N, 128, C, 4)))
    for r in range(N):
        x[r][:, rng.permutation(C)[:8]] = 2.0 ** 30 * (0.76 + 0.04 * rng.random((128, 8, 4)))
    u = d["u"].reshape(N, 128, 8, 16, 4)
    u[:, :, :, :2] = (2.0 ** 30 * (1 - 0.25 * rng.random((N, 128, 8, 2, 4))) * signs(rng)[:, None, :, :, None]).astype(np.float32).astype(BF)
    w = mx_ref.flush((f(rng, N, 128, 2048).astype(np.float32) * np.float32(2.0 ** -6)).astype(BF))
    return {"x": x.astype(np.float32).reshape(N, 128, 4 * C).astype(BF), "u": u.reshape(N, 128, 512), "v": d["v"], **weights(rng, w)}
def setup_inputs_spread(rng):
    d = setup_inputs(rng)
    d["x"] = wide(rng, N, 128, 4 * C, cols=6)
    return d
def check_inputs(d):
    b = []
    for k in ("x", "u", "v"):
        a = np.abs(d[k].astype(np.float32))
        if not (np.isfinite(a).all() and ((a == 0) | (a >= 2.0 ** -30) & (a <= 2.0 ** 30)).all()): b.append("a value of " + k)
    if ((d["wc"] & 127) == 127).any(): b.append("a code of wc")
    for r in range(N):
        s = mx_ref.live(d["ws"][r]).astype(int)
        if ((s > 1) & (np.abs(s - 127) > 46)).any(): b.append("a scale of ws")
    return b
def reference(x, u, v, wc, ws):
    qu = [mx_ref.quantize(u[r]) for r in range(N)]
    lay = [pk(wc[r], ws[r]) for r in range(N)]
    now = [x[r] for r in range(N)]
    flag = [np.zeros((8, C), np.int64) for r in range(N)]
    for t in range(R):
        p, new, made = [], [], []
        for r in range(N):
            q = mx_ref.quantize(now[r])
            s = mx_ref.matmul(qu[r], q)
            e = [chains(s[16 * g], s[16 * g + 1], flag[r][g]) for g in range(8)]
            p.append(np.stack([a for a, b in e]))
            new.append(np.stack([b for a, b in e]))
            d = decode(q).astype(BF)
            one = gcols(d, p[r])
            two = gcols(d, np.where(new[r] == 1, np.roll(p[r], -1, axis=1), p[r]))
            made.append(mx_ref.quantize(((one.astype(np.float32) + two.astype(np.float32)) * np.float32(0.5)).astype(BF)))
            new[r][:, H - 1] = 0
        for r in range(N):
            e = partner(r, t)
            flag[r] = np.concatenate([new[r][:, :H], new[e][:, H:]], axis=1)
            z = join(pick(made[r], np.arange(H)), pick(made[e], np.arange(H, C)))
            d = decode(z).reshape(128, C, 4)
            now[r] = tile([d[:, :, b] + np.maximum(mx_ref.matmul(pick(lay[r], np.arange(128 * b, 128 * b + 128)), z), np.float32(0.0)) * np.float32(0.015625) for b in range(4)])
    y, ol = np.zeros((N, 128, C), np.float32), np.zeros((N, 8, 2 * C), np.float32)
    oc, osc = np.zeros((N, 128, 4 * C), np.uint8), np.zeros((N, 16, C), np.uint8)
    for r in range(N):
        q = mx_ref.quantize(now[r])
        y[r] = mx_ref.matmul(mx_ref.quantize(v[r]), q)
        ol[r] = np.concatenate([p[r], flag[r]], axis=1)
        oc[r], osc[r] = emit(q)
    return {"y": y, "ol": ol, "oc": oc, "osc": osc}

@@ -1,0 +1,790 @@
+from concourse.mybir import dt, AluOpType as A, AxisListType, ActivationFunctionType as AF
+
+C, H, K2, R = 320, 160, 88, 3
+STEP = [1, 2, 4]
+BIG = 2.0 ** 90
+F32, BF, I32, U16, X4, U8 = "float32", "bfloat16", "int32", "uint16", "float8_e4m3fn_x4", "uint8"
+SCRATCH = {}
+SLOT = {}
+
+
+def _buf(names, n, d, where="sbuf"):
+    for s in names.split():
+        SCRATCH[s] = (where, [128, n], d)
+
+
+def _slots(buf, names, n, more=0):
+    for i, s in enumerate(names.split()):
+        SLOT[s] = (buf, n * i)
+    _buf(buf, n * len(names.split()) + more, F32)
+
+
+_buf("P0 P1 P2 P3 P4 P5 P6 P7", 512, F32, "psum")
+_buf("X0 X1 X2 X3 Y DH DG", 1280, BF)
+_buf("XQ0 XQ1 XQ2 XQ3 ZQ0 ZQ1 ZQ2", C, X4)
+_buf("XS0 XS1 XS2 XS3 ZS0 ZS1 ZS2", C, U8)
+_buf("YQ0 YQ1 YQ2", H, X4)
+_buf("YS0 YS1 YS2", H, U8)
+_buf("NS0 NS1 NS2", H, BF)
+_buf("F1 F2 F3", 384, BF)
+_buf("UB VB", 512, BF)
+_buf("UQ VQ UL UR", 128, X4)
+_buf("US VS ULS URS", 128, U8)
+_buf("WQ EQ", 512, X4)
+_buf("WS ES", 512, U8)
+_buf("EB", 2048, BF)
+_buf("ID", 128, BF)
+_buf("IO S D CE RA ME", 656, F32)
+_buf("GT GE CAP PP ZB ON", 640, BF)
+_buf("JK", 1280, BF)
+_buf("SG NTAU FL KP RB TN", 576, BF)
+_buf("RK TAB", 576, F32)
+_buf("NT TG", 304, F32)
+_buf("RL", 1280, F32)
+_buf("WIN", 4 * 1008, BF)
+_buf("NW", 688, BF)
+_buf("PW", 688, F32)
+_buf("W TK", 432, F32)
+_buf("EW", 1168, F32)
+_buf("TF TE", 672, BF)
+_buf("OLT", 640, F32)
+_buf("YO", C, F32)
+_buf("ci", 64, I32)
+_buf("cf", 128, F32)
+_buf("pf", 2, F32)
+_buf("sm", 448, F32)
+_buf("lg", 256, F32)
+_buf("off", 320, U16)
+_buf("of2", 64, U16)
+_buf("cw", 32, F32)
+_buf("so", 64, F32)
+_buf("lw SB", 288, F32)
+_buf("GJ", 384, F32)
+_slots("PB", "SV ZJ MJ FJ FA FB FC INV RW RS", 112, 16)
+_slots("QA", "JR PIT PIJ CJ SRC INS LA LB TZ1 DW DA VA", 96)
+_slots("QB", "TS TZ TM TJ TP TX KZ KT EV XX D0 D1 XO VC", 256)
+_slots("QC", "BD AL AR RM0 KE CS FI", 352)
+
+ENG = ["v", "s", "t", "g"]
+SEMAPHORES = ["e" + e for e in ENG] + ["d%d" % i for i in range(20)] + \
+             ["aq%d" % t for t in range(R)] + ["af%d" % t for t in range(R)] + ["sent"]
+
+
+def V(n, a, b=None, s=1):
+    b = a + 1 if b is None else b
+    if n in SLOT:
+        return ("ap", SLOT[n][0], a + SLOT[n][1], b + SLOT[n][1], s)
+    return ("ap", n, a, b, s)
+
+
+def IND(w, o):
+    return ("ind", w, o)
+
+
+def U8V(w):
+    return ("u8", w)
+
+
+def U32V(w):
+    return ("u32", w)
+
+
+def O(a, n=6, b="off"):
+    return V(b, a, a + n)
+
+
+def touched(x):
+    if not isinstance(x, tuple) or x[0] == "raw":
+        return []
+    if x[0] == "ap":
+        if SCRATCH[x[1]][0] == "psum":
+            return [(x[1], 1)]
+        if x[4] == 1:
+            return [(x[1], ((1 << (x[3] - x[2])) - 1) << x[2])]
+        return [(x[1], sum(1 << i for i in range(x[2], x[3] if x[3] != "end" else -1, x[4])))]
+    if x[0] == "ind":
+        return touched(x[1]) + touched(x[2])
+    return touched(x[-1])
+
+
+def rank_program(g, core, T, topo):
+    rank = T.rank_of(core)
+    if rank is None:
+        return
+    ops = []
+
+    def rec(e, meth, args, nw=1, kw=None, kind="c", extra=None):
+        kw = kw or {}
+        wr, rd = [], []
+        for i, a in enumerate(args):
+            if i < nw and isinstance(a, tuple) and a[0] == "ind":
+                wr += touched(a[1])
+                rd += touched(a[2])
+            elif i < nw:
+                wr += touched(a)
+            else:
+                rd += touched(a)
+        for k, a in kw.items():
+            if k == "accum_out":
+                wr += touched(a)
+            else:
+                rd += touched(a)
+        wr += [r for r in rd if SCRATCH[r[0]][0] == "psum"]
+        ops.append({"e": e, "m": meth, "a": args, "kw": kw, "wr": wr, "rd": rd, "kind": kind, "x": extra})
+
+    def ts(o, i, s1, op0, s2=None, op1=None):
+        rec("v", "tensor_scalar", [o, i, s1, s2, op0] + ([op1] if op1 is not None else []))
+
+    def tt(o, a, b, op):
+        rec("v", "tensor_tensor", [o, a, b, op])
+
+    def cp(o, i):
+        rec("v", "tensor_copy", [o, i])
+
+    def ms(o, c):
+        rec("v", "memset", [o, c])
+
+    def tr(o, i):
+        rec("v", "transpose", [o, i])
+
+    def scan(o, d0, d1, init, op0, op1):
+        rec("v", "tensor_tensor_scan", [o, d0, d1, init, op0, op1])
+
+    def act(o, i, f=AF.Copy, **kw):
+        rec("s", "activation", [o, i, f], kw=kw)
+
+    def lin(o, i, scale=1.0, bias=0.0):
+        act(o, i, AF.Identity if isinstance(bias, tuple) or isinstance(scale, tuple) else AF.Copy, scale=scale, bias=bias)
+
+    def iota(o, pat, base, cm=0):
+        kw = {} if SCRATCH[o[1]][2] == I32 else {"allow_small_or_imprecise_dtypes": True}
+        rec("g", "iota", [o, pat, base, cm], kw=kw)
+
+    def gfill(o, c=0):
+        iota(o, [[0, len(range(o[2], o[3], o[4]))]], c)
+
+    def quant(q, s, i):
+        rec("v", "quantize_mx", [q, s, i], nw=2)
+
+    def mm(p, w, ws, k, x, xs, a, n):
+        rec("t", "matmul_mx", [V(p, 0, n), V(w, 128 * k, 128 * k + 128), V(ws, 128 * k, 128 * k + 128), V(x, a, a + n), V(xs, a, a + n), True, True])
+
+    def dma(e, o, i):
+        rec(e, "dma_start", [o, i], kind="d")
+
+    def conv(src, n, tbuf, a=16, at=None):
+        at = n if at is None else at
+        tr(V(tbuf, 0, n), V(src, a, a + n))
+        tr(V(tbuf, at, at + n + 32), V(src, a - 16, a + n + 16))
+
+    def pick(tbuf, row=0, cols=1):
+        return IND(V(tbuf, 0, 224), O(PK + row, cols))
+
+    QF, HF, P32, M1C, R03, R1N, R124, MEC, INI, DM, NQ16 = [V("cf", i) for i in range(11)]
+    PF = V("pf", 0)
+    BJ, LEJ, CST, KW, JW, RM, B6, HI = 12, 16, 18, 32, 52, 64, 80, 88
+    HB, M0, M1, NT32, NL32, V1, VT, VT1, BB = [V("sm", 32 * i, 32 * i + 32) for i in range(9)]
+    N2, N3, WA, WB = 288, 324, 360, 396
+    OU, OT, PK, PKH, PKL, OI, OR, PK1, OO, OF, O4, O16, OP, OA, OMM, OK_, OF2, O42, O162 = \
+        0, 16, 52, 60, 0, 66, 72, 78, 80, 96, 112, 128, 144, 160, 192, 208, 272, 288, 304
+    OMF, OMB, OL = 0, 20, 40
+    tmp = lambda i, n=6: V("lw", 12 * i, 12 * i + n)
+    rm = lambda r: V("cf", RM + r)
+    zb = lambda n: V("ZB", 0, n)
+
+    dma("y", V("X0", 0, 1280), ("raw", T.x[:]))
+    dma("s", V("UB", 0, 512), ("raw", T.u[:]))
+    dma("y", U8V(V("WQ", 0, 512)), ("raw", T.wc[:]))
+    dma("y", V("WS", 0, 512), ("raw", T.ws[:]))
+    dma("y", V("VB", 0, 512), ("raw", T.v[:]))
+    iota(V("ci", 0), [[0, 1]], 0, 1)
+    iota(V("ci", 16, 50), [[17, 17], [0, 2]], 1)
+    iota(V("ci", 8, 16), [[16, 8]], 0)
+    iota(BB, [[1, 2], [0, 16]], 0)
+    iota(PF, [[0, 1]], 0, 1)
+    iota(V("IO", 0, 656), [[1, 656]], 0)
+    ms(zb(640), 0.0)
+    ms(V("KZ", 0, 256), 0.0)
+    ms(V("TG", 0, 144), 0.5)
+    ms(V("TG", 144, 304), 2.0)
+    ms(V("NT", 140), 0.0)
+    ts(V("ci", 1), V("ci", 0), 15, A.bitwise_and)
+    ts(V("ci", 2), V("ci", 0), 4, A.arith_shift_right, 1, A.bitwise_and)
+    ts(V("ci", 3), V("ci", 0), 31, A.bitwise_and)
+    scan(V("NT", 0, 140), V("TG", 0, 140), zb(140), 2.0 ** 71, A.mult, A.add)
+    cp(V("cf", 0, 3), V("ci", 1, 4))
+    scan(V("NT", 141, 290), V("TG", 144, 293), zb(149), -2.0 ** -70, A.mult, A.add)
+    ts(O(OT, 34), V("ci", 16, 50), QF, A.add)
+    ts(O(OT + 34, 1), QF, 17.0, A.mult, 17.0, A.add)
+    ts(O(OT + 35, 1), QF, 17.0, A.mult, 17.0, A.add)
+    lin(V("PB", 0, 568), zb(568))
+    act(V("RK", 0, 576), IND(V("NT", 0, 290), O(OT, 36)))
+    cp(O(OU, 8), V("ci", 8, 16))
+    ts(O(OU + 8, 8), V("ci", 8, 16), 1.0, A.add)
+    ts(V1, BB, HF, A.is_equal)
+    ms(V("S", 640, 656), -BIG)
+    ts(HB, V1, 2 * BIG, A.mult, -BIG, A.add)
+    ts(M0, V1, -4465.5, A.mult, 4000.0, A.add)
+    ms(V("EB", 0, 2048), 0.0)
+    tr(V("TAB", 0, 576), V("RK", 0, 576))
+    quant(V("UQ", 0, 128), V("US", 0, 128), V("UB", 0, 512))
+    for nm, o in (("UL", OU), ("UR", OU + 8)):
+        cp(U32V(V(nm, 0, 128)), IND(U32V(V("UQ", 0, 128)), O(o, 8)))
+        act(V(nm + "S", 0, 128), IND(V("US", 0, 128), O(o, 8)))
+    quant(V("XQ0", 0, C), V("XS0", 0, C), V("X0", 0, 1280))
+    for h in range(2):
+        tt(V("sm", 96 + 16 * h, 112 + 16 * h), V("TAB", 32, 544, 32), V("sm", 16 * h, 16 * h + 16), A.min)
+        tt(V("sm", 128 + 16 * h, 144 + 16 * h), V("NT", 17, 289, 17), V("sm", 16 * h, 16 * h + 16), A.min)
+    lin(NQ16, QF, -1.0 / 16)
+    mm("P4", "UL", "ULS", 0, "XQ0", "XS0", 0, C)
+    mm("P5", "UR", "URS", 0, "XQ0", "XS0", 0, C)
+    cp(V("S", 0, 640, 2), V("P4", 0, C))
+    act(V("S", 1, 640, 2), V("P5", 0, C))
+
+    rows = {1: (-1, 0, 0, -1, 0, 0, 0, 0), 2: (2, 2, -1, -2, 2, 2, 0, 650), 3: (0, -1, 0, 1, -1, -1, 0, -320),
+            5: (0, 2, 0, 0, 2, 1, 1, 640), 6: (0, 1, 0, 0, 1, 0, 0, 0), 7: (0, 0, 512, 0, 0, 832, 1, 840),
+            8: (0, 0, 512, 0, 0, 0, 1, 520), 9: (0, 1, 369, 0, 1, 1, 0, 1), 10: (1, 0, -369, -1, 0, 369, 0, 0),
+            11: (0, 0, 1, 0, 0, -1, 0, 1), 12: (1, 1, 0, 0, 1, 1, 0, 1), 13: (0, 0, -2, 0, 0, 2, 0, 0)}
+    iota(V("lg", 0, 6), [[16, 2], [0, 3]], 0)
+    iota(V("lg", 8, 14), [[0, 2], [7, 3]], 5)
+    iota(V("lg", 16, 22), [[0, 2], [112, 3]], 112)
+    iota(V("cf", KW, KW + 20), [[16, 20]], 0)
+    iota(V("cf", JW, JW + 6), [[32, 3], [0, 2]], 0)
+    iota(V("PIT", 0, K2), [[1024, K2 // 2], [0, 2]], 1024)
+    gfill(V("PIT", K2, 96))
+    for q, co in rows.items():
+        for k, c in enumerate(co):
+            if c:
+                iota(V("KZ", 32 * k + q, 32 * k + 32, 16), [[0, 2]], c)
+    iota(V("TN", 0, 576), [[16, 6], [-1, 96]], 0)
+    gfill(V("RA", 640, 656))
+    gfill(V("D0", 0, 192, 2), -(2 ** 23))
+    gfill(V("SB", 0, 288))
+    gfill(V("SB", 98, 192, 16), 1)
+    gfill(V("SB", 192, 288, 16), 1)
+    for nm, a, n, c in (("DW", 0, 192, 0), ("W", 0, C, 1), ("CS", 0, 352, 0), ("EV", 0, 224, 0), ("TK", 0, 432, 0), ("EW", 0, C, 0),
+                        ("FI", 0, 16, 0), ("FI", 336, 352, 0), ("NW", 0, C, 0), ("NW", C, 368, 1), ("NW", 368, 688, 0),
+                        ("F1", 0, 32, 0), ("F1", 352, 384, 0), ("F2", 0, 32, 0), ("F2", 352, 384, 0)):
+        gfill(V(nm, a, n), c)
+
+    s16 = [16.0 ** -(i + 1) for i in range(5)]
+    u1 = 2.0 ** -23
+    co = [(0.0, -x) for x in s16] + [(0.0, -u1)] + [(s16[i] - s16[i + 1], 0.0) for i in range(4)] + \
+         [(s16[4], 0.0), (-u1, -u1 / 2), (u1, u1 / 4), (0.0, -u1 / 2)]
+
+    def c1():
+        ts(M1C, QF, 0.0, A.is_equal, 8000.0, A.mult)
+        for i in range(7):
+            ts(V("cf", CST + i), QF, co[i][0], A.mult, co[i][1], A.add)
+        ts(M1C, M1C, -4000.0, A.add)
+        ts(V("ID", 0, 128), V("IO", 0, 128), PF, A.is_equal)
+        ts(M1, M0, M1C, A.max)
+
+    def c2():
+        for i in range(7, 12):
+            lin(V("cf", CST + i), QF, co[i][0], co[i][1])
+
+    def c2b():
+        for i in range(12, 14):
+            lin(V("cf", CST + i), QF, co[i][0], co[i][1])
+        lin(V("ON", 0, 640), zb(640), 1.0, 1.0)
+
+    def c3():
+        for b in range(4):
+            cp(V("EB", 513 * b, 512 * (b + 1), 4), V("ID", 0, 128))
+        ts(V("cf", RM, RM + 16), V("IO", 0, 16), QF, A.is_equal)
+        quant(V("EQ", 0, 512), V("ES", 0, 512), V("EB", 0, 2048))
+
+    def c4():
+        ts(V("lg", 0, 6), V("lg", 0, 6), QF, A.add)
+        ts(R124, rm(1), rm(2), A.add, rm(4), A.add)
+        tt(V("lg", 0, 6), V("lg", 0, 6), V("lg", 8, 14), A.min)
+        ts(MEC, rm(0), 95.0, A.mult)
+        ts(V("ci", 8, 14), V("lg", 0, 6), HF, A.add)
+        ts(V("ME", 648, 656), zb(8), MEC, A.add)
+        ts(V("ci", 16, 22), V("ci", 8, 14), 1, A.bitwise_and)
+        ts(V("lg", 0, 6), V("lg", 0, 6), 16.0, A.mult)
+        tt(V("lg", 16, 22), V("lg", 16, 22), V("ci", 16, 22), A.mult)
+        ts(MEC, R124, 65536.0, A.mult, MEC, A.add)
+        tt(V("cf", B6, B6 + 6), V("lg", 0, 6), V("lg", 16, 22), A.add)
+
+    def c5():
+        ts(V("cf", KW, KW + 20), V("cf", KW, KW + 20), QF, A.add)
+        ts(O(PK, 8), V("IO", 0, 8), V("cf", B6), A.add)
+        ts(O(PKH, 6), V("IO", 0, 6), V("cf", B6 + 1), A.add)
+        ts(O(PK1, 1), V("cf", B6 + 1), 1.0, A.add)
+        cp(O(PKL, 2), V("cf", B6 + 2, B6 + 6, 3))
+        ts(V("cf", BJ, BJ + 4), V("cf", KW, KW + 4), -4.0, A.mult, 4.0 * K2 - 2, A.add)
+        ts(V("cf", LEJ, LEJ + 2), V("cf", KW + 4, KW + 6), -float(K2), A.add, 4.0, A.mult)
+        ts(V("cf", HI, HI + 2), V("cf", KW + 4, KW + 6), 1.0 - K2, A.add, 4.0, A.mult)
+        ts(V("cf", HI + 2, HI + 4), V("cf", KW + 4, KW + 6), 1.0 - K2, A.add, 2.0 * C, A.mult)
+        ts(DM, QF, -8.0, A.add, 0.0, A.max)
+
+    def c6():
+        ts(INI, rm(1), rm(4), A.add, 369.0, A.mult)
+        ts(V("JR", 0, 96), V("IO", 0, 96), rm(0), A.mult)
+        ts(V("PIT", 0, 96), V("PIT", 0, 96), R124, A.mult)
+        ts(INI, INI, rm(2), A.add)
+        ts(V("cf", HI + 3), V("cf", HI + 3), DM, A.add)
+        ts(tmp(22), V("cf", JW, JW + 6), P32, A.add, 336.0, A.add)
+        ts(tmp(23), V("cf", JW, JW + 6), P32, A.add, 850.0, A.add)
+        ts(R1N, rm(1), -1.0, A.mult)
+        ts(R03, rm(0), rm(3), A.add)
+
+    kt = lambda i: V("KT", 32 * i)
+
+    def c7():
+        tr(V("KT", 0, 256), V("KZ", 0, 256))
+        ms(V("KP", 0, 576), 1.0)
+        ts(V("CE", 640, 656), V("IO", 0, 16), kt(6), A.mult, kt(7), A.add)
+        ms(V("KP", 0, 576, 96), 0.0)
+
+    def c7s():
+        lin(V("CE", 0, 640, 2), V("IO", 0, C), kt(1), kt(2))
+        lin(V("CE", 1, 640, 2), V("IO", 0, C), kt(4), kt(5))
+
+    def c8():
+        ts(V("RA", 0, 640, 2), zb(C), kt(0), A.add)
+        ts(V("RA", 1, 640, 2), zb(C), kt(3), A.add)
+        ts(V("NTAU", 0, 576), V("TN", 0, 576), QF, A.add, 0.5, A.is_lt)
+
+    def c9():
+        lin(V("SB", 194, 288, 16), zb(6), 1.0, 2.0 ** -20)
+
+    def c10():
+        lin(V("AL", 0, C), zb(C), 1.0, kt(0))
+        lin(V("AR", 0, C), zb(C), 1.0, kt(3))
+        act(V("PW", 0, 368), V("IO", 0, 368))
+        act(V("PW", 368, 688), V("IO", 0, C))
+
+    def row(c):
+        return IND(V("TK", 0, 432), O(c, 1))
+
+    for t in range(R):
+        XQ, XS, F, ZQ, ZS = "XQ%d" % t, "XS%d" % t, "F%d" % t, "ZQ%d" % t, "ZS%d" % t
+        Fn, Xn, XQn, XSn = "F%d" % (t + 1), "X%d" % (t + 1), "XQ%d" % (t + 1), "XS%d" % (t + 1)
+        last = t == R - 1
+
+        def dmm():
+            for b in range(4):
+                mm("P%d" % b, "EQ", "ES", b, XQ, XS, 0, C)
+
+        def dh(b, nm="DH"):
+            return lambda: lin(V(nm, C * b, C * b + C), V("P%d" % b, 0, C), 0.5)
+
+        def mf(b):
+            return lambda: tt(V("WIN", 1008 * b + 368, 1008 * b + 688), IND(V("DH", C * b, C * b + C), O(OMF, 20, "of2")), V("DG", C * b, C * b + C), A.add)
+
+        def lists():
+            conv(F, C, "TF", 32)
+            cp(V("lg", 176, 208), IND(V("TF", 0, 672), O(PKL, 2)))
+            tt(V("lg", 176, 196), V("lg", 176, 196), V("cf", KW, KW + 20), A.add)
+            cp(O(OMF, 20, "of2"), V("lg", 176, 196))
+
+        l2 = [lambda: conv(F, C, "TE", 31),
+              lambda: ts(V("lg", 208, 240), IND(V("TE", 0, 672), O(PKL, 2)), -321.0, A.mult, 320.0, A.add),
+              lambda: tt(V("lg", 208, 228), V("lg", 208, 228), V("cf", KW, KW + 20), A.add),
+              lambda: cp(O(OMB, 20, "of2"), V("lg", 208, 228))]
+
+        def runs():
+            scan(V("RA", 1, 640, 2), V(F, 31, 351), V("AR", 0, C), 0.0, A.mult, A.add)
+            scan(V("RA", 638, "end", -2), V(F, 351, 31, -1), V("AL", 0, C), 0.0, A.mult, A.add)
+
+        if t == 0:
+            fv = [[c1], [], [c3, dmm], [c4], [c5], [c6], [], [c7]]
+            fs = [[c2], [c2b], [lambda: lin(V("PB", 568, 1136), zb(568))], [dh(0)], [dh(1)], [dh(2)], [dh(3)], []]
+            late = [c8]
+        else:
+            dmm()
+            fv = [[lists], [], [l2[0]], [l2[1], mf(0)], [l2[2], mf(1)], [runs], [], [l2[3], mf(2)]]
+            fs = [[dh(b // 2, ("DH", "DG")[b % 2])] for b in range(8)]
+            late = [mf(3)]
+        neg = V("TAB", 17 * 32)
+        cnt = V("lg", 240)
+        cw = lambda i: V("cw", i)
+        for it in range(1, 9):
+            act(V("JK", 640 * (it % 2), 640 * (it % 2) + 640), V("D" if it == 8 else "S", 0, 640), AF.Sign, bias=neg, accum_out=cnt)
+            for f in fs[it - 1]:
+                f()
+            init = cw(16 + it)
+            if it == 2:
+                ts(BB, HB, neg, A.min)
+                scan(V("sm", N2 + 1, N2 + 33), VT1, NL32, 2.0 ** 70, A.min, A.max)
+                tr(V("sm", N2, N2 + 32), BB)
+                ts(V("sm", WA, WA + 33), V("sm", N2, N2 + 33), -1.0, A.mult, 2.0 ** -69, A.max)
+                ts(V("sm", WB, WB + 33), V("sm", N2, N2 + 33), 0.5, A.mult)
+                tt(V("sm", WA, WA + 33), V("sm", WA, WA + 33), V("sm", WB, WB + 33), A.max)
+                ts(V("sm", WA, WA + 33), V("sm", WA, WA + 33), NQ16, A.mult)
+                tt(V("sm", N3, N3 + 33), V("sm", WA, WA + 33), V("sm", N2, N2 + 33), A.add)
+            if it == 3:
+                scan(BB, VT1, V("sm", N2, N2 + 32), V("sm", N2 + 32), A.min, A.max)
+                lo = V("sm", 287)
+                ts(cw(14), lo, -1.0, A.mult, 2.0 ** -69, A.max)
+                ts(cw(14), lo, 0.5, A.mult, cw(14), A.max)
+                ts(V("cw", 0, 14), V("cf", CST, CST + 14), cw(14), A.mult)
+            if 3 <= it <= 6:
+                ts(init, neg, cw(3 + it), A.add)
+            if it == 7:
+                init = cw(11)
+                ts(cw(15), neg, cw(10), A.add)
+                ts(V("D", 0, 640), V("S", 0, 640), cw(15), A.add)
+            if it == 8:
+                ts(init, neg, cw(12), A.add)
+            for f in fv[it - 1]:
+                f()
+            out = V("so", 32 * (it % 2), 32 * (it % 2) + 32)
+            if it <= 2:
+                ts(V1, M0, cnt, A.subtract, 2.0 ** 85, A.mult)
+                tr(VT1, V1)
+                if it == 1:
+                    scan(out, VT1, NT32, V("TAB", 0), A.min, A.max)
+                else:
+                    scan(out, VT1, V("sm", N3, N3 + 32), V("sm", N3 + 32), A.min, A.max)
+            else:
+                ts(V1, M0 if it == 8 else M1, cnt, A.is_le, cw(it - 3), A.mult)
+                tr(VT, V1)
+                scan(out, VT, zb(32), init, A.add, A.add)
+            neg = V("so", 32 * (it % 2) + 31)
+        act(V("GT", 0, 640), V("D", 0, 640), AF.Sign, bias=neg, accum_out=cnt)
+        if t == 0:
+            c7s()
+        else:
+            lin(V("ME", 0, 640), zb(640), 1.0, MEC)
+        ts(cw(26), neg, -1.0, A.mult, cw(13), A.add)
+        ts(V("GE", 0, 640), V("D", 0, 640), cw(26), A.is_gt, 2.0, A.mult)
+        ts(cw(27), cnt, -1.0, A.mult, -640.0, A.add)
+        scan(V("CAP", 0, 640), V("GT", 0, 640), V("ON", 0, 640), cw(27), A.add, A.add)
+        scan(V("PP", 0, 640), V("GE", 0, 640), V("CAP", 0, 640), -2.0 * K2, A.add, A.min)
+        scan(V("CAP", 0, C), V("PP", 0, 640, 2), V("PP", 1, 640, 2), -1024.0, A.max, A.add)
+        for c in range(4):
+            act(V("JK", C * c, C * c + C), V("CAP", 0, C), AF.Sign, bias=V("cf", BJ + c), accum_out=V("lg", 244 + c))
+        for c in range(2):
+            ts(V("GT", C * c, C * c + C), V("CAP", 0, C), V("cf", LEJ + c), A.max, V("cf", HI + c), A.min)
+        for c in range(2):
+            rec("v", "tensor_reduce", [V("lg", 248 + c), V("GT", C * c, C * c + C), AxisListType.X, A.add])
+        for c in range(2):
+            ts(O(OI + 4 + c, 1), V("lg", 248 + c), -0.5, A.mult, V("cf", HI + 2 + c), A.add)
+        for f in late:
+            f()
+        ts(O(OI, 4), V("lg", 244, 248), -1.0, A.mult, 320.0, A.add)
+        cp(V("SV", 16, 112), IND(V("S", 0, 656), O(OI)))
+        act(V("CJ", 0, 96), IND(V("CE", 0, 656), O(OI)))
+        conv("SV", 96, "TS")
+        ts(V("lg", 0, 16), pick("TS"), -1.0, A.mult)
+        for c in range(6):
+            act(V("SG", 96 * c, 96 * c + 96), V("SV", 16, 112), AF.Sign, bias=V("lg", c))
+        tt(V("ZJ", 16, 112), IND(V("RA", 0, 656), O(OI)), V("CJ", 0, 96), A.add)
+        lin(V("SRC", 0, 96), V("ZJ", 16, 112), rm(6))
+        lin(V("LA", 0, 96), V("ZJ", 16, 112), R1N)
+        lin(V("D0", 1, 192, 2), V("ZJ", 16, 112), rm(1))
+        if t == 0:
+            lin(V("ME", 0, 640), zb(640), 1.0, MEC)
+        for c in range(0, 6, 2):
+            tt(V("FL", 96 * c, 96 * c + 192), V("SG", 96 * c, 96 * c + 192), V("NTAU", 96 * c, 96 * c + 192), A.is_ge)
+        conv("ZJ", 96, "TZ")
+        scan(V("RB", 0, 576), V("KP", 0, 576), V("FL", 0, 576), 0.0, A.mult, A.add)
+        tt(V("SRC", 0, 96), V("SRC", 0, 96), V("JR", 0, 96), A.add)
+        cp(O(OR), V("RB", 95, 576, 96))
+        cp(O(OO, 16), pick("TZ", 2))
+        cp(IND(V("INV", 16, 112), O(OR)), V("SRC", 0, 96))
+        act(V("PIJ", 0, 96), IND(V("PIT", 0, 96), O(OR)))
+        z = lambda r: V("TZ", r, 96, 16)
+        lin(tmp(3), z(12), -1.0, 336.0)
+        cp(V("INS", 0, 96, 2), V("INV", 17, 112, 2))
+        act(V("INS", 1, 96, 2), V("INV", 16, 112, 2))
+        tr(V("TZ1", 0, 96), V("ZJ", 17, 113))
+        tt(V("MJ", 16, 112), IND(V("INS", 0, 96), O(OR)), V("PIJ", 0, 96), A.add)
+        lin(V("SB", 97, 192, 16), z(12), 1.0, 369.0)
+        lin(tmp(21), z(1), 1.0, 1.0)
+        if last:
+            lin(V("SB", 100, 192, 16), z(12), 1.0, 369.0)
+            lin(V("SB", 196, 288, 16), z(6), 1.0, 1.0)
+        tt(tmp(1), V("TZ1", 3, 96, 16), z(12), A.add)
+        cp(IND(V("ME", 0, 656), O(OI)), V("MJ", 16, 112))
+        tt(tmp(2), tmp(22), z(3), A.add)
+        tt(V("FJ", 16, 112), IND(V("ME", 0, 656), O(OO)), V("ZJ", 16, 112), A.add)
+        ts(tmp(1), tmp(1), 0.0, A.is_equal)
+        conv("FJ", 96, "TJ")
+        act(V("D1", 1, 192, 2), V("FJ", 16, 112))
+        cp(O(OF, 16), pick("TJ"))
+        ts(O(OF2, 16), pick("TJ"), 2.0, A.mult, 1.0, A.add)
+
+        def s1():
+            conv("MJ", 96, "TM")
+            ts(tmp(0), V("TJ", 4, 96, 16), 65536.0, A.not_equal)
+            ts(O(OMM, 16), pick("TM"), 2.0, A.mult, 1.0, A.add)
+
+        def s2():
+            conv("INV", 96, "TP")
+            cp(O(OP, 16), pick("TP", 6))
+
+        def s3():
+            tt(tmp(20), tmp(0), z(8), A.mult)
+            ts(tmp(0), tmp(20), 0.0, A.is_gt)
+            tt(tmp(1), tmp(1), tmp(0), A.max)
+            tt(tmp(2), tmp(2), tmp(0), A.mult)
+            tt(tmp(3), tmp(3), tmp(1), A.mult)
+            tt(V("SB", 96, 192, 16), tmp(23), tmp(1), A.mult)
+            tt(V("SB", 0, 96, 16), tmp(2), z(3), A.subtract)
+            tt(V("SB", 1, 96, 16), tmp(3), z(12), A.add)
+
+        def s4():
+            tr(V("RS", 16, 112), V("SB", 0, 96))
+            tr(V("VC", 0, 192), V("SB", 96, 288))
+
+        def s5():
+            conv("RS", 96, "TS")
+            cp(O(OA, 32), pick("TS", 0, 2))
+
+        def gj(b):
+            return lambda: act(V("GJ", 96 * b, 96 * b + 96), IND(V("DH", C * b, C * b + C), O(OP)))
+
+        def jm(b):
+            tt(V("WIN", 1008 * b + C, 1008 * b + 368), V("GJ", 96 * b, 96 * b + 96, 2), V("GJ", 96 * b + 1, 96 * b + 96, 2), A.add)
+
+        def s7():
+            lin(V("SB", 193, 288, 16), V("TM", 4, 96, 16), 1.0 / 1024, 320.0)
+
+        side = [[s2], [], [s1], [s3], [], [s4], [s5], []]
+        sides = [[], [] if t else [c9], [gj(0)], [s7], [gj(1)], [gj(2)], [gj(3)], []]
+        la, fb, n = "LA", "FJ", 0
+        for o, o2, on, on2 in ((OF, OF2, O4, O42), (O4, O42, O16, O162), (O16, O162, None, None)):
+            fa = fb
+            for k in range(3 if on else 2):
+                act(V("D1", 0, 192, 2), IND(V("XO", 0, 192), O(o2)) if n else IND(V("FJ", 16, 112), O(o)))
+                for _i in range((2, 1, 0)[k] if on else 0):
+                    fo = [x for x in ("FA", "FB", "FC") if x != fa and x != fb][0]
+                    act(V(fo, 16, 112), IND(V(fa, 16, 112), O(o)))
+                    fa = fo
+                if on:
+                    lo_ = "LB" if la == "LA" else "LA"
+                    tt(V(lo_, 0, 96), IND(V(la, 0, 96), O(o)), V("D0", 1, 192, 2), A.subtract)
+                    la = lo_
+                scan(V("XO", 0, 192), V("D0", 0, 192), V("D1", 0, 192), 0.0, A.add, A.max)
+                if on and k == 1:
+                    conv(fa, 96, "TS")
+                    cp(O(on, 16), pick("TS"))
+                    ts(O(on2, 16), pick("TS"), 2.0, A.mult, 1.0, A.add)
+                if on and k == 2:
+                    cp(V("D1", 1, 192, 2), V("XO", 1, 192, 2))
+                    ts(V("D0", 1, 192, 2), V(la, 0, 96), -1.0, A.mult)
+                for f in sides[n] + side[n]:
+                    f()
+                n += 1
+            fb = fa
+        act(V("XX", 96, 192), IND(V("XO", 0, 192), O(OMM)))
+        cp(V("XX", 0, 96), V("XO", 1, 192, 2))
+        jm(0)
+        tr(V("TX", 0, 192), V("XX", 0, 192))
+        jm(1)
+        if t == 0:
+            lin(V("RM0", 0, C), zb(C), 1.0, R03)
+        for b in range(4):
+            if t:
+                act(V("WIN", 1008 * b + 688, 1008 * b + 1008), V("P%d" % b, 0, C))
+                act(V("WIN", 1008 * b, 1008 * b + C), IND(V("WIN", 1008 * b + 368, 1008 * b + 1008), O(OMB, 20, "of2")))
+            else:
+                act(V("WIN", 1008 * b, 1008 * b + C), V("P%d" % b, 0, C))
+                act(V("WIN", 1008 * b + 368, 1008 * b + 688), V("P%d" % b, 0, C))
+        if t == 0:
+            c10()
+        else:
+            act(V("NW", 0, C), V(F, 31, 31 + C))
+            act(V("NW", 368, 688), V(F, 32, 32 + C))
+        x1 = lambda r: V("TX", r, 96, 16)
+        x2 = lambda r: V("TX", 96 + r, 192, 16)
+        d1, d2 = V("lw", 60, 66), V("lw", 66, 72)
+        tt(tmp(5, 12), V("TX", 4, 192, 16), V("TX", 1, 192, 16), A.subtract)
+        tt(tmp(6), x1(4), V("TM", 4, 96, 16), A.not_equal)
+        tt(V("DW", 2, 96, 16), x1(3), x2(3), A.max)
+        tt(tmp(7, 12), V("TX", 2, 192, 16), V("TX", 4, 192, 16), A.subtract)
+        tt(tmp(8), tmp(6), d2, A.mult)
+        tt(tmp(9), V("DW", 2, 96, 16), z(3), A.is_equal)
+        tt(tmp(11), V("lw", 90, 96), z(5), A.subtract)
+        tt(tmp(10), tmp(8), d1, A.add)
+        tt(tmp(12), tmp(7), z(5), A.subtract)
+        tt(tmp(10), tmp(10), tmp(9), A.mult)
+        tt(tmp(11), tmp(11), tmp(6), A.mult)
+        tt(V("DW", 0, 96, 16), tmp(10), tmp(21), A.add)
+        tt(V("DW", 3, 96, 16), tmp(10), tmp(21), A.add)
+        tt(tmp(12), tmp(11), tmp(12), A.is_ge)
+        tr(V("RW", 16, 112), V("DW", 0, 96))
+        tt(tmp(13), d1, tmp(8), A.subtract)
+        cp(IND(V("W", 0, 432), O(OA)), V("RW", 16, 112))
+        conv("RW", 96, "TP")
+        tt(tmp(13), tmp(13), tmp(12), A.mult)
+        tt(tmp(14), tmp(12), z(1), A.mult)
+        tt(tmp(17), tmp(12), tmp(6), A.mult)
+        scan(V("CS", 1, C + 1), V("W", 0, C), V("RM0", 0, C), 0.0, A.add, A.mult)
+        ts(O(OMM, 16), pick("TP", 2), -1.0, A.mult)
+        tt(tmp(13), tmp(13), tmp(8), A.add)
+        tt(tmp(15), tmp(12), z(10), A.mult)
+        tt(tmp(16), tmp(12), z(13), A.mult)
+        tt(tmp(14), tmp(14), tmp(20), A.add)
+        tt(tmp(17), tmp(17), z(7), A.mult)
+        tt(tmp(18), tmp(13), tmp(12), A.subtract)
+        tt(V("DA", 1, 96, 16), tmp(15), z(9), A.add)
+        tt(V("DA", 2, 96, 16), tmp(16), z(11), A.add)
+        tt(tmp(18), tmp(18), z(7), A.add)
+        tt(V("DA", 0, 96, 16), tmp(14), tmp(13), A.add)
+        if last:
+            tt(V("DA", 4, 96, 16), tmp(15), z(9), A.add)
+        tt(V("DA", 3, 96, 16), tmp(18), tmp(17), A.subtract)
+        tt(V("EV", 112, 208), IND(V("CS", 0, 352), O(OA + 16)), V("VC", 0, 96), A.add)
+        tr(V("VA", 0, 96), V("DA", 0, 96))
+        jm(2)
+        tt(V("EV", 16, 112), IND(V("CS", 0, 352), O(OMM)), V("VA", 0, 96), A.add)
+        jm(3)
+        conv("EV", 192, "TK", 16, 208)
+        cp(O(OK_, 64), IND(V("TK", 0, 432), O(PKH, 4)))
+        cp(IND(V("EW", 0, 1168), O(OK_, 12)), V("EV", 16, 208))
+        cp(IND(V("EW", 0, 1168), O(OK_ + 48)), V("VC", 96, 192))
+        ts(V("KE", 0, C), V("EW", 0, C), 0.0, A.is_equal)
+        scan(V("FI", 16, 336), V("KE", 0, C), V("EW", 0, C), INI, A.mult, A.add)
+        YQ, YS, NS = "YQ%d" % t, "YS%d" % t, "NS%d" % t
+        for hf in (1, 0):
+            o = O(OL + 10 * hf, 10, "of2")
+            conv("FI", H, "TK", 16 + H * hf, 208)
+            tt(V("lg", 96, 112), row(PKH), V("cf", KW + 10 * hf, KW + 10 * hf + 16), A.subtract)
+            tt(V("lg", 112, 128), row(PKH + 2), V("lg", 96, 112), A.mult)
+            tt(V("lg", 128, 144), row(PK1), V("lg", 112, 128), A.subtract)
+            ts(o, V("lg", 128, 138), -0.75, A.add)
+            for b in range(4):
+                y, w = V("Y", 640 * hf + b, 640 * hf + 640, 4), IND(V("WIN", 1008 * b, 1008 * b + 688), o)
+                cp(y, w) if b < 2 else act(y, w)
+            if hf:
+                quant(V(YQ, 0, H), V(YS, 0, H), V("Y", 640, 1280))
+                rec("g", "remote", [U8V(V(ZQ, H, C)), U8V(V(YQ, 0, H))], nw=0, kind="r", extra=("aq%d" % t, t))
+                rec("g", "remote", [V(ZS, H, C), V(YS, 0, H)], nw=0, kind="r", extra=("aq%d" % t, t))
+                act(V(NS, 0, H), IND(V("NW", 0, 688), o))
+                rec("g", "remote", [V(Fn, 192, 352), V(NS, 0, H)], nw=0, kind="r", extra=("af%d" % t, t))
+            else:
+                quant(V(ZQ, 0, H), V(ZS, 0, H), V("Y", 0, 640))
+            if last:
+                tt(V("lg", 144, 160), row(PKH + 4), V("lg", 112, 128), A.subtract)
+                ts(O(OMF + 10 * hf, 10, "of2"), V("lg", 144, 154), -0.75, A.add)
+        for hf in range(2):
+            a = H * hf
+            if hf:
+                rec("n", "arrive", [V(ZQ, H, C), V(ZS, H, C)], nw=2, kind="a", extra=("aq%d" % t, t, 2))
+                rec("n", "arrive", [V(Fn, 192, 352)], kind="a", extra=("af%d" % t, t, 1))
+            for b in range(4):
+                mm("P%d" % (4 + b), "WQ", "WS", b, ZQ, ZS, a, H)
+                mm("P%d" % b, "EQ", "ES", b, ZQ, ZS, a, H)
+            for b in range(4):
+                act(V("RL", C * b + a, C * b + a + H), V("P%d" % (4 + b), 0, H), AF.Relu, scale=0.015625)
+                tt(V(Xn, 4 * a + b, 4 * a + 640, 4), V("P%d" % b, 0, H), V("RL", C * b + a, C * b + a + H), A.add)
+            if hf == 0:
+                act(V(Fn, 32, 192), IND(V("NW", 0, 688), O(OL, 10, "of2")))
+                lin(V(Fn, 191), zb(1))
+            if not last:
+                lin(V("BD", a + hf, a + H + 1), V(Fn, 31 + a + hf, 32 + a + H), -2 * BIG, BIG)
+            quant(V(XQn, a, a + H), V(XSn, a, a + H), V(Xn, 4 * a, 4 * a + 640))
+            if not last:
+                mm("P4", "UL", "ULS", 0, XQn, XSn, a, H)
+                mm("P5", "UR", "URS", 0, XQn, XSn, a, H)
+                tt(V("S", 2 * a, 2 * a + C, 2), V("P4", 0, H), V("BD", a, a + H), A.min)
+                tt(V("S", 2 * a + 1, 2 * a + C, 2), V("P5", 0, H), V("BD", a + 1, a + H + 1), A.min)
+                if hf == 0:
+                    gfill(V("W", 0, C), 1)
+                    gfill(V("EW", 0, C))
+                    if t == 0:
+                        quant(V("VQ", 0, 128), V("VS", 0, 128), V("VB", 0, 512))
+            else:
+                mm("P4", "VQ", "VS", 0, XQn, XSn, a, H)
+                dma("y", ("raw", T.oc[:, 4 * a:4 * a + 640]), U8V(V(XQn, a, a + H)))
+                act(V("YO", a, a + H), V("P4", 0, H))
+                dma("s", ("raw", T.y[:, a:a + H]), V("YO", a, a + H))
+                if hf == 0:
+                    cp(V("OLT", 0, C), IND(V("PW", 0, 688), O(OMF, 20, "of2")))
+                    dma("y", ("raw", T.ol[:, 0:C]), ("rows", slice(0, 128, 16), V("OLT", 0, C)))
+    cp(V("OLT", C, 640), V("F3", 32, 352))
+    for k in range(4):
+        dma("s" if k % 2 else "y", ("raw", T.osc[4 * k:4 * k + 4, :]), ("rows", slice(32 * k, 32 * k + 4), V("XS3", 0, C)))
+    dma("y", ("raw", T.ol[:, C:640]), ("rows", slice(0, 128, 16), V("OLT", C, 640)))
+    emit(g, core, rank, T, topo, ops)
+
+
+def emit(g, core, rank, T, topo, ops):
+    qs = {"v": g.vector, "s": g.scalar, "t": g.tensor, "g": g, "y": g.sync}
+
+    def ap(x, rows=slice(None)):
+        if not isinstance(x, tuple):
+            return x
+        if x[0] == "raw":
+            return x[1]
+        if x[0] == "ap":
+            return T[x[1]][rows, slice(x[2], None if x[3] == "end" else x[3], x[4] if x[4] != 1 else None)]
+        if x[0] == "rows":
+            return ap(x[2], x[1])
+        if x[0] == "ind":
+            return ap(x[1]).indirect(ap(x[2]))
+        return ap(x[1]).bitcast(dt.uint8 if x[0] == "u8" else dt.uint32)
+
+    hist = {}
+    for i, o in enumerate(ops):
+        dep = set()
+        rd = o["rd"] if o["kind"] != "r" else touched(o["a"][1])
+        for nm, m in rd:
+            dep.update(j for j, w, m2 in hist.get(nm, []) if w and m2 & m)
+        for nm, m in o["wr"]:
+            dep.update(j for j, w, m2 in hist.get(nm, []) if m2 & m)
+        o["dep"] = dep
+        for nm, m in o["wr"]:
+            hist[nm] = [(j, w, m2 & ~m) for j, w, m2 in hist.get(nm, []) if m2 & ~m] + [(i, True, m)]
+        if o["kind"] != "r":
+            for nm, m in rd:
+                hist.setdefault(nm, []).append((i, False, m))
+    known = {e: {} for e in qs}
+    for o in ops:
+        o["clock"] = {}
+        if o["kind"] == "a":
+            continue
+        kn = known[o["e"]]
+        o["need"] = []
+        for j in sorted(o["dep"], reverse=True):
+            p = ops[j]
+            key = p["e"] if p["kind"] == "c" else ("x", j)
+            if kn.get(key, -1) >= j:
+                continue
+            o["need"].append(j)
+            p["sig"] = True
+            kn[key] = j
+            for k2, v2 in p["clock"].items():
+                if kn.get(k2, -1) < v2:
+                    kn[k2] = v2
+        o["clock"] = dict(kn)
+    count = {e: 0 for e in ENG}
+    nd, sent, final = 0, 0, []
+    v = g.vector
+    calls = {"tensor_scalar": v.tensor_scalar, "tensor_tensor": v.tensor_tensor, "tensor_copy": v.tensor_copy, "memset": v.memset,
+             "transpose": v.transpose, "tensor_tensor_scan": v.tensor_tensor_scan, "quantize_mx": v.quantize_mx,
+             "tensor_reduce": v.tensor_reduce, "activation": g.scalar.activation, "matmul_mx": g.tensor.matmul_mx, "iota": g.iota}
+    for o in ops:
+        if o["kind"] == "a":
+            nm, t, n = o["x"]
+            o["wait"] = (nm, n * len(topo.engines(T.cores[rank ^ STEP[t]], core)))
+            final.append(o["wait"])
+            continue
+        q = qs[o["e"]]
+        for j in o["need"]:
+            q.wait_ge(T.sem[ops[j]["wait"][0]], ops[j]["wait"][1])
+        a = [ap(x) for x in o["a"]]
+        if o["kind"] == "r":
+            dst = T.cores[rank ^ STEP[o["x"][1]]]
+            rid, pid = topo.addr(dst, core)
+            g.remote_dma(a[0], a[1], T.sem[o["x"][0]], T.sem.sent, pid, rid, topo.mask(core, dst))
+            sent += len(topo.engines(core, dst))
+        elif o["kind"] == "d":
+            o["wait"] = ("d%d" % nd, 16)
+            nd += 1
+            q.dma_start(a[0], a[1]).then_inc(T.sem[o["wait"][0]], 16)
+            final.append(o["wait"])
+        else:
+            ins = calls[o["m"]](*a, **{k: ap(x) for k, x in o["kw"].items()})
+            if o.get("sig"):
+                count[o["e"]] += 1
+                o["wait"] = ("e" + o["e"], count[o["e"]])
+                ins.then_inc(T.sem[o["wait"][0]], 1)
+    for nm, n in final + [("sent", sent)] + [("e" + e, count[e]) for e in ENG if count[e]]:
+        g.wait_ge(T.sem[nm], n)

@@ -44,7 +44,8 @@ _buf("RL", 1280, F32)
 _buf("WIN", 4 * 1008, BF)
 _buf("NW", 688, BF)
 _buf("PW", 688, F32)
-_buf("W TK", 432, F32)
+_buf("W", 432, F32)
+_buf("TK", 672, F32)
 _buf("EW", 1168, F32)
 _buf("TF TE", 672, BF)
 _buf("OLT", 640, F32)
@@ -180,13 +181,13 @@ def rank_program(g, core, T, topo):
     def pick(tbuf, row=0, cols=1):
         return IND(V(tbuf, 0, 224), O(PK + row, cols))
 
-    QF, HF, P32, M1C, R03, R1N, R124, MEC, INI, DM, NQ16 = [V("cf", i) for i in range(11)]
+    QF, HF, P32, M1C, R03, R1N, R124, MEC, INI, DM = [V("cf", i) for i in range(10)]
     PF = V("pf", 0)
     BJ, LEJ, CST, KW, JW, RM, B6, HI = 12, 16, 18, 32, 52, 64, 80, 88
     HB, M0, M1, NT32, NL32, V1, VT, VT1, BB = [V("sm", 32 * i, 32 * i + 32) for i in range(9)]
     N2, N3, WA, WB = 288, 324, 360, 396
-    OU, OT, PK, PKH, PKL, OI, OR, PK1, OO, OF, O4, O16, OP, OA, OMM, OK_, OF2, O42, O162 = \
-        0, 16, 52, 60, 0, 66, 72, 78, 80, 96, 112, 128, 144, 160, 192, 208, 272, 288, 304
+    OU, OT, PK, PKH, PKL, OI, OR, OO, OF, O4, O16, OP, OA, OMM, OK_, OF2, O42, O162 = \
+        0, 16, 52, 60, 0, 66, 72, 80, 96, 112, 128, 144, 160, 192, 208, 272, 288, 304
     OMF, OMB, OL = 0, 20, 40
     tmp = lambda i, n=6: V("lw", 12 * i, 12 * i + n)
     rm = lambda r: V("cf", RM + r)
@@ -217,29 +218,32 @@ def rank_program(g, core, T, topo):
     ts(O(OT, 34), V("ci", 16, 50), QF, A.add)
     ts(O(OT + 34, 1), QF, 17.0, A.mult, 17.0, A.add)
     ts(O(OT + 35, 1), QF, 17.0, A.mult, 17.0, A.add)
-    lin(V("PB", 0, 568), zb(568))
+    for b in range(3):
+        lin(V("EB", 512 * b, 512 * b + 512), zb(512))
     act(V("RK", 0, 576), IND(V("NT", 0, 290), O(OT, 36)))
     cp(O(OU, 8), V("ci", 8, 16))
     ts(O(OU + 8, 8), V("ci", 8, 16), 1.0, A.add)
     ts(V1, BB, HF, A.is_equal)
     ms(V("S", 640, 656), -BIG)
+    ms(V("EB", 1536, 2048), 0.0)
     ts(HB, V1, 2 * BIG, A.mult, -BIG, A.add)
     ts(M0, V1, -4465.5, A.mult, 4000.0, A.add)
-    ms(V("EB", 0, 2048), 0.0)
-    tr(V("TAB", 0, 576), V("RK", 0, 576))
     quant(V("UQ", 0, 128), V("US", 0, 128), V("UB", 0, 512))
+    quant(V("XQ0", 0, C), V("XS0", 0, C), V("X0", 0, 1280))
     for nm, o in (("UL", OU), ("UR", OU + 8)):
         cp(U32V(V(nm, 0, 128)), IND(U32V(V("UQ", 0, 128)), O(o, 8)))
         act(V(nm + "S", 0, 128), IND(V("US", 0, 128), O(o, 8)))
-    quant(V("XQ0", 0, C), V("XS0", 0, C), V("X0", 0, 1280))
-    for h in range(2):
-        tt(V("sm", 96 + 16 * h, 112 + 16 * h), V("TAB", 32, 544, 32), V("sm", 16 * h, 16 * h + 16), A.min)
-        tt(V("sm", 128 + 16 * h, 144 + 16 * h), V("NT", 17, 289, 17), V("sm", 16 * h, 16 * h + 16), A.min)
-    lin(NQ16, QF, -1.0 / 16)
+    tr(V("TAB", 0, 576), V("RK", 0, 576))
+    lin(V("cf", 92), QF, 1.0 / 16, 1.0)
+    lin(V("cf", 93), QF, -1.0 / 32, 1.0)
+    lin(V("cf", 94), QF, -2.0 ** -73)
     mm("P4", "UL", "ULS", 0, "XQ0", "XS0", 0, C)
     mm("P5", "UR", "URS", 0, "XQ0", "XS0", 0, C)
     cp(V("S", 0, 640, 2), V("P4", 0, C))
     act(V("S", 1, 640, 2), V("P5", 0, C))
+    for h in range(2):
+        tt(V("sm", 96 + 16 * h, 112 + 16 * h), V("TAB", 32, 544, 32), V("sm", 16 * h, 16 * h + 16), A.min)
+        tt(V("sm", 128 + 16 * h, 144 + 16 * h), V("NT", 17, 289, 17), V("sm", 16 * h, 16 * h + 16), A.min)
 
     rows = {1: (-1, 0, 0, -1, 0, 0, 0, 0), 2: (2, 2, -1, -2, 2, 2, 0, 650), 3: (0, -1, 0, 1, -1, -1, 0, -320),
             5: (0, 2, 0, 0, 2, 1, 1, 640), 6: (0, 1, 0, 0, 1, 0, 0, 0), 7: (0, 0, 512, 0, 0, 832, 1, 840),
@@ -249,7 +253,7 @@ def rank_program(g, core, T, topo):
     iota(V("lg", 8, 14), [[0, 2], [7, 3]], 5)
     iota(V("lg", 16, 22), [[0, 2], [112, 3]], 112)
     iota(V("cf", KW, KW + 20), [[16, 20]], 0)
-    iota(V("cf", JW, JW + 6), [[32, 3], [0, 2]], 0)
+    iota(V("cf", JW, JW + 12), [[32, 6], [0, 2]], 0)
     iota(V("PIT", 0, K2), [[1024, K2 // 2], [0, 2]], 1024)
     gfill(V("PIT", K2, 96))
     for q, co in rows.items():
@@ -258,11 +262,12 @@ def rank_program(g, core, T, topo):
                 iota(V("KZ", 32 * k + q, 32 * k + 32, 16), [[0, 2]], c)
     iota(V("TN", 0, 576), [[16, 6], [-1, 96]], 0)
     gfill(V("RA", 640, 656))
+    gfill(V("PB", 0, 1136))
     gfill(V("D0", 0, 192, 2), -(2 ** 23))
     gfill(V("SB", 0, 288))
     gfill(V("SB", 98, 192, 16), 1)
     gfill(V("SB", 192, 288, 16), 1)
-    for nm, a, n, c in (("DW", 0, 192, 0), ("W", 0, C, 1), ("CS", 0, 352, 0), ("EV", 0, 224, 0), ("TK", 0, 432, 0), ("EW", 0, C, 0),
+    for nm, a, n, c in (("DW", 0, 192, 0), ("W", 0, C, 1), ("CS", 0, 352, 0), ("EV", 0, 224, 0), ("TK", 192, 208, 0), ("EW", 0, C, 0),
                         ("FI", 0, 16, 0), ("FI", 336, 352, 0), ("NW", 0, C, 0), ("NW", C, 368, 1), ("NW", 368, 688, 0),
                         ("F1", 0, 32, 0), ("F1", 352, 384, 0), ("F2", 0, 32, 0), ("F2", 352, 384, 0)):
         gfill(V(nm, a, n), c)
@@ -270,83 +275,84 @@ def rank_program(g, core, T, topo):
     s16 = [16.0 ** -(i + 1) for i in range(5)]
     u1 = 2.0 ** -23
     co = [(0.0, -x) for x in s16] + [(0.0, -u1)] + [(s16[i] - s16[i + 1], 0.0) for i in range(4)] + \
-         [(s16[4], 0.0), (-u1, -u1 / 2), (u1, u1 / 4), (0.0, -u1 / 2)]
+         [(s16[4], 0.0), (-u1, -u1 / 2), (u1, u1 / 4), (-u1, -3 * u1 / 4)]
 
     def c1():
         ts(M1C, QF, 0.0, A.is_equal, 8000.0, A.mult)
-        for i in range(7):
+        for i in range(5):
             ts(V("cf", CST + i), QF, co[i][0], A.mult, co[i][1], A.add)
         ts(M1C, M1C, -4000.0, A.add)
+        for i in range(5, 7):
+            ts(V("cf", CST + i), QF, co[i][0], A.mult, co[i][1], A.add)
         ts(V("ID", 0, 128), V("IO", 0, 128), PF, A.is_equal)
         ts(M1, M0, M1C, A.max)
 
     def c2():
-        for i in range(7, 12):
+        for i in range(7, 14):
             lin(V("cf", CST + i), QF, co[i][0], co[i][1])
 
     def c2b():
-        for i in range(12, 14):
-            lin(V("cf", CST + i), QF, co[i][0], co[i][1])
-        lin(V("ON", 0, 640), zb(640), 1.0, 1.0)
+        lin(V("ON", 0, 640), zb(640), 1.0, -1.0)
+        lin(V("CAP", 639), zb(1))
 
     def c3():
         for b in range(4):
             cp(V("EB", 513 * b, 512 * (b + 1), 4), V("ID", 0, 128))
         ts(V("cf", RM, RM + 16), V("IO", 0, 16), QF, A.is_equal)
-        quant(V("EQ", 0, 512), V("ES", 0, 512), V("EB", 0, 2048))
+        ts(V("lg", 0, 6), V("lg", 0, 6), QF, A.add)
 
     def c4():
-        ts(V("lg", 0, 6), V("lg", 0, 6), QF, A.add)
-        ts(R124, rm(1), rm(2), A.add, rm(4), A.add)
         tt(V("lg", 0, 6), V("lg", 0, 6), V("lg", 8, 14), A.min)
-        ts(MEC, rm(0), 95.0, A.mult)
+        quant(V("EQ", 0, 512), V("ES", 0, 512), V("EB", 0, 2048))
         ts(V("ci", 8, 14), V("lg", 0, 6), HF, A.add)
-        ts(V("ME", 648, 656), zb(8), MEC, A.add)
-        ts(V("ci", 16, 22), V("ci", 8, 14), 1, A.bitwise_and)
-        ts(V("lg", 0, 6), V("lg", 0, 6), 16.0, A.mult)
-        tt(V("lg", 16, 22), V("lg", 16, 22), V("ci", 16, 22), A.mult)
-        ts(MEC, R124, 65536.0, A.mult, MEC, A.add)
-        tt(V("cf", B6, B6 + 6), V("lg", 0, 6), V("lg", 16, 22), A.add)
+        ts(R124, rm(1), rm(2), A.add, rm(4), A.add)
+        ts(MEC, rm(0), 95.0, A.mult)
+        ts(V("lg", 24, 30), V("lg", 0, 6), 16.0, A.mult)
 
     def c5():
+        ts(V("ci", 16, 22), V("ci", 8, 14), 1, A.bitwise_and)
         ts(V("cf", KW, KW + 20), V("cf", KW, KW + 20), QF, A.add)
-        ts(O(PK, 8), V("IO", 0, 8), V("cf", B6), A.add)
-        ts(O(PKH, 6), V("IO", 0, 6), V("cf", B6 + 1), A.add)
-        ts(O(PK1, 1), V("cf", B6 + 1), 1.0, A.add)
-        cp(O(PKL, 2), V("cf", B6 + 2, B6 + 6, 3))
+        ts(V("ME", 648, 656), zb(8), MEC, A.add)
+        ts(DM, QF, -8.0, A.add, 0.0, A.max)
+        ts(INI, rm(1), rm(4), A.add, 369.0, A.mult)
+        tt(V("lg", 16, 22), V("lg", 16, 22), V("ci", 16, 22), A.mult)
         ts(V("cf", BJ, BJ + 4), V("cf", KW, KW + 4), -4.0, A.mult, 4.0 * K2 - 2, A.add)
         ts(V("cf", LEJ, LEJ + 2), V("cf", KW + 4, KW + 6), -float(K2), A.add, 4.0, A.mult)
         ts(V("cf", HI, HI + 2), V("cf", KW + 4, KW + 6), 1.0 - K2, A.add, 4.0, A.mult)
         ts(V("cf", HI + 2, HI + 4), V("cf", KW + 4, KW + 6), 1.0 - K2, A.add, 2.0 * C, A.mult)
-        ts(DM, QF, -8.0, A.add, 0.0, A.max)
+        tt(V("cf", B6, B6 + 6), V("lg", 24, 30), V("lg", 16, 22), A.add)
+        ts(MEC, R124, 65536.0, A.mult, MEC, A.add)
 
     def c6():
-        ts(INI, rm(1), rm(4), A.add, 369.0, A.mult)
+        ts(O(PK, 8), V("IO", 0, 8), V("cf", B6), A.add)
+        ts(O(PKH, 4), V("IO", 0, 4), V("cf", B6 + 1), A.add)
+        for i, r in enumerate((0, 1, 2, 4)):
+            ts(O(PKL + 2 * i, 2), V("cf", B6 + 2, B6 + 6, 3), float(r), A.add)
         ts(V("JR", 0, 96), V("IO", 0, 96), rm(0), A.mult)
         ts(V("PIT", 0, 96), V("PIT", 0, 96), R124, A.mult)
         ts(INI, INI, rm(2), A.add)
         ts(V("cf", HI + 3), V("cf", HI + 3), DM, A.add)
         ts(tmp(22), V("cf", JW, JW + 6), P32, A.add, 336.0, A.add)
         ts(tmp(23), V("cf", JW, JW + 6), P32, A.add, 850.0, A.add)
-        ts(R1N, rm(1), -1.0, A.mult)
-        ts(R03, rm(0), rm(3), A.add)
 
     kt = lambda i: V("KT", 32 * i)
 
-    def c7():
+    def c6b():
         tr(V("KT", 0, 256), V("KZ", 0, 256))
+
+    def c7():
         ms(V("KP", 0, 576), 1.0)
         ts(V("CE", 640, 656), V("IO", 0, 16), kt(6), A.mult, kt(7), A.add)
+        ts(R1N, rm(1), -1.0, A.mult)
+        ts(R03, rm(0), rm(3), A.add)
+        ts(V("NTAU", 0, 576), V("TN", 0, 576), QF, A.add, 0.5, A.is_lt)
         ms(V("KP", 0, 576, 96), 0.0)
 
     def c7s():
         lin(V("CE", 0, 640, 2), V("IO", 0, C), kt(1), kt(2))
         lin(V("CE", 1, 640, 2), V("IO", 0, C), kt(4), kt(5))
-
-    def c8():
-        ts(V("RA", 0, 640, 2), zb(C), kt(0), A.add)
-        ts(V("RA", 1, 640, 2), zb(C), kt(3), A.add)
-        ts(V("NTAU", 0, 576), V("TN", 0, 576), QF, A.add, 0.5, A.is_lt)
+        lin(V("RA", 0, 640, 2), zb(C), 1.0, kt(0))
+        lin(V("RA", 1, 640, 2), zb(C), 1.0, kt(3))
 
     def c9():
         lin(V("SB", 194, 288, 16), zb(6), 1.0, 2.0 ** -20)
@@ -358,7 +364,7 @@ def rank_program(g, core, T, topo):
         act(V("PW", 368, 688), V("IO", 0, C))
 
     def row(c):
-        return IND(V("TK", 0, 432), O(c, 1))
+        return IND(V("TK", 0, 672), O(c, 2))
 
     for t in range(R):
         XQ, XS, F, ZQ, ZS = "XQ%d" % t, "XS%d" % t, "F%d" % t, "ZQ%d" % t, "ZS%d" % t
@@ -375,12 +381,9 @@ def rank_program(g, core, T, topo):
         def mf(b):
             return lambda: tt(V("WIN", 1008 * b + 368, 1008 * b + 688), IND(V("DH", C * b, C * b + C), O(OMF, 20, "of2")), V("DG", C * b, C * b + C), A.add)
 
-        def lists():
-            conv(F, C, "TF", 32)
-            cp(V("lg", 176, 208), IND(V("TF", 0, 672), O(PKL, 2)))
-            tt(V("lg", 176, 196), V("lg", 176, 196), V("cf", KW, KW + 20), A.add)
-            cp(O(OMF, 20, "of2"), V("lg", 176, 196))
-
+        l1 = [lambda: conv(F, C, "TF", 32),
+              lambda: tt(V("lg", 176, 208), IND(V("TF", 0, 672), O(PKL, 2)), V("cf", KW, KW + 32), A.add),
+              lambda: cp(O(OMF, 20, "of2"), V("lg", 176, 196))]
         l2 = [lambda: conv(F, C, "TE", 31),
               lambda: ts(V("lg", 208, 240), IND(V("TE", 0, 672), O(PKL, 2)), -321.0, A.mult, 320.0, A.add),
               lambda: tt(V("lg", 208, 228), V("lg", 208, 228), V("cf", KW, KW + 20), A.add),
@@ -391,14 +394,12 @@ def rank_program(g, core, T, topo):
             scan(V("RA", 638, "end", -2), V(F, 351, 31, -1), V("AL", 0, C), 0.0, A.mult, A.add)
 
         if t == 0:
-            fv = [[c1], [], [c3, dmm], [c4], [c5], [c6], [], [c7]]
-            fs = [[c2], [c2b], [lambda: lin(V("PB", 568, 1136), zb(568))], [dh(0)], [dh(1)], [dh(2)], [dh(3)], []]
-            late = [c8]
+            fv = [[c1], [], [c3], [c4, dmm], [c5], [c6], [c6b], [c7]]
+            fs = [[c2], [], [c2b], [], [dh(0)], [dh(1)], [dh(2)], [dh(3)]]
         else:
             dmm()
-            fv = [[lists], [], [l2[0]], [l2[1], mf(0)], [l2[2], mf(1)], [runs], [], [l2[3], mf(2)]]
+            fv = [[l1[0], l2[0], l1[1]], [], [l1[2]], [l2[1], mf(0)], [l2[2], mf(1)], [l2[3], runs], [], [mf(2)]]
             fs = [[dh(b // 2, ("DH", "DG")[b % 2])] for b in range(8)]
-            late = [mf(3)]
         neg = V("TAB", 17 * 32)
         cnt = V("lg", 240)
         cw = lambda i: V("cw", i)
@@ -411,25 +412,25 @@ def rank_program(g, core, T, topo):
                 ts(BB, HB, neg, A.min)
                 scan(V("sm", N2 + 1, N2 + 33), VT1, NL32, 2.0 ** 70, A.min, A.max)
                 tr(V("sm", N2, N2 + 32), BB)
-                ts(V("sm", WA, WA + 33), V("sm", N2, N2 + 33), -1.0, A.mult, 2.0 ** -69, A.max)
-                ts(V("sm", WB, WB + 33), V("sm", N2, N2 + 33), 0.5, A.mult)
-                tt(V("sm", WA, WA + 33), V("sm", WA, WA + 33), V("sm", WB, WB + 33), A.max)
-                ts(V("sm", WA, WA + 33), V("sm", WA, WA + 33), NQ16, A.mult)
-                tt(V("sm", N3, N3 + 33), V("sm", WA, WA + 33), V("sm", N2, N2 + 33), A.add)
+                ts(V("sm", WA, WA + 33), V("sm", N2, N2 + 33), V("cf", 92), A.mult)
+                ts(V("sm", WB, WB + 33), V("sm", N2, N2 + 33), V("cf", 93), A.mult)
+                ts(V("sm", N3, N3 + 33), V("sm", N2, N2 + 33), V("cf", 94), A.add)
+                tt(V("sm", WA, WA + 33), V("sm", WA, WA + 33), V("sm", WB, WB + 33), A.min)
+                tt(V("sm", N3, N3 + 33), V("sm", N3, N3 + 33), V("sm", WA, WA + 33), A.min)
             if it == 3:
-                scan(BB, VT1, V("sm", N2, N2 + 32), V("sm", N2 + 32), A.min, A.max)
                 lo = V("sm", 287)
                 ts(cw(14), lo, -1.0, A.mult, 2.0 ** -69, A.max)
                 ts(cw(14), lo, 0.5, A.mult, cw(14), A.max)
                 ts(V("cw", 0, 14), V("cf", CST, CST + 14), cw(14), A.mult)
-            if 3 <= it <= 6:
+                ts(init, cw(14), V("cf", CST + 6), A.mult, neg, A.add)
+            if 4 <= it <= 6:
                 ts(init, neg, cw(3 + it), A.add)
             if it == 7:
                 init = cw(11)
-                ts(cw(15), neg, cw(10), A.add)
-                ts(V("D", 0, 640), V("S", 0, 640), cw(15), A.add)
+                ts(V("D", 0, 640), V("S", 0, 640), neg, A.add, cw(10), A.add)
             if it == 8:
                 ts(init, neg, cw(12), A.add)
+                ts(cw(26), neg, -1.0, A.mult, cw(13), A.add)
             for f in fv[it - 1]:
                 f()
             out = V("so", 32 * (it % 2), 32 * (it % 2) + 32)
@@ -440,20 +441,20 @@ def rank_program(g, core, T, topo):
                     scan(out, VT1, NT32, V("TAB", 0), A.min, A.max)
                 else:
                     scan(out, VT1, V("sm", N3, N3 + 32), V("sm", N3 + 32), A.min, A.max)
+                    scan(BB, VT1, V("sm", N2, N2 + 32), V("sm", N2 + 32), A.min, A.max)
             else:
                 ts(V1, M0 if it == 8 else M1, cnt, A.is_le, cw(it - 3), A.mult)
                 tr(VT, V1)
                 scan(out, VT, zb(32), init, A.add, A.add)
             neg = V("so", 32 * (it % 2) + 31)
-        act(V("GT", 0, 640), V("D", 0, 640), AF.Sign, bias=neg, accum_out=cnt)
+        act(V("GT", 0, 640), V("D", 0, 640), AF.Sign, bias=neg)
         if t == 0:
             c7s()
         else:
             lin(V("ME", 0, 640), zb(640), 1.0, MEC)
-        ts(cw(26), neg, -1.0, A.mult, cw(13), A.add)
-        ts(V("GE", 0, 640), V("D", 0, 640), cw(26), A.is_gt, 2.0, A.mult)
-        ts(cw(27), cnt, -1.0, A.mult, -640.0, A.add)
-        scan(V("CAP", 0, 640), V("GT", 0, 640), V("ON", 0, 640), cw(27), A.add, A.add)
+        scan(BB, zb(32), VT, cw(26), A.add, A.subtract)
+        ts(V("GE", 0, 640), V("D", 0, 640), V("sm", 287), A.is_gt, 2.0, A.mult)
+        scan(V("CAP", 638, "end", -1), V("ON", 0, 639), V("GT", 639, 0, -1), 0.0, A.add, A.subtract)
         scan(V("PP", 0, 640), V("GE", 0, 640), V("CAP", 0, 640), -2.0 * K2, A.add, A.min)
         scan(V("CAP", 0, C), V("PP", 0, 640, 2), V("PP", 1, 640, 2), -1024.0, A.max, A.add)
         for c in range(4):
@@ -464,16 +465,17 @@ def rank_program(g, core, T, topo):
             rec("v", "tensor_reduce", [V("lg", 248 + c), V("GT", C * c, C * c + C), AxisListType.X, A.add])
         for c in range(2):
             ts(O(OI + 4 + c, 1), V("lg", 248 + c), -0.5, A.mult, V("cf", HI + 2 + c), A.add)
-        for f in late:
-            f()
         ts(O(OI, 4), V("lg", 244, 248), -1.0, A.mult, 320.0, A.add)
         cp(V("SV", 16, 112), IND(V("S", 0, 656), O(OI)))
         act(V("CJ", 0, 96), IND(V("CE", 0, 656), O(OI)))
         conv("SV", 96, "TS")
+        tt(V("ZJ", 16, 112), IND(V("RA", 0, 656), O(OI)), V("CJ", 0, 96), A.add)
         ts(V("lg", 0, 16), pick("TS"), -1.0, A.mult)
         for c in range(6):
             act(V("SG", 96 * c, 96 * c + 96), V("SV", 16, 112), AF.Sign, bias=V("lg", c))
-        tt(V("ZJ", 16, 112), IND(V("RA", 0, 656), O(OI)), V("CJ", 0, 96), A.add)
+        if t:
+            mf(3)()
+        conv("ZJ", 96, "TZ")
         lin(V("SRC", 0, 96), V("ZJ", 16, 112), rm(6))
         lin(V("LA", 0, 96), V("ZJ", 16, 112), R1N)
         lin(V("D0", 1, 192, 2), V("ZJ", 16, 112), rm(1))
@@ -481,60 +483,38 @@ def rank_program(g, core, T, topo):
             lin(V("ME", 0, 640), zb(640), 1.0, MEC)
         for c in range(0, 6, 2):
             tt(V("FL", 96 * c, 96 * c + 192), V("SG", 96 * c, 96 * c + 192), V("NTAU", 96 * c, 96 * c + 192), A.is_ge)
-        conv("ZJ", 96, "TZ")
-        scan(V("RB", 0, 576), V("KP", 0, 576), V("FL", 0, 576), 0.0, A.mult, A.add)
         tt(V("SRC", 0, 96), V("SRC", 0, 96), V("JR", 0, 96), A.add)
-        cp(O(OR), V("RB", 95, 576, 96))
+        scan(V("RB", 0, 576), V("KP", 0, 576), V("FL", 0, 576), 0.0, A.mult, A.add)
         cp(O(OO, 16), pick("TZ", 2))
+        tr(V("TZ1", 0, 96), V("ZJ", 17, 113))
+        cp(O(OR), V("RB", 95, 576, 96))
         cp(IND(V("INV", 16, 112), O(OR)), V("SRC", 0, 96))
         act(V("PIJ", 0, 96), IND(V("PIT", 0, 96), O(OR)))
         z = lambda r: V("TZ", r, 96, 16)
         lin(tmp(3), z(12), -1.0, 336.0)
+        tt(tmp(1), V("TZ1", 3, 96, 16), z(12), A.add)
+        tt(tmp(2), tmp(22), z(3), A.add)
         cp(V("INS", 0, 96, 2), V("INV", 17, 112, 2))
         act(V("INS", 1, 96, 2), V("INV", 16, 112, 2))
-        tr(V("TZ1", 0, 96), V("ZJ", 17, 113))
+        conv("INV", 96, "TP")
         tt(V("MJ", 16, 112), IND(V("INS", 0, 96), O(OR)), V("PIJ", 0, 96), A.add)
         lin(V("SB", 97, 192, 16), z(12), 1.0, 369.0)
         lin(tmp(21), z(1), 1.0, 1.0)
         if last:
             lin(V("SB", 100, 192, 16), z(12), 1.0, 369.0)
             lin(V("SB", 196, 288, 16), z(6), 1.0, 1.0)
-        tt(tmp(1), V("TZ1", 3, 96, 16), z(12), A.add)
-        cp(IND(V("ME", 0, 656), O(OI)), V("MJ", 16, 112))
-        tt(tmp(2), tmp(22), z(3), A.add)
-        tt(V("FJ", 16, 112), IND(V("ME", 0, 656), O(OO)), V("ZJ", 16, 112), A.add)
+        cp(O(OP, 16), pick("TP", 6))
         ts(tmp(1), tmp(1), 0.0, A.is_equal)
+        cp(IND(V("ME", 0, 656), O(OI)), V("MJ", 16, 112))
+        conv("MJ", 96, "TM")
+        tt(V("FJ", 16, 112), IND(V("ME", 0, 656), O(OO)), V("ZJ", 16, 112), A.add)
+        ts(O(OMM, 16), pick("TM"), 2.0, A.mult, 1.0, A.add)
         conv("FJ", 96, "TJ")
+        lin(V("SB", 193, 288, 16), V("TM", 4, 96, 16), 1.0 / 1024, 320.0)
         act(V("D1", 1, 192, 2), V("FJ", 16, 112))
         cp(O(OF, 16), pick("TJ"))
         ts(O(OF2, 16), pick("TJ"), 2.0, A.mult, 1.0, A.add)
-
-        def s1():
-            conv("MJ", 96, "TM")
-            ts(tmp(0), V("TJ", 4, 96, 16), 65536.0, A.not_equal)
-            ts(O(OMM, 16), pick("TM"), 2.0, A.mult, 1.0, A.add)
-
-        def s2():
-            conv("INV", 96, "TP")
-            cp(O(OP, 16), pick("TP", 6))
-
-        def s3():
-            tt(tmp(20), tmp(0), z(8), A.mult)
-            ts(tmp(0), tmp(20), 0.0, A.is_gt)
-            tt(tmp(1), tmp(1), tmp(0), A.max)
-            tt(tmp(2), tmp(2), tmp(0), A.mult)
-            tt(tmp(3), tmp(3), tmp(1), A.mult)
-            tt(V("SB", 96, 192, 16), tmp(23), tmp(1), A.mult)
-            tt(V("SB", 0, 96, 16), tmp(2), z(3), A.subtract)
-            tt(V("SB", 1, 96, 16), tmp(3), z(12), A.add)
-
-        def s4():
-            tr(V("RS", 16, 112), V("SB", 0, 96))
-            tr(V("VC", 0, 192), V("SB", 96, 288))
-
-        def s5():
-            conv("RS", 96, "TS")
-            cp(O(OA, 32), pick("TS", 0, 2))
+        ts(tmp(0), V("TJ", 4, 96, 16), 65536.0, A.not_equal)
 
         def gj(b):
             return lambda: act(V("GJ", 96 * b, 96 * b + 96), IND(V("DH", C * b, C * b + C), O(OP)))
@@ -542,11 +522,18 @@ def rank_program(g, core, T, topo):
         def jm(b):
             tt(V("WIN", 1008 * b + C, 1008 * b + 368), V("GJ", 96 * b, 96 * b + 96, 2), V("GJ", 96 * b + 1, 96 * b + 96, 2), A.add)
 
-        def s7():
-            lin(V("SB", 193, 288, 16), V("TM", 4, 96, 16), 1.0 / 1024, 320.0)
+        def s4():
+            tr(V("RS", 16, 112), V("SB", 0, 96))
+            tr(V("VC", 0, 192), V("SB", 96, 288))
 
-        side = [[s2], [], [s1], [s3], [], [s4], [s5], []]
-        sides = [[], [] if t else [c9], [gj(0)], [s7], [gj(1)], [gj(2)], [gj(3)], []]
+        post = [[lambda: tt(tmp(20), tmp(0), z(8), A.mult)],
+                [lambda: ts(tmp(0), tmp(20), 0.0, A.is_gt)],
+                [lambda: tt(tmp(1), tmp(1), tmp(0), A.max), lambda: tt(tmp(2), tmp(2), tmp(0), A.mult)],
+                [lambda: tt(tmp(3), tmp(3), tmp(1), A.mult), lambda: tt(V("SB", 96, 192, 16), tmp(23), tmp(1), A.mult),
+                 lambda: tt(V("SB", 0, 96, 16), tmp(2), z(3), A.subtract), lambda: jm(0)],
+                [lambda: tt(V("SB", 1, 96, 16), tmp(3), z(12), A.add)],
+                [s4], [lambda: conv("RS", 96, "TS"), lambda: jm(1)], []]
+        sides = [[], [] if t else [c9], [gj(0)], [], [gj(1)], [gj(2)], [gj(3)], []]
         la, fb, n = "LA", "FJ", 0
         for o, o2, on, on2 in ((OF, OF2, O4, O42), (O4, O42, O16, O162), (O16, O162, None, None)):
             fa = fb
@@ -560,31 +547,36 @@ def rank_program(g, core, T, topo):
                     lo_ = "LB" if la == "LA" else "LA"
                     tt(V(lo_, 0, 96), IND(V(la, 0, 96), O(o)), V("D0", 1, 192, 2), A.subtract)
                     la = lo_
-                scan(V("XO", 0, 192), V("D0", 0, 192), V("D1", 0, 192), 0.0, A.add, A.max)
-                if on and k == 1:
-                    conv(fa, 96, "TS")
+                if on and k == 2:
                     cp(O(on, 16), pick("TS"))
                     ts(O(on2, 16), pick("TS"), 2.0, A.mult, 1.0, A.add)
+                scan(V("XO", 0, 192), V("D0", 0, 192), V("D1", 0, 192), 0.0, A.add, A.max)
                 if on and k == 2:
-                    cp(V("D1", 1, 192, 2), V("XO", 1, 192, 2))
                     ts(V("D0", 1, 192, 2), V(la, 0, 96), -1.0, A.mult)
-                for f in sides[n] + side[n]:
+                    cp(V("D1", 1, 192, 2), V("XO", 1, 192, 2))
+                for f in sides[n] + post[n]:
                     f()
+                if on and k == 1:
+                    conv(fa, 96, "TS")
                 n += 1
             fb = fa
         act(V("XX", 96, 192), IND(V("XO", 0, 192), O(OMM)))
+        cp(O(OA, 32), pick("TS", 0, 2))
         cp(V("XX", 0, 96), V("XO", 1, 192, 2))
-        jm(0)
+        jm(2)
+        jm(3)
         tr(V("TX", 0, 192), V("XX", 0, 192))
-        jm(1)
         if t == 0:
             lin(V("RM0", 0, C), zb(C), 1.0, R03)
         for b in range(4):
             if t:
                 act(V("WIN", 1008 * b + 688, 1008 * b + 1008), V("P%d" % b, 0, C))
-                act(V("WIN", 1008 * b, 1008 * b + C), IND(V("WIN", 1008 * b + 368, 1008 * b + 1008), O(OMB, 20, "of2")))
             else:
                 act(V("WIN", 1008 * b, 1008 * b + C), V("P%d" % b, 0, C))
+        for b in range(4):
+            if t:
+                act(V("WIN", 1008 * b, 1008 * b + C), IND(V("WIN", 1008 * b + 368, 1008 * b + 1008), O(OMB, 20, "of2")))
+            else:
                 act(V("WIN", 1008 * b + 368, 1008 * b + 688), V("P%d" % b, 0, C))
         if t == 0:
             c10()
@@ -600,55 +592,51 @@ def rank_program(g, core, T, topo):
         tt(tmp(7, 12), V("TX", 2, 192, 16), V("TX", 4, 192, 16), A.subtract)
         tt(tmp(8), tmp(6), d2, A.mult)
         tt(tmp(9), V("DW", 2, 96, 16), z(3), A.is_equal)
-        tt(tmp(11), V("lw", 90, 96), z(5), A.subtract)
+        tt(tmp(12), V("lw", 90, 96), tmp(7), A.is_ge)
         tt(tmp(10), tmp(8), d1, A.add)
-        tt(tmp(12), tmp(7), z(5), A.subtract)
+        tt(tmp(13), d1, tmp(8), A.subtract)
+        tt(tmp(17), tmp(12), tmp(6), A.mult)
+        tt(tmp(14), tmp(12), z(1), A.mult)
+        tt(tmp(18), tmp(8), z(7), A.add)
         tt(tmp(10), tmp(10), tmp(9), A.mult)
-        tt(tmp(11), tmp(11), tmp(6), A.mult)
+        tt(tmp(11), tmp(8), tmp(20), A.add)
+        tt(tmp(13), tmp(13), tmp(12), A.mult)
+        tt(tmp(17), tmp(17), z(7), A.mult)
+        tt(tmp(18), tmp(18), tmp(12), A.subtract)
         tt(V("DW", 0, 96, 16), tmp(10), tmp(21), A.add)
         tt(V("DW", 3, 96, 16), tmp(10), tmp(21), A.add)
-        tt(tmp(12), tmp(11), tmp(12), A.is_ge)
-        tr(V("RW", 16, 112), V("DW", 0, 96))
-        tt(tmp(13), d1, tmp(8), A.subtract)
-        cp(IND(V("W", 0, 432), O(OA)), V("RW", 16, 112))
-        conv("RW", 96, "TP")
-        tt(tmp(13), tmp(13), tmp(12), A.mult)
-        tt(tmp(14), tmp(12), z(1), A.mult)
-        tt(tmp(17), tmp(12), tmp(6), A.mult)
-        scan(V("CS", 1, C + 1), V("W", 0, C), V("RM0", 0, C), 0.0, A.add, A.mult)
-        ts(O(OMM, 16), pick("TP", 2), -1.0, A.mult)
-        tt(tmp(13), tmp(13), tmp(8), A.add)
         tt(tmp(15), tmp(12), z(10), A.mult)
         tt(tmp(16), tmp(12), z(13), A.mult)
-        tt(tmp(14), tmp(14), tmp(20), A.add)
-        tt(tmp(17), tmp(17), z(7), A.mult)
-        tt(tmp(18), tmp(13), tmp(12), A.subtract)
+        tt(tmp(14), tmp(14), tmp(11), A.add)
+        tt(tmp(18), tmp(18), tmp(17), A.subtract)
+        tr(V("RW", 16, 112), V("DW", 0, 96))
         tt(V("DA", 1, 96, 16), tmp(15), z(9), A.add)
         tt(V("DA", 2, 96, 16), tmp(16), z(11), A.add)
-        tt(tmp(18), tmp(18), z(7), A.add)
         tt(V("DA", 0, 96, 16), tmp(14), tmp(13), A.add)
+        tt(V("DA", 3, 96, 16), tmp(18), tmp(13), A.add)
+        cp(IND(V("W", 0, 432), O(OA)), V("RW", 16, 112))
+        conv("RW", 96, "TP")
         if last:
             tt(V("DA", 4, 96, 16), tmp(15), z(9), A.add)
-        tt(V("DA", 3, 96, 16), tmp(18), tmp(17), A.subtract)
-        tt(V("EV", 112, 208), IND(V("CS", 0, 352), O(OA + 16)), V("VC", 0, 96), A.add)
+        scan(V("CS", 1, C + 1), V("W", 0, C), V("RM0", 0, C), 0.0, A.add, A.mult)
+        ts(O(OMM, 16), pick("TP", 2), -1.0, A.mult)
         tr(V("VA", 0, 96), V("DA", 0, 96))
-        jm(2)
+        tt(V("EV", 112, 208), IND(V("CS", 0, 352), O(OA + 16)), V("VC", 0, 96), A.add)
         tt(V("EV", 16, 112), IND(V("CS", 0, 352), O(OMM)), V("VA", 0, 96), A.add)
-        jm(3)
         conv("EV", 192, "TK", 16, 208)
         cp(O(OK_, 64), IND(V("TK", 0, 432), O(PKH, 4)))
         cp(IND(V("EW", 0, 1168), O(OK_, 12)), V("EV", 16, 208))
         cp(IND(V("EW", 0, 1168), O(OK_ + 48)), V("VC", 96, 192))
         ts(V("KE", 0, C), V("EW", 0, C), 0.0, A.is_equal)
         scan(V("FI", 16, 336), V("KE", 0, C), V("EW", 0, C), INI, A.mult, A.add)
+        conv("FI", C, "TK")
+        tt(V("lg", 64, 96), row(PKL), V("cf", KW, KW + 32), A.subtract)
+        tt(V("lg", 96, 128), row(PKL + 4), V("lg", 64, 96), A.mult)
+        tt(V("lg", 128, 160), row(PKL + 2), V("lg", 96, 128), A.subtract)
+        ts(O(OL, 20, "of2"), V("lg", 128, 148), -0.75, A.add)
         YQ, YS, NS = "YQ%d" % t, "YS%d" % t, "NS%d" % t
         for hf in (1, 0):
             o = O(OL + 10 * hf, 10, "of2")
-            conv("FI", H, "TK", 16 + H * hf, 208)
-            tt(V("lg", 96, 112), row(PKH), V("cf", KW + 10 * hf, KW + 10 * hf + 16), A.subtract)
-            tt(V("lg", 112, 128), row(PKH + 2), V("lg", 96, 112), A.mult)
-            tt(V("lg", 128, 144), row(PK1), V("lg", 112, 128), A.subtract)
-            ts(o, V("lg", 128, 138), -0.75, A.add)
             for b in range(4):
                 y, w = V("Y", 640 * hf + b, 640 * hf + 640, 4), IND(V("WIN", 1008 * b, 1008 * b + 688), o)
                 cp(y, w) if b < 2 else act(y, w)
@@ -660,48 +648,50 @@ def rank_program(g, core, T, topo):
                 rec("g", "remote", [V(Fn, 192, 352), V(NS, 0, H)], nw=0, kind="r", extra=("af%d" % t, t))
             else:
                 quant(V(ZQ, 0, H), V(ZS, 0, H), V("Y", 0, 640))
-            if last:
-                tt(V("lg", 144, 160), row(PKH + 4), V("lg", 112, 128), A.subtract)
-                ts(O(OMF + 10 * hf, 10, "of2"), V("lg", 144, 154), -0.75, A.add)
+        if last:
+            tt(V("lg", 128, 160), row(PKL + 6), V("lg", 96, 128), A.subtract)
+            ts(O(OMF, 20, "of2"), V("lg", 128, 148), -0.75, A.add)
         for hf in range(2):
             a = H * hf
             if hf:
                 rec("n", "arrive", [V(ZQ, H, C), V(ZS, H, C)], nw=2, kind="a", extra=("aq%d" % t, t, 2))
                 rec("n", "arrive", [V(Fn, 192, 352)], kind="a", extra=("af%d" % t, t, 1))
+            else:
+                act(V(Fn, 32, 192), IND(V("NW", 0, 688), O(OL, 10, "of2")))
             for b in range(4):
                 mm("P%d" % (4 + b), "WQ", "WS", b, ZQ, ZS, a, H)
                 mm("P%d" % b, "EQ", "ES", b, ZQ, ZS, a, H)
             for b in range(4):
                 act(V("RL", C * b + a, C * b + a + H), V("P%d" % (4 + b), 0, H), AF.Relu, scale=0.015625)
                 tt(V(Xn, 4 * a + b, 4 * a + 640, 4), V("P%d" % b, 0, H), V("RL", C * b + a, C * b + a + H), A.add)
-            if hf == 0:
-                act(V(Fn, 32, 192), IND(V("NW", 0, 688), O(OL, 10, "of2")))
-                lin(V(Fn, 191), zb(1))
+                if hf == 0 and b == 0:
+                    lin(V(Fn, 191), zb(1))
             if not last:
                 lin(V("BD", a + hf, a + H + 1), V(Fn, 31 + a + hf, 32 + a + H), -2 * BIG, BIG)
             quant(V(XQn, a, a + H), V(XSn, a, a + H), V(Xn, 4 * a, 4 * a + 640))
             if not last:
                 mm("P4", "UL", "ULS", 0, XQn, XSn, a, H)
                 mm("P5", "UR", "URS", 0, XQn, XSn, a, H)
+                if hf == 0 and t == 0:
+                    quant(V("VQ", 0, 128), V("VS", 0, 128), V("VB", 0, 512))
                 tt(V("S", 2 * a, 2 * a + C, 2), V("P4", 0, H), V("BD", a, a + H), A.min)
                 tt(V("S", 2 * a + 1, 2 * a + C, 2), V("P5", 0, H), V("BD", a + 1, a + H + 1), A.min)
                 if hf == 0:
                     gfill(V("W", 0, C), 1)
                     gfill(V("EW", 0, C))
-                    if t == 0:
-                        quant(V("VQ", 0, 128), V("VS", 0, 128), V("VB", 0, 512))
             else:
                 mm("P4", "VQ", "VS", 0, XQn, XSn, a, H)
                 dma("y", ("raw", T.oc[:, 4 * a:4 * a + 640]), U8V(V(XQn, a, a + H)))
+                if hf:
+                    for k in range(4):
+                        dma("s" if k % 2 else "y", ("raw", T.osc[4 * k:4 * k + 4, :]), ("rows", slice(32 * k, 32 * k + 4), V("XS3", 0, C)))
+                    cp(V("OLT", C, 640), V("F3", 32, 352))
+                    dma("y", ("raw", T.ol[:, C:640]), ("rows", slice(0, 128, 16), V("OLT", C, 640)))
                 act(V("YO", a, a + H), V("P4", 0, H))
                 dma("s", ("raw", T.y[:, a:a + H]), V("YO", a, a + H))
                 if hf == 0:
                     cp(V("OLT", 0, C), IND(V("PW", 0, 688), O(OMF, 20, "of2")))
                     dma("y", ("raw", T.ol[:, 0:C]), ("rows", slice(0, 128, 16), V("OLT", 0, C)))
-    cp(V("OLT", C, 640), V("F3", 32, 352))
-    for k in range(4):
-        dma("s" if k % 2 else "y", ("raw", T.osc[4 * k:4 * k + 4, :]), ("rows", slice(32 * k, 32 * k + 4), V("XS3", 0, C)))
-    dma("y", ("raw", T.ol[:, C:640]), ("rows", slice(0, 128, 16), V("OLT", C, 640)))
     emit(g, core, rank, T, topo, ops)
 
 
@@ -720,6 +710,10 @@ def emit(g, core, rank, T, topo, ops):
         if x[0] == "ind":
             return ap(x[1]).indirect(ap(x[2]))
         return ap(x[1]).bitcast(dt.uint8 if x[0] == "u8" else dt.uint32)
+
+    def engines(src):
+        es = [topo.engines(src, T.cores[T.rank_of(src) ^ s]) for s in STEP]
+        return [e for e in es[0] if all(e in x for x in es)]
 
     hist = {}
     for i, o in enumerate(ops):
@@ -763,7 +757,7 @@ def emit(g, core, rank, T, topo, ops):
     for o in ops:
         if o["kind"] == "a":
             nm, t, n = o["x"]
-            o["wait"] = (nm, n * len(topo.engines(T.cores[rank ^ STEP[t]], core)))
+            o["wait"] = (nm, n * len(engines(T.cores[rank ^ STEP[t]])))
             final.append(o["wait"])
             continue
         q = qs[o["e"]]
@@ -773,8 +767,8 @@ def emit(g, core, rank, T, topo, ops):
         if o["kind"] == "r":
             dst = T.cores[rank ^ STEP[o["x"][1]]]
             rid, pid = topo.addr(dst, core)
-            g.remote_dma(a[0], a[1], T.sem[o["x"][0]], T.sem.sent, pid, rid, topo.mask(core, dst))
-            sent += len(topo.engines(core, dst))
+            g.remote_dma(a[0], a[1], T.sem[o["x"][0]], T.sem.sent, pid, rid, sum(1 << e for e in engines(core)))
+            sent += len(engines(core))
         elif o["kind"] == "d":
             o["wait"] = ("d%d" % nd, 16)
             nd += 1

@@ -3,6 +3,8 @@ from concourse.mybir import dt, AluOpType as A, AxisListType, ActivationFunction
 C, H, K2, R = 320, 160, 88, 3
 STEP = [1, 2, 4]
 BIG = 2.0 ** 90
+U = 1.0 / 1024
+NA = (13, 16, 16)
 F32, BF, I32, U16, X4, U8 = "float32", "bfloat16", "int32", "uint16", "float8_e4m3fn_x4", "uint8"
 SCRATCH = {}
 SLOT = {}
@@ -13,10 +15,10 @@ def _buf(names, n, d, where="sbuf"):
         SCRATCH[s] = (where, [128, n], d)
 
 
-def _slots(buf, names, n, more=0):
+def _slots(buf, names, n, more=0, d=F32):
     for i, s in enumerate(names.split()):
         SLOT[s] = (buf, n * i)
-    _buf(buf, n * len(names.split()) + more, F32)
+    _buf(buf, n * len(names.split()) + more, d)
 
 
 _buf("P0 P1 P2 P3 P4 P5 P6 P7", 512, F32, "psum")
@@ -26,7 +28,7 @@ _buf("XS0 XS1 XS2 XS3 ZS0 ZS1 ZS2", C, U8)
 _buf("YQ0 YQ1 YQ2", H, X4)
 _buf("YS0 YS1 YS2", H, U8)
 _buf("NS0 NS1 NS2", H, BF)
-_buf("F1 F2 F3", 384, BF)
+_buf("F1 F2 F3", 416, BF)
 _buf("UB VB", 512, BF)
 _buf("UQ VQ UL UR", 128, X4)
 _buf("US VS ULS URS", 128, U8)
@@ -34,37 +36,50 @@ _buf("WQ EQ", 512, X4)
 _buf("WS ES", 512, U8)
 _buf("EB", 2048, BF)
 _buf("ID", 128, BF)
-_buf("IO S D CE RA ME", 656, F32)
-_buf("GT GE CAP PP ZB ON", 640, BF)
+_buf("CB", 1024, BF)
+_buf("CI", 1024, BF)
+_buf("CQ", 256, X4)
+_buf("CP", 256, U8)
+_buf("TA", 5 * 1280, BF)
+_buf("AQ", 5 * C, X4)
+_buf("AP", 5 * C, U8)
+_buf("TB", 3 * 768, BF)
+_buf("BQ", 3 * 192, X4)
+_buf("BP", 3 * 192, U8)
+_buf("SW", 656, F32)
+_buf("IO SM SC", 336, F32)
+_buf("M", 352, F32)
+_buf("TM", 704, F32)
+_buf("MW CW", 32, F32)
+_buf("CV", 224, F32)
+_buf("TC TR", 416, F32)
+_buf("EQV", 192, BF)
+_buf("MSK", 16, F32)
+_buf("MK GT GE CAP PP ZB", C, BF)
 _buf("JK", 1280, BF)
-_buf("SG NTAU FL KP RB TN", 576, BF)
-_buf("RK TAB", 576, F32)
-_buf("NT TG", 304, F32)
+_buf("YV KZ KT", C, F32)
 _buf("RL", 1280, F32)
 _buf("WIN", 4 * 1008, BF)
 _buf("NW", 688, BF)
 _buf("PW", 688, F32)
-_buf("W", 432, F32)
-_buf("TK", 672, F32)
-_buf("EW", 1168, F32)
-_buf("TF TE", 672, BF)
+_buf("W1 W2", 432, F32)
+_buf("TK", 704, F32)
+_buf("EW", 1536, F32)
+_buf("TF TE TQ", 704, BF)
 _buf("OLT", 640, F32)
 _buf("YO", C, F32)
-_buf("ci", 64, I32)
-_buf("cf", 128, F32)
-_buf("pf", 2, F32)
-_buf("sm", 448, F32)
+_buf("ci HI", 96, I32)
+_buf("cf", 96, F32)
+_buf("sm", 32, F32)
 _buf("lg", 256, F32)
-_buf("off", 320, U16)
-_buf("of2", 64, U16)
-_buf("cw", 32, F32)
-_buf("so", 64, F32)
+_buf("off", 448, U16)
 _buf("lw SB", 288, F32)
 _buf("GJ", 384, F32)
-_slots("PB", "SV ZJ MJ FJ FA FB FC INV RW RS", 112, 16)
-_slots("QA", "JR PIT PIJ CJ SRC INS LA LB TZ1 DW DA VA", 96)
-_slots("QB", "TS TZ TM TJ TP TX KZ KT EV XX D0 D1 XO VC", 256)
-_slots("QC", "BD AL AR RM0 KE CS FI", 352)
+_slots("PB", "FJ FA FB FC RW RS", 112, 16)
+_slots("QA", "LA LB DW VM WV VR VC TN XX UA UC N1 N2 N3", 96)
+_slots("QB", "TS TJ TP TX D0 D4 D16 D1 XO CJ MT FS FR DA VA", 224)
+_slots("QC", "CEL CER KE CS FI EV", 352)
+_slots("QE", "RA RB AL AR", 352, 0, BF)
 
 ENG = ["v", "s", "t", "g"]
 SEMAPHORES = ["e" + e for e in ENG] + ["d%d" % i for i in range(20)] + \
@@ -90,8 +105,8 @@ def U32V(w):
     return ("u32", w)
 
 
-def O(a, n=6, b="off"):
-    return V(b, a, a + n)
+def O(a, n=6):
+    return V("off", a, a + n)
 
 
 def touched(x):
@@ -108,15 +123,21 @@ def touched(x):
     return touched(x[-1])
 
 
+ROWS = {1: (0, -U, -U, 0, -U, -U), 2: (U, U, U / 2, U, 0, 0), 4: (-1, 0, 0, -1, 0, 0),
+        5: (0, U, U, 0, U, U), 6: (1, 0, 0, 1, 1, 0), 7: (1, 1, 1, 1, 1, 1), 8: (0, 0, 0, 0, 0, 1),
+        9: (-1, -1, 689, 1, 0, 2), 10: (2, 1, -687, -2, -1, 687), 11: (0, -U, 0, 0, -U, 0)}
+SINK = {0: (K2, 0), 1: (-1000 - 331 * U, U), 2: (-1000, 0), 3: (-1000, 0), 4: (-330, 0), 8: (1, 0), 9: (2, 0)}
+
+
 def rank_program(g, core, T, topo):
     rank = T.rank_of(core)
     if rank is None:
         return
     ops = []
 
-    def rec(e, meth, args, nw=1, kw=None, kind="c", extra=None):
+    def rec(e, meth, args, nw=1, kw=None, kind="c", extra=None, behind=None):
         kw = kw or {}
-        wr, rd = [], []
+        wr, rd = [], touched(behind)
         for i, a in enumerate(args):
             if i < nw and isinstance(a, tuple) and a[0] == "ind":
                 wr += touched(a[1])
@@ -130,7 +151,6 @@ def rank_program(g, core, T, topo):
                 wr += touched(a)
             else:
                 rd += touched(a)
-        wr += [r for r in rd if SCRATCH[r[0]][0] == "psum"]
         ops.append({"e": e, "m": meth, "a": args, "kw": kw, "wr": wr, "rd": rd, "kind": kind, "x": extra})
 
     def ts(o, i, s1, op0, s2=None, op1=None):
@@ -148,6 +168,9 @@ def rank_program(g, core, T, topo):
     def tr(o, i):
         rec("v", "transpose", [o, i])
 
+    def red(o, i, op):
+        rec("v", "tensor_reduce", [o, i, AxisListType.X, op])
+
     def scan(o, d0, d1, init, op0, op1):
         rec("v", "tensor_tensor_scan", [o, d0, d1, init, op0, op1])
 
@@ -164,535 +187,568 @@ def rank_program(g, core, T, topo):
     def gfill(o, c=0):
         iota(o, [[0, len(range(o[2], o[3], o[4]))]], c)
 
-    def quant(q, s, i):
-        rec("v", "quantize_mx", [q, s, i], nw=2)
+    def quant(q, s, x, a, n):
+        rec("v", "quantize_mx", [V(q, a, a + n), V(s, a, a + n), V(x[0], x[1], x[1] + 4 * n)], nw=2)
 
-    def mm(p, w, ws, k, x, xs, a, n):
-        rec("t", "matmul_mx", [V(p, 0, n), V(w, 128 * k, 128 * k + 128), V(ws, 128 * k, 128 * k + 128), V(x, a, a + n), V(xs, a, a + n), True, True])
+    def mm(p, w, ws, k, x, xs, a, n, start=True, stop=True):
+        rec("t", "matmul_mx", [V(p, 0, n), V(w, 128 * k, 128 * k + 128), V(ws, 128 * k, 128 * k + 128), V(x, a, a + n), V(xs, a, a + n), start, stop],
+            extra=None if start else "acc")
 
-    def dma(e, o, i):
-        rec(e, "dma_start", [o, i], kind="d")
+    def dma(e, o, i, behind=None):
+        rec(e, "dma_start", [o, i], kind="d", behind=behind)
 
-    def conv(src, n, tbuf, a=16, at=None):
-        at = n if at is None else at
-        tr(V(tbuf, 0, n), V(src, a, a + n))
-        tr(V(tbuf, at, at + n + 32), V(src, a - 16, a + n + 16))
+    def conv(src, n, tbuf, a=16, at=0):
+        tr(V(tbuf, at, at + n), V(src, a, a + n))
+        tr(V(tbuf, at + n, at + 2 * n + 32), V(src, a - 16, a + n + 16))
 
-    def pick(tbuf, row=0, cols=1):
-        return IND(V(tbuf, 0, 224), O(PK + row, cols))
+    PKS = {}
+    for n, r in ((160, 0), (192, 0), (96, 0), (96, 6), (96, 3), (160, 7), (160, 1), (160, 2)):
+        PKS[n, r] = 2 * len(PKS)
+    PKA, PKE, OU, OREP = 16, 18, 20, 36
+    OI, OR, O1, O4, O4D, O16, O16D, O1D, OP, OA, OMM, OK_, OL, OPL, OMF, OMB, OSA, OSB = \
+        48, 64, 80, 96, 112, 128, 144, 160, 176, 192, 224, 240, 272, 304, 336, 368, 400, 416
+    HO = lambda base, h: O(base + 16 * h, 10)
 
-    QF, HF, P32, M1C, R03, R1N, R124, MEC, INI, DM = [V("cf", i) for i in range(10)]
-    PF = V("pf", 0)
-    BJ, LEJ, CST, KW, JW, RM, B6, HI = 12, 16, 18, 32, 52, 64, 80, 88
-    HB, M0, M1, NT32, NL32, V1, VT, VT1, BB = [V("sm", 32 * i, 32 * i + 32) for i in range(9)]
-    N2, N3, WA, WB = 288, 324, 360, 396
-    OU, OT, PK, PKH, PKL, OI, OR, OO, OF, O4, O16, OP, OA, OMM, OK_, OF2, O42, O162 = \
-        0, 16, 52, 60, 0, 66, 72, 80, 96, 112, 128, 144, 160, 192, 208, 272, 288, 304
-    OMF, OMB, OL = 0, 20, 40
+    def pick(tbuf, n, row=0, at=0):
+        return IND(V(tbuf, at, at + 2 * n + 32), O(PKS[n, row], 1))
+
+    QF, HF, P32, G16, PF = [V("cf", i) for i in range(5)]
+    KB, KW, RJ, J2, PR, CC = 8, 16, 48, 64, 68, 80
     tmp = lambda i, n=6: V("lw", 12 * i, 12 * i + n)
-    rm = lambda r: V("cf", RM + r)
     zb = lambda n: V("ZB", 0, n)
+    kt = lambda i: V("KT", 32 * i)
+    fa_ = lambda h: 32 + 192 * h
+    rj = V("cf", RJ, RJ + 6)
 
-    dma("y", V("X0", 0, 1280), ("raw", T.x[:]))
     dma("s", V("UB", 0, 512), ("raw", T.u[:]))
-    dma("y", U8V(V("WQ", 0, 512)), ("raw", T.wc[:]))
-    dma("y", V("WS", 0, 512), ("raw", T.ws[:]))
-    dma("y", V("VB", 0, 512), ("raw", T.v[:]))
+    dma("y", V("X0", 0, 640), ("raw", T.x[:, 0:640]))
+    dma("s", V("X0", 640, 1280), ("raw", T.x[:, 640:1280]))
+    dma("y", U8V(V("WQ", 0, 512)), ("raw", T.wc[:]), V("X0", 0, 1280))
+    dma("y", V("WS", 0, 512), ("raw", T.ws[:]), V("X0", 0, 1280))
+    dma("y", V("VB", 0, 512), ("raw", T.v[:]), V("X0", 0, 1280))
     iota(V("ci", 0), [[0, 1]], 0, 1)
-    iota(V("ci", 16, 50), [[17, 17], [0, 2]], 1)
     iota(V("ci", 8, 16), [[16, 8]], 0)
-    iota(BB, [[1, 2], [0, 16]], 0)
+    iota(V("cf", J2, J2 + 2), [[16, 2]], 0)
     iota(PF, [[0, 1]], 0, 1)
-    iota(V("IO", 0, 656), [[1, 656]], 0)
-    ms(zb(640), 0.0)
-    ms(V("KZ", 0, 256), 0.0)
-    ms(V("TG", 0, 144), 0.5)
-    ms(V("TG", 144, 304), 2.0)
-    ms(V("NT", 140), 0.0)
+    iota(V("CI", 0, 512), [[16, 8], [0, 64]], 0)
+    iota(V("IO", 0, 336), [[1, 336]], 0)
+    iota(V("CI", 512, 1024), [[4, 32], [0, 16]], 0)
+    iota(V("cf", KW, KW + 32), [[16, 32]], 0)
+    iota(rj, [[32, 3], [0, 2]], 0)
+    iota(V("ci", 24, 36), [[1, 12]], -1)
+    ms(zb(C), 0.0)
+    ms(V("KZ", 0, C), 0.0)
+    for a in range(0, 2048, 256):
+        act(V("EB", a, a + 256), zb(256))
+    for nm, a, n, c in (("M", 0, 16, 0.0), ("M", 336, 352, 0.0), ("SM", C, 336, -BIG),
+                        ("SC", C, 336, -BIG), ("CV", 0, 16, -BIG), ("SW", 640, 656, -BIG)):
+        ms(V(nm, a, n), c)
     ts(V("ci", 1), V("ci", 0), 15, A.bitwise_and)
     ts(V("ci", 2), V("ci", 0), 4, A.arith_shift_right, 1, A.bitwise_and)
     ts(V("ci", 3), V("ci", 0), 31, A.bitwise_and)
-    scan(V("NT", 0, 140), V("TG", 0, 140), zb(140), 2.0 ** 71, A.mult, A.add)
-    cp(V("cf", 0, 3), V("ci", 1, 4))
-    scan(V("NT", 141, 290), V("TG", 144, 293), zb(149), -2.0 ** -70, A.mult, A.add)
-    ts(O(OT, 34), V("ci", 16, 50), QF, A.add)
-    ts(O(OT + 34, 1), QF, 17.0, A.mult, 17.0, A.add)
-    ts(O(OT + 35, 1), QF, 17.0, A.mult, 17.0, A.add)
-    for b in range(3):
-        lin(V("EB", 512 * b, 512 * b + 512), zb(512))
-    act(V("RK", 0, 576), IND(V("NT", 0, 290), O(OT, 36)))
+    ts(V("ci", 4), V("ci", 0), 112, A.bitwise_and)
     cp(O(OU, 8), V("ci", 8, 16))
     ts(O(OU + 8, 8), V("ci", 8, 16), 1.0, A.add)
-    ts(V1, BB, HF, A.is_equal)
-    ms(V("S", 640, 656), -BIG)
-    ms(V("EB", 1536, 2048), 0.0)
-    ts(HB, V1, 2 * BIG, A.mult, -BIG, A.add)
-    ts(M0, V1, -4465.5, A.mult, 4000.0, A.add)
-    quant(V("UQ", 0, 128), V("US", 0, 128), V("UB", 0, 512))
-    quant(V("XQ0", 0, C), V("XS0", 0, C), V("X0", 0, 1280))
+    cp(V("cf", 0, 4), V("ci", 1, 5))
+    ts(V("cf", J2, J2 + 2), V("cf", J2, J2 + 2), QF, A.add)
+    ts(V("ci", 16, 18), V("cf", J2, J2 + 2), HF, A.add)
+    ts(V("ci", 18, 20), V("ci", 16, 18), 1, A.bitwise_and)
+    ts(V("cf", J2 + 2, J2 + 4), V("cf", J2, J2 + 2), 16.0, A.mult)
+    pn = {160: 0, 192: 1, 96: 2, 288: 3}
+    for n, i in pn.items():
+        ts(V("cf", PR + 2 * i, PR + 2 * i + 2), V("ci", 18, 20), n + 16.0, A.mult)
+        tt(V("cf", PR + 2 * i, PR + 2 * i + 2), V("cf", PR + 2 * i, PR + 2 * i + 2), V("cf", J2 + 2, J2 + 4), A.add)
+    for (n, r), o in PKS.items():
+        ts(O(o, 1), V("cf", PR + 2 * pn[n]), float(r), A.add, 2 * n + 31.0, A.min)
+    ts(O(PKE, 2), V("cf", PR + 6, PR + 8), 607.0, A.min)
+    for r in range(2):
+        ts(O(PKA + r, 1), V("cf", PR + 4), float(r), A.add, 223.0, A.min)
+    ts(O(OREP, 12), V("ci", 24, 36), 0.0, A.max)
+    for k in range(2):
+        ts(V("CB", 512 * k, 512 * k + 512), V("CI", 512 * k, 512 * k + 512), G16, A.is_equal)
+        quant("CQ", "CP", ("CB", 512 * k), 128 * k, 128)
+    ts(V("ID", 0, 128), V("IO", 0, 128), PF, A.is_equal)
+    for b in range(4):
+        cp(V("EB", 513 * b, 512 * (b + 1), 4), V("ID", 0, 128))
+    quant("EQ", "ES", ("EB", 0), 0, 512)
+    ts(V("cf", KW, KW + 32), V("cf", KW, KW + 32), QF, A.add)
+    ts(V("cf", KB, KB + 6), V("cf", KW, KW + 6), 0.5, A.add)
+    ts(V("MSK", 0, 16), V("IO", 0, 16), QF, A.is_gt)
+    table = {}
+    for q, co in ROWS.items():
+        for k, c in enumerate(co):
+            table[q, k] = c
+    for q, co in SINK.items():
+        table[q, 6], table[q, 7] = co
+    table[0, 8], table[1, 9] = U, 1
+    for (q, k), c in table.items():
+        if c:
+            iota(V("KZ", 32 * k + q, 32 * k + 32, 16), [[0, 2]], int(c * 2048))
+    tr(V("KT", 0, C), V("KZ", 0, C))
+    ts(V("KT", 0, C, 32), V("KT", 0, C, 32), 1.0 / 2048, A.mult)
+    ts(rj, rj, P32, A.add)
+    ts(V("ci", 40, 46), rj, 0.5, A.mult, -0.25, A.add)
+    ts(V("XO", 184, 200, 2), V("IO", 0, 8), kt(7), A.mult, kt(6), A.add)
+    for i, (a, b, s) in enumerate(((1, 4, 1), (4, 13, 4), (16, 49, 16))):
+        ts(V("cf", CC + 3 * i, CC + 3 * i + 3), V("IO", a, b, s), kt(9), A.mult, U, A.mult)
+    ts(V("cf", CC + 9), kt(9), -47 * U, A.mult)
+    ts(V("FJ", 104, 112), V("XO", 184, 200, 2), V("cf", CC + 9), A.add)
+    ts(tmp(22), rj, 336.0, A.add)
+    ts(tmp(23), V("ci", 40, 46), 322.0, A.add)
+    lin(V("CEL", 0, 336), V("IO", 0, 336), kt(0), kt(2))
+    lin(V("CER", 0, 336), V("IO", 0, 336), kt(3), kt(5))
+    lin(V("AL", 0, H), zb(H), 1.0, kt(1))
+    lin(V("AR", 0, H), zb(H), 1.0, kt(4))
+    act(V("PW", 0, C), V("IO", 0, C))
+    lin(V("PW", 368, 688), V("IO", 0, C), -1.0, C - 1.0)
+    for nm, a, n, c in (("CAP", C - 1, C, K2), ("CV", 208, 224, 0), ("FJ", 0, 16, 0), ("PB", 112, 688, 0), ("D0", 0, 192, -(2 ** 23)),
+                        ("D4", 0, 192, -(2 ** 23)), ("D16", 0, 192, -(2 ** 23)),
+                        ("SB", 0, 288, 0), ("DW", 0, 96, 0), ("DA", 0, 192, 0), ("W1", 0, 432, 0), ("W2", C, 432, 0),
+                        ("CS", 0, 352, 0), ("EV", 0, 352, 0), ("EW", 0, C, 1), ("FI", 0, 16, 0), ("FI", 336, 352, 0), ("NW", 0, C, 0),
+                        ("NW", C, 368, 1), ("NW", 368, 688, 0), ("RA", 0, 352, 0), ("RB", 0, 352, 0), ("SW", 0, 640, 0), ("PW", C, 368, 0)):
+        gfill(V(nm, a, n), c)
+    gfill(V("OLT", C + H - 1, 640, H))
+    for nm in ("F1", "F2"):
+        for a in (0, 192, 384):
+            gfill(V(nm, a, a + 32))
+    ts(V("SB", 192, 288, 16), rj, 1200.0, A.add, U, A.mult)
+    cp(V("DA", 97, 192, 16), tmp(23))
+
+    quant("UQ", "US", ("UB", 0), 0, 128)
     for nm, o in (("UL", OU), ("UR", OU + 8)):
         cp(U32V(V(nm, 0, 128)), IND(U32V(V("UQ", 0, 128)), O(o, 8)))
         act(V(nm + "S", 0, 128), IND(V("US", 0, 128), O(o, 8)))
-    tr(V("TAB", 0, 576), V("RK", 0, 576))
-    lin(V("cf", 92), QF, 1.0 / 16, 1.0)
-    lin(V("cf", 93), QF, -1.0 / 32, 1.0)
-    lin(V("cf", 94), QF, -2.0 ** -73)
-    mm("P4", "UL", "ULS", 0, "XQ0", "XS0", 0, C)
-    mm("P5", "UR", "URS", 0, "XQ0", "XS0", 0, C)
-    cp(V("S", 0, 640, 2), V("P4", 0, C))
-    act(V("S", 1, 640, 2), V("P5", 0, C))
     for h in range(2):
-        tt(V("sm", 96 + 16 * h, 112 + 16 * h), V("TAB", 32, 544, 32), V("sm", 16 * h, 16 * h + 16), A.min)
-        tt(V("sm", 128 + 16 * h, 144 + 16 * h), V("NT", 17, 289, 17), V("sm", 16 * h, 16 * h + 16), A.min)
+        quant("XQ0", "XS0", ("X0", 640 * h), H * h, H)
+    mm("P5", "UR", "URS", 0, "XQ0", "XS0", 0, C)
+    mm("P4", "UL", "ULS", 0, "XQ0", "XS0", 0, C)
+    act(V("SC", 0, C), V("P5", 0, C))
+    tt(V("M", 16, 16 + C), V("P4", 0, C), V("SC", 0, C), A.max)
+    act(V("SM", 0, C), V("P4", 0, C))
+    for h in range(2):
+        conv("M", H, "TM", 16 + H * h, 352 * h)
+        cp(V("MW", 16 * h, 16 * h + 16), pick("TM", H, 0, 352 * h))
+    quant("VQ", "VS", ("VB", 0), 0, 128)
 
-    rows = {1: (-1, 0, 0, -1, 0, 0, 0, 0), 2: (2, 2, -1, -2, 2, 2, 0, 650), 3: (0, -1, 0, 1, -1, -1, 0, -320),
-            5: (0, 2, 0, 0, 2, 1, 1, 640), 6: (0, 1, 0, 0, 1, 0, 0, 0), 7: (0, 0, 512, 0, 0, 832, 1, 840),
-            8: (0, 0, 512, 0, 0, 0, 1, 520), 9: (0, 1, 369, 0, 1, 1, 0, 1), 10: (1, 0, -369, -1, 0, 369, 0, 0),
-            11: (0, 0, 1, 0, 0, -1, 0, 1), 12: (1, 1, 0, 0, 1, 1, 0, 1), 13: (0, 0, -2, 0, 0, 2, 0, 0)}
-    iota(V("lg", 0, 6), [[16, 2], [0, 3]], 0)
-    iota(V("lg", 8, 14), [[0, 2], [7, 3]], 5)
-    iota(V("lg", 16, 22), [[0, 2], [112, 3]], 112)
-    iota(V("cf", KW, KW + 20), [[16, 20]], 0)
-    iota(V("cf", JW, JW + 12), [[32, 6], [0, 2]], 0)
-    iota(V("PIT", 0, K2), [[1024, K2 // 2], [0, 2]], 1024)
-    gfill(V("PIT", K2, 96))
-    for q, co in rows.items():
-        for k, c in enumerate(co):
-            if c:
-                iota(V("KZ", 32 * k + q, 32 * k + 32, 16), [[0, 2]], c)
-    iota(V("TN", 0, 576), [[16, 6], [-1, 96]], 0)
-    gfill(V("RA", 640, 656))
-    gfill(V("PB", 0, 1136))
-    gfill(V("D0", 0, 192, 2), -(2 ** 23))
-    gfill(V("SB", 0, 288))
-    gfill(V("SB", 98, 192, 16), 1)
-    gfill(V("SB", 192, 288, 16), 1)
-    for nm, a, n, c in (("DW", 0, 192, 0), ("W", 0, C, 1), ("CS", 0, 352, 0), ("EV", 0, 224, 0), ("TK", 192, 208, 0), ("EW", 0, C, 0),
-                        ("FI", 0, 16, 0), ("FI", 336, 352, 0), ("NW", 0, C, 0), ("NW", C, 368, 1), ("NW", 368, 688, 0),
-                        ("F1", 0, 32, 0), ("F1", 352, 384, 0), ("F2", 0, 32, 0), ("F2", 352, 384, 0)):
-        gfill(V(nm, a, n), c)
-
-    s16 = [16.0 ** -(i + 1) for i in range(5)]
-    u1 = 2.0 ** -23
-    co = [(0.0, -x) for x in s16] + [(0.0, -u1)] + [(s16[i] - s16[i + 1], 0.0) for i in range(4)] + \
-         [(s16[4], 0.0), (-u1, -u1 / 2), (u1, u1 / 4), (-u1, -3 * u1 / 4)]
-
-    def c1():
-        ts(M1C, QF, 0.0, A.is_equal, 8000.0, A.mult)
-        for i in range(5):
-            ts(V("cf", CST + i), QF, co[i][0], A.mult, co[i][1], A.add)
-        ts(M1C, M1C, -4000.0, A.add)
-        for i in range(5, 7):
-            ts(V("cf", CST + i), QF, co[i][0], A.mult, co[i][1], A.add)
-        ts(V("ID", 0, 128), V("IO", 0, 128), PF, A.is_equal)
-        ts(M1, M0, M1C, A.max)
-
-    def c2():
-        for i in range(7, 14):
-            lin(V("cf", CST + i), QF, co[i][0], co[i][1])
-
-    def c2b():
-        lin(V("ON", 0, 640), zb(640), 1.0, -1.0)
-        lin(V("CAP", 639), zb(1))
-
-    def c3():
-        for b in range(4):
-            cp(V("EB", 513 * b, 512 * (b + 1), 4), V("ID", 0, 128))
-        ts(V("cf", RM, RM + 16), V("IO", 0, 16), QF, A.is_equal)
-        ts(V("lg", 0, 6), V("lg", 0, 6), QF, A.add)
-
-    def c4():
-        tt(V("lg", 0, 6), V("lg", 0, 6), V("lg", 8, 14), A.min)
-        quant(V("EQ", 0, 512), V("ES", 0, 512), V("EB", 0, 2048))
-        ts(V("ci", 8, 14), V("lg", 0, 6), HF, A.add)
-        ts(R124, rm(1), rm(2), A.add, rm(4), A.add)
-        ts(MEC, rm(0), 95.0, A.mult)
-        ts(V("lg", 24, 30), V("lg", 0, 6), 16.0, A.mult)
-
-    def c5():
-        ts(V("ci", 16, 22), V("ci", 8, 14), 1, A.bitwise_and)
-        ts(V("cf", KW, KW + 20), V("cf", KW, KW + 20), QF, A.add)
-        ts(V("ME", 648, 656), zb(8), MEC, A.add)
-        ts(DM, QF, -8.0, A.add, 0.0, A.max)
-        ts(INI, rm(1), rm(4), A.add, 369.0, A.mult)
-        tt(V("lg", 16, 22), V("lg", 16, 22), V("ci", 16, 22), A.mult)
-        ts(V("cf", BJ, BJ + 4), V("cf", KW, KW + 4), -4.0, A.mult, 4.0 * K2 - 2, A.add)
-        ts(V("cf", LEJ, LEJ + 2), V("cf", KW + 4, KW + 6), -float(K2), A.add, 4.0, A.mult)
-        ts(V("cf", HI, HI + 2), V("cf", KW + 4, KW + 6), 1.0 - K2, A.add, 4.0, A.mult)
-        ts(V("cf", HI + 2, HI + 4), V("cf", KW + 4, KW + 6), 1.0 - K2, A.add, 2.0 * C, A.mult)
-        tt(V("cf", B6, B6 + 6), V("lg", 24, 30), V("lg", 16, 22), A.add)
-        ts(MEC, R124, 65536.0, A.mult, MEC, A.add)
-
-    def c6():
-        ts(O(PK, 8), V("IO", 0, 8), V("cf", B6), A.add)
-        ts(O(PKH, 4), V("IO", 0, 4), V("cf", B6 + 1), A.add)
-        for i, r in enumerate((0, 1, 2, 4)):
-            ts(O(PKL + 2 * i, 2), V("cf", B6 + 2, B6 + 6, 3), float(r), A.add)
-        ts(V("JR", 0, 96), V("IO", 0, 96), rm(0), A.mult)
-        ts(V("PIT", 0, 96), V("PIT", 0, 96), R124, A.mult)
-        ts(INI, INI, rm(2), A.add)
-        ts(V("cf", HI + 3), V("cf", HI + 3), DM, A.add)
-        ts(tmp(22), V("cf", JW, JW + 6), P32, A.add, 336.0, A.add)
-        ts(tmp(23), V("cf", JW, JW + 6), P32, A.add, 850.0, A.add)
-
-    kt = lambda i: V("KT", 32 * i)
-
-    def c6b():
-        tr(V("KT", 0, 256), V("KZ", 0, 256))
-
-    def c7():
-        ms(V("KP", 0, 576), 1.0)
-        ts(V("CE", 640, 656), V("IO", 0, 16), kt(6), A.mult, kt(7), A.add)
-        ts(R1N, rm(1), -1.0, A.mult)
-        ts(R03, rm(0), rm(3), A.add)
-        ts(V("NTAU", 0, 576), V("TN", 0, 576), QF, A.add, 0.5, A.is_lt)
-        ms(V("KP", 0, 576, 96), 0.0)
-
-    def c7s():
-        lin(V("CE", 0, 640, 2), V("IO", 0, C), kt(1), kt(2))
-        lin(V("CE", 1, 640, 2), V("IO", 0, C), kt(4), kt(5))
-        lin(V("RA", 0, 640, 2), zb(C), 1.0, kt(0))
-        lin(V("RA", 1, 640, 2), zb(C), 1.0, kt(3))
-
-    def c9():
-        lin(V("SB", 194, 288, 16), zb(6), 1.0, 2.0 ** -20)
-
-    def c10():
-        lin(V("AL", 0, C), zb(C), 1.0, kt(0))
-        lin(V("AR", 0, C), zb(C), 1.0, kt(3))
-        act(V("PW", 0, 368), V("IO", 0, 368))
-        act(V("PW", 368, 688), V("IO", 0, C))
-
-    def row(c):
-        return IND(V("TK", 0, 672), O(c, 2))
+    win = lambda b, a, n=C: V("WIN", 1008 * b + a, 1008 * b + a + n)
+    winr = lambda b: V("WIN", 1008 * b + 1007, 1008 * b + 687, -1)
 
     for t in range(R):
         XQ, XS, F, ZQ, ZS = "XQ%d" % t, "XS%d" % t, "F%d" % t, "ZQ%d" % t, "ZS%d" % t
         Fn, Xn, XQn, XSn = "F%d" % (t + 1), "X%d" % (t + 1), "XQ%d" % (t + 1), "XS%d" % (t + 1)
         last = t == R - 1
-
-        def dmm():
-            for b in range(4):
-                mm("P%d" % b, "EQ", "ES", b, XQ, XS, 0, C)
-
-        def dh(b, nm="DH"):
-            return lambda: lin(V(nm, C * b, C * b + C), V("P%d" % b, 0, C), 0.5)
-
-        def mf(b):
-            return lambda: tt(V("WIN", 1008 * b + 368, 1008 * b + 688), IND(V("DH", C * b, C * b + C), O(OMF, 20, "of2")), V("DG", C * b, C * b + C), A.add)
-
-        l1 = [lambda: conv(F, C, "TF", 32),
-              lambda: tt(V("lg", 176, 208), IND(V("TF", 0, 672), O(PKL, 2)), V("cf", KW, KW + 32), A.add),
-              lambda: cp(O(OMF, 20, "of2"), V("lg", 176, 196))]
-        l2 = [lambda: conv(F, C, "TE", 31),
-              lambda: ts(V("lg", 208, 240), IND(V("TE", 0, 672), O(PKL, 2)), -321.0, A.mult, 320.0, A.add),
-              lambda: tt(V("lg", 208, 228), V("lg", 208, 228), V("cf", KW, KW + 20), A.add),
-              lambda: cp(O(OMB, 20, "of2"), V("lg", 208, 228))]
-
-        def runs():
-            scan(V("RA", 1, 640, 2), V(F, 31, 351), V("AR", 0, C), 0.0, A.mult, A.add)
-            scan(V("RA", 638, "end", -2), V(F, 351, 31, -1), V("AL", 0, C), 0.0, A.mult, A.add)
-
-        if t == 0:
-            fv = [[c1], [], [c3], [c4, dmm], [c5], [c6], [c6b], [c7]]
-            fs = [[c2], [], [c2b], [], [dh(0)], [dh(1)], [dh(2)], [dh(3)]]
-        else:
-            dmm()
-            fv = [[l1[0], l2[0], l1[1]], [], [l1[2]], [l2[1], mf(0)], [l2[2], mf(1)], [l2[3], runs], [], [mf(2)]]
-            fs = [[dh(b // 2, ("DH", "DG")[b % 2])] for b in range(8)]
-        neg = V("TAB", 17 * 32)
-        cnt = V("lg", 240)
-        cw = lambda i: V("cw", i)
-        for it in range(1, 9):
-            act(V("JK", 640 * (it % 2), 640 * (it % 2) + 640), V("D" if it == 8 else "S", 0, 640), AF.Sign, bias=neg, accum_out=cnt)
-            for f in fs[it - 1]:
-                f()
-            init = cw(16 + it)
-            if it == 2:
-                ts(BB, HB, neg, A.min)
-                scan(V("sm", N2 + 1, N2 + 33), VT1, NL32, 2.0 ** 70, A.min, A.max)
-                tr(V("sm", N2, N2 + 32), BB)
-                ts(V("sm", WA, WA + 33), V("sm", N2, N2 + 33), V("cf", 92), A.mult)
-                ts(V("sm", WB, WB + 33), V("sm", N2, N2 + 33), V("cf", 93), A.mult)
-                ts(V("sm", N3, N3 + 33), V("sm", N2, N2 + 33), V("cf", 94), A.add)
-                tt(V("sm", WA, WA + 33), V("sm", WA, WA + 33), V("sm", WB, WB + 33), A.min)
-                tt(V("sm", N3, N3 + 33), V("sm", N3, N3 + 33), V("sm", WA, WA + 33), A.min)
-            if it == 3:
-                lo = V("sm", 287)
-                ts(cw(14), lo, -1.0, A.mult, 2.0 ** -69, A.max)
-                ts(cw(14), lo, 0.5, A.mult, cw(14), A.max)
-                ts(V("cw", 0, 14), V("cf", CST, CST + 14), cw(14), A.mult)
-                ts(init, cw(14), V("cf", CST + 6), A.mult, neg, A.add)
-            if 4 <= it <= 6:
-                ts(init, neg, cw(3 + it), A.add)
-            if it == 7:
-                init = cw(11)
-                ts(V("D", 0, 640), V("S", 0, 640), neg, A.add, cw(10), A.add)
-            if it == 8:
-                ts(init, neg, cw(12), A.add)
-                ts(cw(26), neg, -1.0, A.mult, cw(13), A.add)
-            for f in fv[it - 1]:
-                f()
-            out = V("so", 32 * (it % 2), 32 * (it % 2) + 32)
-            if it <= 2:
-                ts(V1, M0, cnt, A.subtract, 2.0 ** 85, A.mult)
-                tr(VT1, V1)
-                if it == 1:
-                    scan(out, VT1, NT32, V("TAB", 0), A.min, A.max)
+        for i in range(20):
+            s = V("MW", i + 6 * (i // 10))
+            for a, n in ((0, H), (H, H)) if t and i < 10 else ((0, C),):
+                o = V("TA", 1280 * (i // 4) + 4 * a + i % 4, 1280 * (i // 4) + 4 * (a + n), 4)
+                if i < NA[t]:
+                    act(o, V("M", 16 + a, 16 + a + n), AF.Sign, scale=-1.0, bias=s)
                 else:
-                    scan(out, VT1, V("sm", N3, N3 + 32), V("sm", N3 + 32), A.min, A.max)
-                    scan(BB, VT1, V("sm", N2, N2 + 32), V("sm", N2 + 32), A.min, A.max)
-            else:
-                ts(V1, M0 if it == 8 else M1, cnt, A.is_le, cw(it - 3), A.mult)
-                tr(VT, V1)
-                scan(out, VT, zb(32), init, A.add, A.add)
-            neg = V("so", 32 * (it % 2) + 31)
-        act(V("GT", 0, 640), V("D", 0, 640), AF.Sign, bias=neg)
-        if t == 0:
-            c7s()
-        else:
-            lin(V("ME", 0, 640), zb(640), 1.0, MEC)
-        scan(BB, zb(32), VT, cw(26), A.add, A.subtract)
-        ts(V("GE", 0, 640), V("D", 0, 640), V("sm", 287), A.is_gt, 2.0, A.mult)
-        scan(V("CAP", 638, "end", -1), V("ON", 0, 639), V("GT", 639, 0, -1), 0.0, A.add, A.subtract)
-        scan(V("PP", 0, 640), V("GE", 0, 640), V("CAP", 0, 640), -2.0 * K2, A.add, A.min)
-        scan(V("CAP", 0, C), V("PP", 0, 640, 2), V("PP", 1, 640, 2), -1024.0, A.max, A.add)
-        for c in range(4):
-            act(V("JK", C * c, C * c + C), V("CAP", 0, C), AF.Sign, bias=V("cf", BJ + c), accum_out=V("lg", 244 + c))
-        for c in range(2):
-            ts(V("GT", C * c, C * c + C), V("CAP", 0, C), V("cf", LEJ + c), A.max, V("cf", HI + c), A.min)
-        for c in range(2):
-            rec("v", "tensor_reduce", [V("lg", 248 + c), V("GT", C * c, C * c + C), AxisListType.X, A.add])
-        for c in range(2):
-            ts(O(OI + 4 + c, 1), V("lg", 248 + c), -0.5, A.mult, V("cf", HI + 2 + c), A.add)
-        ts(O(OI, 4), V("lg", 244, 248), -1.0, A.mult, 320.0, A.add)
-        cp(V("SV", 16, 112), IND(V("S", 0, 656), O(OI)))
-        act(V("CJ", 0, 96), IND(V("CE", 0, 656), O(OI)))
-        conv("SV", 96, "TS")
-        tt(V("ZJ", 16, 112), IND(V("RA", 0, 656), O(OI)), V("CJ", 0, 96), A.add)
-        ts(V("lg", 0, 16), pick("TS"), -1.0, A.mult)
+                    ts(o, V("M", 16 + a, 16 + a + n), s, A.is_lt, 2.0, A.mult)
+        order = (0, 1, 4, 2, 3) if t else (4, 0, 1, 3, 2)
+        for k in order:
+            for a, n in ((0, H), (H, H)) if t and k < 2 else ((0, C),):
+                quant("AQ", "AP", ("TA", 4 * (C * k + a)), C * k + a, n)
+            mm("P7", "CQ", "CP", 0, "AQ", "AP", C * k, C, k == order[0], k == order[4])
+        s0, sg, a1, a2, a3, tau = [V("sm", i) for i in range(6)]
+        ts(V("MK", 0, C), V("P7", 0, C), 2 * K2 - 0.5 - 16 * NA[t], A.is_gt, -1024.0, A.mult)
+        act(V("JK", 0, C), V("MK", 0, C), accum_out=s0)
+        lin(sg, s0, -4.0, -4096.0 * (C - K2 + 0.5))
+        tt(V("YV", 0, C), V("P7", 0, C), V("MK", 0, C), A.add)
+        red(a2, V("YV", 0, C), A.min)
+        red(a1, V("YV", 0, C), A.max)
+        lin(a3, a2, 1.0, 1024.0)
+        ts(tau, a1, sg, A.max, a3, A.min)
+        ts(V("GT", 0, C), V("P7", 0, C), tau, A.is_lt)
+        ts(V("GE", 0, C), V("P7", 0, C), tau, A.is_le)
+        scan(V("CAP", C - 2, "end", -1), zb(C - 1), V("GT", C - 1, 0, -1), float(K2), A.add, A.subtract)
+        scan(V("PP", 0, C), V("GE", 0, C), V("CAP", 0, C), 0.0, A.add, A.min)
         for c in range(6):
-            act(V("SG", 96 * c, 96 * c + 96), V("SV", 16, 112), AF.Sign, bias=V("lg", c))
+            a, n = 16 * c, min(C - K2 + 16, C - 16 * c)
+            if c < 4:
+                act(V("JK", C * c, C * c + n), V("PP", a, a + n), AF.Sign, scale=-1.0, bias=V("cf", KB + c), accum_out=V("sm", 8 + c))
+                ts(O(OI + c, 1), V("sm", 8 + c), 0.5, A.mult, a + n / 2, A.add)
+            else:
+                j = "GT" if c == 4 else "GE"
+                ts(V(j, 0, n), V("PP", a, a + n), V("cf", KB + c), A.is_lt)
+                red(V("sm", 8 + c), V(j, 0, n), A.add)
+                ts(O(OI + c, 1), V("sm", 8 + c), float(a), A.add)
+        cp(V("CV", 16, 208, 2), IND(V("SM", 0, 336), O(OI)))
+        act(V("CV", 17, 208, 2), IND(V("SC", 0, 336), O(OI)))
+        act(V("CJ", 0, 192, 2), IND(V("CEL", 0, 336), O(OI)))
+        act(V("CJ", 1, 192, 2), IND(V("CER", 0, 336), O(OI)))
         if t:
-            mf(3)()
-        conv("ZJ", 96, "TZ")
-        lin(V("SRC", 0, 96), V("ZJ", 16, 112), rm(6))
-        lin(V("LA", 0, 96), V("ZJ", 16, 112), R1N)
-        lin(V("D0", 1, 192, 2), V("ZJ", 16, 112), rm(1))
-        if t == 0:
-            lin(V("ME", 0, 640), zb(640), 1.0, MEC)
-        for c in range(0, 6, 2):
-            tt(V("FL", 96 * c, 96 * c + 192), V("SG", 96 * c, 96 * c + 192), V("NTAU", 96 * c, 96 * c + 192), A.is_ge)
-        tt(V("SRC", 0, 96), V("SRC", 0, 96), V("JR", 0, 96), A.add)
-        scan(V("RB", 0, 576), V("KP", 0, 576), V("FL", 0, 576), 0.0, A.mult, A.add)
-        cp(O(OO, 16), pick("TZ", 2))
-        tr(V("TZ1", 0, 96), V("ZJ", 17, 113))
-        cp(O(OR), V("RB", 95, 576, 96))
-        cp(IND(V("INV", 16, 112), O(OR)), V("SRC", 0, 96))
-        act(V("PIJ", 0, 96), IND(V("PIT", 0, 96), O(OR)))
-        z = lambda r: V("TZ", r, 96, 16)
-        lin(tmp(3), z(12), -1.0, 336.0)
-        tt(tmp(1), V("TZ1", 3, 96, 16), z(12), A.add)
-        tt(tmp(2), tmp(22), z(3), A.add)
-        cp(V("INS", 0, 96, 2), V("INV", 17, 112, 2))
-        act(V("INS", 1, 96, 2), V("INV", 16, 112, 2))
-        conv("INV", 96, "TP")
-        tt(V("MJ", 16, 112), IND(V("INS", 0, 96), O(OR)), V("PIJ", 0, 96), A.add)
-        lin(V("SB", 97, 192, 16), z(12), 1.0, 369.0)
-        lin(tmp(21), z(1), 1.0, 1.0)
-        if last:
-            lin(V("SB", 100, 192, 16), z(12), 1.0, 369.0)
-            lin(V("SB", 196, 288, 16), z(6), 1.0, 1.0)
-        cp(O(OP, 16), pick("TP", 6))
-        ts(tmp(1), tmp(1), 0.0, A.is_equal)
-        cp(IND(V("ME", 0, 656), O(OI)), V("MJ", 16, 112))
-        conv("MJ", 96, "TM")
-        tt(V("FJ", 16, 112), IND(V("ME", 0, 656), O(OO)), V("ZJ", 16, 112), A.add)
-        ts(O(OMM, 16), pick("TM"), 2.0, A.mult, 1.0, A.add)
+            tt(V("MT", 0, 192, 2), IND(V("RA", 16, 352), O(OI)), V("CJ", 0, 192, 2), A.add)
+            tt(V("MT", 1, 192, 2), IND(V("RB", 16, 352), O(OI)), V("CJ", 1, 192, 2), A.add)
+        else:
+            lin(V("MT", 0, 192), V("CJ", 0, 192), 1.0, V("cf", CC + 9))
+        conv("CV", 192, "TC")
+        cp(V("CW", 0, 16), pick("TC", 192))
+        tt(V("EQV", 0, 192), IND(V("CW", 0, 16), O(OREP, 12)), V("CV", 0, 192), A.is_equal)
+        for q in range(16):
+            lin(V("TB", 768 * 2 + 3 + 4 * q, 768 * 3, 64), V("EQV", q, 192, 16), V("MSK", q))
+        for c in range(11):
+            a, m = 768 * (c // 4) + c % 4, 16 * c + 32
+            ts(V("TB", a, a + 4 * m - c % 4, 4), V("CV", 0, m), V("CW", c), A.is_lt)
+            if m < 192:
+                ts(V("TB", a + 4 * m, 768 * (c // 4 + 1), 4), V("CV", m, 192), V("CW", c), A.is_le)
+        for k in range(3):
+            quant("BQ", "BP", ("TB", 768 * k), 192 * k, 192)
+            mm("P7", "CQ", "CP", 1, "BQ", "BP", 192 * k, 192, k == 0, k == 2)
+        conv("P7", 192, "TR")
+        for e in range(2):
+            tt(V("FS", e, 176, 2), V("P7", 17 - e, 192, 2), V("MT", e, 176, 2), A.add)
+        cp(O(OR, 16), pick("TR", 192))
+        cp(IND(V("FR", 0, 192), O(OR, 11)), V("FS", 0, 176))
+        cp(V("FJ", 16, 104, 2), V("FR", 1, K2, 2))
+        act(V("FJ", 17, 104, 2), V("FR", 0, K2, 2))
         conv("FJ", 96, "TJ")
-        lin(V("SB", 193, 288, 16), V("TM", 4, 96, 16), 1.0 / 1024, 320.0)
-        act(V("D1", 1, 192, 2), V("FJ", 16, 112))
-        cp(O(OF, 16), pick("TJ"))
-        ts(O(OF2, 16), pick("TJ"), 2.0, A.mult, 1.0, A.add)
-        ts(tmp(0), V("TJ", 4, 96, 16), 65536.0, A.not_equal)
-
-        def gj(b):
-            return lambda: act(V("GJ", 96 * b, 96 * b + 96), IND(V("DH", C * b, C * b + C), O(OP)))
-
-        def jm(b):
-            tt(V("WIN", 1008 * b + C, 1008 * b + 368), V("GJ", 96 * b, 96 * b + 96, 2), V("GJ", 96 * b + 1, 96 * b + 96, 2), A.add)
-
-        def s4():
-            tr(V("RS", 16, 112), V("SB", 0, 96))
-            tr(V("VC", 0, 192), V("SB", 96, 288))
-
-        post = [[lambda: tt(tmp(20), tmp(0), z(8), A.mult)],
-                [lambda: ts(tmp(0), tmp(20), 0.0, A.is_gt)],
-                [lambda: tt(tmp(1), tmp(1), tmp(0), A.max), lambda: tt(tmp(2), tmp(2), tmp(0), A.mult)],
-                [lambda: tt(tmp(3), tmp(3), tmp(1), A.mult), lambda: tt(V("SB", 96, 192, 16), tmp(23), tmp(1), A.mult),
-                 lambda: tt(V("SB", 0, 96, 16), tmp(2), z(3), A.subtract), lambda: jm(0)],
-                [lambda: tt(V("SB", 1, 96, 16), tmp(3), z(12), A.add)],
-                [s4], [lambda: conv("RS", 96, "TS"), lambda: jm(1)], []]
-        sides = [[], [] if t else [c9], [gj(0)], [], [gj(1)], [gj(2)], [gj(3)], []]
-        la, fb, n = "LA", "FJ", 0
-        for o, o2, on, on2 in ((OF, OF2, O4, O42), (O4, O42, O16, O162), (O16, O162, None, None)):
-            fa = fb
-            for k in range(3 if on else 2):
-                act(V("D1", 0, 192, 2), IND(V("XO", 0, 192), O(o2)) if n else IND(V("FJ", 16, 112), O(o)))
-                for _i in range((2, 1, 0)[k] if on else 0):
+        ts(O(O1, 16), pick("TJ", 96), float(K2), A.min)
+        cp(O(OP, 16), pick("TJ", 96, 6))
+        z = lambda r: V("TJ", r, 96, 16)
+        for b in range(4):
+            dh = V("DH", C * b, C * b + C)
+            mm("P%d" % b, "EQ", "ES", b, XQ, XS, 0, C)
+            act(dh, V("P%d" % b, 0, C))
+            if t:
+                lin(win(b, 0), dh, 2.0)
+                act(V("DG", C * b, C * b + C), IND(dh, O(OMF, 20)))
+                tt(win(b, C), V("P%d" % b, 0, C), V("DG", C * b, C * b + C), A.add)
+                act(winr(b), IND(win(b, 0, 2 * C), O(OMB, 20)))
+            else:
+                lin(win(b, C), dh, 2.0)
+                lin(winr(b), dh, 2.0)
+            act(V("GJ", 96 * b, 96 * b + 96), IND(dh, O(OP)))
+            tt(win(b, 2 * C, 48), V("GJ", 96 * b, 96 * b + 96, 2), V("GJ", 96 * b + 1, 96 * b + 96, 2), A.add)
+        if t:
+            for h in range(2):
+                act(V("NW", H * h, H * h + H - 1), V(F, fa_(h), fa_(h) + H - 1))
+                act(V("NW", 687 - H * h, 687 - H * h - H, -1), V(F, fa_(h) - 1, fa_(h) + H - 1))
+        ts(tmp(0), z(3), float(K2), A.is_lt)
+        tt(tmp(2), tmp(22), z(4), A.add)
+        lin(tmp(3), z(7), -1.0, float(C))
+        tt(tmp(0), tmp(0), z(8), A.mult)
+        tt(tmp(2), tmp(2), tmp(0), A.mult)
+        tt(tmp(3), tmp(3), tmp(0), A.mult)
+        tt(V("SB", 0, 96, 16), tmp(2), z(4), A.subtract)
+        tt(V("SB", 1, 96, 16), tmp(3), z(7), A.add)
+        lin(V("SB", 96, 192, 16), z(11))
+        for r in (1, 2) if last else (1,):
+            lin(V("SB", 192 + r, 288, 16), z(7), 1.0, 2.0)
+        tr(V("RS", 16, 112), V("SB", 0, 96))
+        tr(V("WV", 0, 192), V("SB", 96, 288))
+        conv("RS", 96, "TP")
+        cp(O(OA, 32), IND(V("TP", 0, 224), O(PKA, 2)))
+        lin(V("W2", 0, C), zb(C), 1.0, kt(8))
+        cp(IND(V("W2", 0, 432), O(OA)), V("WV", 0, 96))
+        ts(V("TN", 0, 96), IND(V("W2", 0, 432), O(OA + 16)), 0.0, A.is_le)
+        tt(V("VC", 0, 96), V("TN", 0, 96), V("VR", 0, 96), A.mult)
+        if t:
+            lin(tmp(20), tmp(0), 0.5)
+            tt(tmp(20), tmp(20), z(5), A.subtract)
+        else:
+            tt(tmp(20), z(4), tmp(23), A.add)
+        if last:
+            lin(V("DA", 98, 192, 16), z(6), 1.0, 2.0)
+        fb = "FJ"
+        if t:
+            ts(O(O1D, 16), pick("TJ", 96), float(K2), A.min, 2.0, A.mult)
+            act(V("D1", 1, 176, 2), V("FJ", 16, 104))
+            ts(V("VM", 0, 96), V("FJ", 16, 112), kt(9), A.mult)
+            ts(V("HI", 0, 96), V("FJ", 16, 112), kt(9), A.mult)
+            tt(V("D0", 1, 192, 2), V("VM", 0, 96), V("HI", 0, 96), A.subtract)
+            act(V("LA", 0, 96), V("D0", 1, 192, 2))
+        cur = V("FJ", 16, 112)
+        la = "LA"
+        for st, (o, o2, on, on2, d0, dn) in enumerate(((O1, O1D, O4, O4D, "D0", "D4"), (O4, O4D, O16, O16D, "D4", "D16"), (O16, O16D, None, None, "D16", None))):
+            steps = 3 if on else 2
+            if on:
+                fa = fb
+                for k in range(3):
                     fo = [x for x in ("FA", "FB", "FC") if x != fa and x != fb][0]
                     act(V(fo, 16, 112), IND(V(fa, 16, 112), O(o)))
                     fa = fo
+                fb = fa
+            if t:
+                for k in range(steps):
+                    act(V("D1", 0, 192, 2), IND(V("XO", 8, 200), O(o2)) if st + k else IND(cur, O(o)))
+                    scan(V("XO", 7, 183), V(d0, 0, 176), V("D1", 0, 176), 0.0, A.add, A.max)
+                    if on:
+                        lo_ = "LB" if la == "LA" else "LA"
+                        for out in [V(dn, 1, 192, 2)] * (k == 2) + [V(lo_, 0, 96)] * (k < 2 or st == 0):
+                            tt(out, IND(V(la, 0, 96), O(o)), V(d0, 1, 192, 2), A.add)
+                        la = lo_
                 if on:
-                    lo_ = "LB" if la == "LA" else "LA"
-                    tt(V(lo_, 0, 96), IND(V(la, 0, 96), O(o)), V("D0", 1, 192, 2), A.subtract)
-                    la = lo_
-                if on and k == 2:
-                    cp(O(on, 16), pick("TS"))
-                    ts(O(on2, 16), pick("TS"), 2.0, A.mult, 1.0, A.add)
-                scan(V("XO", 0, 192), V("D0", 0, 192), V("D1", 0, 192), 0.0, A.add, A.max)
-                if on and k == 2:
-                    ts(V("D0", 1, 192, 2), V(la, 0, 96), -1.0, A.mult)
-                    cp(V("D1", 1, 192, 2), V("XO", 1, 192, 2))
-                for f in sides[n] + post[n]:
-                    f()
-                if on and k == 1:
-                    conv(fa, 96, "TS")
-                n += 1
-            fb = fa
-        act(V("XX", 96, 192), IND(V("XO", 0, 192), O(OMM)))
-        cp(O(OA, 32), pick("TS", 0, 2))
-        cp(V("XX", 0, 96), V("XO", 1, 192, 2))
-        jm(2)
-        jm(3)
-        tr(V("TX", 0, 192), V("XX", 0, 192))
-        if t == 0:
-            lin(V("RM0", 0, C), zb(C), 1.0, R03)
-        for b in range(4):
-            if t:
-                act(V("WIN", 1008 * b + 688, 1008 * b + 1008), V("P%d" % b, 0, C))
+                    cp(V("D1", 1, 176, 2), V("XO", 8, 184, 2))
             else:
-                act(V("WIN", 1008 * b, 1008 * b + C), V("P%d" % b, 0, C))
-        for b in range(4):
-            if t:
-                act(V("WIN", 1008 * b, 1008 * b + C), IND(V("WIN", 1008 * b + 368, 1008 * b + 1008), O(OMB, 20, "of2")))
-            else:
-                act(V("WIN", 1008 * b + 368, 1008 * b + 688), V("P%d" % b, 0, C))
-        if t == 0:
-            c10()
-        else:
-            act(V("NW", 0, C), V(F, 31, 31 + C))
-            act(V("NW", 368, 688), V(F, 32, 32 + C))
+                for k in range(steps):
+                    lin(V("N%d" % (k + 1), 0, 96), cur, 1.0, V("cf", CC + 3 * st + k))
+                for k in range(steps):
+                    nx = V("UC" if cur == V("UA", 0, 96) else "UA", 0, 96)
+                    tt(nx, IND(cur, O(o)), V("N%d" % (k + 1), 0, 96), A.max)
+                    cur = nx
+            if on:
+                conv(fb, 96, "TS")
+                ts(O(on, 16), pick("TS", 96), float(K2), A.min)
+                if t:
+                    ts(O(on2, 16), pick("TS", 96), float(K2), A.min, 2.0, A.mult)
+        nm, a, s = ("XO", 8, 2) if t else ("QA", cur[2], 1)
+        cp(V("XX", 0, 96, 2), V(nm, a + s, a + 96 * s, 2 * s))
+        act(V("XX", 1, 96, 2), V(nm, a, a + 96 * s, 2 * s))
+        tr(V("TX", 0, 96), V(nm, a, a + 96 * s, s))
+        tr(V("TX", 96, 192), V("XX", 0, 96))
         x1 = lambda r: V("TX", r, 96, 16)
         x2 = lambda r: V("TX", 96 + r, 192, 16)
         d1, d2 = V("lw", 60, 66), V("lw", 66, 72)
-        tt(tmp(5, 12), V("TX", 4, 192, 16), V("TX", 1, 192, 16), A.subtract)
-        tt(tmp(6), x1(4), V("TM", 4, 96, 16), A.not_equal)
-        tt(V("DW", 2, 96, 16), x1(3), x2(3), A.max)
-        tt(tmp(7, 12), V("TX", 2, 192, 16), V("TX", 4, 192, 16), A.subtract)
+        tt(tmp(6), x1(3), rj, A.not_equal)
+        tt(tmp(5, 12), V("TX", 3, 192, 16), V("TX", 1, 192, 16), A.subtract)
+        tt(V("DW", 3, 96, 16), x1(4), x2(4), A.max)
+        tt(tmp(7, 12), V("TX", 2, 192, 16), V("TX", 3, 192, 16), A.subtract)
         tt(tmp(8), tmp(6), d2, A.mult)
-        tt(tmp(9), V("DW", 2, 96, 16), z(3), A.is_equal)
-        tt(tmp(12), V("lw", 90, 96), tmp(7), A.is_ge)
+        tt(tmp(9), V("DW", 3, 96, 16), z(4), A.is_equal)
+        tt(tmp(12), tmp(7), V("lw", 90, 96), A.is_ge)
         tt(tmp(10), tmp(8), d1, A.add)
-        tt(tmp(13), d1, tmp(8), A.subtract)
-        tt(tmp(17), tmp(12), tmp(6), A.mult)
-        tt(tmp(14), tmp(12), z(1), A.mult)
-        tt(tmp(18), tmp(8), z(7), A.add)
-        tt(tmp(10), tmp(10), tmp(9), A.mult)
-        tt(tmp(11), tmp(8), tmp(20), A.add)
-        tt(tmp(13), tmp(13), tmp(12), A.mult)
-        tt(tmp(17), tmp(17), z(7), A.mult)
-        tt(tmp(18), tmp(18), tmp(12), A.subtract)
-        tt(V("DW", 0, 96, 16), tmp(10), tmp(21), A.add)
-        tt(V("DW", 3, 96, 16), tmp(10), tmp(21), A.add)
-        tt(tmp(15), tmp(12), z(10), A.mult)
-        tt(tmp(16), tmp(12), z(13), A.mult)
-        tt(tmp(14), tmp(14), tmp(11), A.add)
-        tt(tmp(18), tmp(18), tmp(17), A.subtract)
+        tt(V("DW", 0, 96, 16), tmp(10), tmp(9), A.mult)
+        lin(tmp(14), tmp(6), -800.0 * U, 799.0 * U)
+        tt(tmp(14), tmp(14), d1, A.add)
+        if t:
+            tt(tmp(11), d1, tmp(20), A.add)
+            tt(tmp(13), d1, z(5), A.subtract)
+            lin(tmp(16), tmp(12), 400.0 * U)
+            tt(tmp(13), tmp(8), tmp(13), A.subtract)
+            tt(tmp(15), tmp(12), z(10), A.mult)
+            tt(tmp(13), tmp(13), tmp(12), A.mult)
+            for r in (1, 2) if last else (1,):
+                tt(V("DA", r, 96, 16), tmp(15), z(9), A.add)
+            tt(V("DA", 96, 192, 16), tmp(14), tmp(16), A.add)
+            tt(V("DA", 0, 96, 16), tmp(13), tmp(11), A.add)
+        else:
+            ts(tmp(16), d1, 1.5 * U, A.is_gt, 400.0 * U, A.mult)
+            lin(tmp(20), tmp(20), -1.0, 2.0)
+            tt(tmp(16), tmp(16), tmp(8), A.add)
+            tt(tmp(15), tmp(12), tmp(20), A.mult)
+            tt(tmp(13), tmp(16), tmp(14), A.subtract)
+            tt(V("DA", 1, 96, 16), tmp(15), tmp(23), A.add)
+            tt(tmp(13), tmp(13), tmp(12), A.mult)
+            tt(V("DA", 0, 96, 16), tmp(13), tmp(14), A.add)
+        ne = 288 if t else 192
         tr(V("RW", 16, 112), V("DW", 0, 96))
-        tt(V("DA", 1, 96, 16), tmp(15), z(9), A.add)
-        tt(V("DA", 2, 96, 16), tmp(16), z(11), A.add)
-        tt(V("DA", 0, 96, 16), tmp(14), tmp(13), A.add)
-        tt(V("DA", 3, 96, 16), tmp(18), tmp(13), A.add)
-        cp(IND(V("W", 0, 432), O(OA)), V("RW", 16, 112))
+        cp(IND(V("W1", 0, 432), O(OA)), V("RW", 16, 112))
         conv("RW", 96, "TP")
-        if last:
-            tt(V("DA", 4, 96, 16), tmp(15), z(9), A.add)
-        scan(V("CS", 1, C + 1), V("W", 0, C), V("RM0", 0, C), 0.0, A.add, A.mult)
-        ts(O(OMM, 16), pick("TP", 2), -1.0, A.mult)
-        tr(V("VA", 0, 96), V("DA", 0, 96))
-        tt(V("EV", 112, 208), IND(V("CS", 0, 352), O(OA + 16)), V("VC", 0, 96), A.add)
+        scan(V("CS", 1, C + 1), V("W1", 0, C), V("W2", 0, C), 0.0, A.add, A.add)
+        ts(O(OMM, 16), pick("TP", 96, 3), -1.0, A.mult)
+        tr(V("VA", 0, ne - 96), V("DA", 0, ne - 96))
+        tt(V("EV", 112, 208), IND(V("CS", 0, 352), O(OA + 16)), V("VC", 0, 96), A.max)
         tt(V("EV", 16, 112), IND(V("CS", 0, 352), O(OMM)), V("VA", 0, 96), A.add)
-        conv("EV", 192, "TK", 16, 208)
-        cp(O(OK_, 64), IND(V("TK", 0, 432), O(PKH, 4)))
-        cp(IND(V("EW", 0, 1168), O(OK_, 12)), V("EV", 16, 208))
-        cp(IND(V("EW", 0, 1168), O(OK_ + 48)), V("VC", 96, 192))
-        ts(V("KE", 0, C), V("EW", 0, C), 0.0, A.is_equal)
-        scan(V("FI", 16, 336), V("KE", 0, C), V("EW", 0, C), INI, A.mult, A.add)
-        conv("FI", C, "TK")
-        tt(V("lg", 64, 96), row(PKL), V("cf", KW, KW + 32), A.subtract)
-        tt(V("lg", 96, 128), row(PKL + 4), V("lg", 64, 96), A.mult)
-        tt(V("lg", 128, 160), row(PKL + 2), V("lg", 96, 128), A.subtract)
-        ts(O(OL, 20, "of2"), V("lg", 128, 148), -0.75, A.add)
+        if t:
+            tt(V("EV", 208, 304), IND(V("CS", 0, 352), O(OMM)), V("VA", 96, 192), A.add)
+        conv("EV", ne, "TK")
+        if t:
+            ts(O(OK_, 32), IND(V("TK", 0, 608), O(PKE, 2)), 1024.0, A.mult)
+        else:
+            ts(O(OK_, 16), pick("TK", 192), 1024.0, A.mult)
+        cp(IND(V("EW", 0, 1536), O(OK_, 12)), V("EV", 16, 208))
+        if t:
+            cp(IND(V("EW", 0, 1536), O(OK_ + 12)), V("EV", 208, 304))
+        ts(V("KE", 0, C), V("EW", 0, C), 1.0, A.is_equal)
+        scan(V("FI", 16, 336), V("KE", 0, C), V("EW", 0, C), 1.0, A.mult, A.add)
+        for h in (1, 0):
+            conv("FI", H, "TK", 16 + H * h, 352 * h)
+            ts(O(OL + 16 * h, 16), pick("TK", H, 1, 352 * h), -2.0, A.add)
+            if last:
+                ts(O(OPL + 16 * h, 16), pick("TK", H, 2, 352 * h), -2.0, A.add)
+        if not last:
+            gfill(V("W1", 0, C))
+            gfill(V("EW", 0, C), 1)
         YQ, YS, NS = "YQ%d" % t, "YS%d" % t, "NS%d" % t
         for hf in (1, 0):
-            o = O(OL + 10 * hf, 10, "of2")
+            o = HO(OL, hf)
             for b in range(4):
-                y, w = V("Y", 640 * hf + b, 640 * hf + 640, 4), IND(V("WIN", 1008 * b, 1008 * b + 688), o)
-                cp(y, w) if b < 2 else act(y, w)
+                y, w = V("Y", 640 * hf + b, 640 * hf + 640, 4), IND(win(b, C, 688), o)
+                ts(y, w, 0.5, A.mult) if b < 2 else lin(y, w, 0.5)
             if hf:
-                quant(V(YQ, 0, H), V(YS, 0, H), V("Y", 640, 1280))
+                quant(YQ, YS, ("Y", 640), 0, H)
                 rec("g", "remote", [U8V(V(ZQ, H, C)), U8V(V(YQ, 0, H))], nw=0, kind="r", extra=("aq%d" % t, t))
                 rec("g", "remote", [V(ZS, H, C), V(YS, 0, H)], nw=0, kind="r", extra=("aq%d" % t, t))
                 act(V(NS, 0, H), IND(V("NW", 0, 688), o))
-                rec("g", "remote", [V(Fn, 192, 352), V(NS, 0, H)], nw=0, kind="r", extra=("af%d" % t, t))
+                rec("g", "remote", [V(Fn, 224, 384), V(NS, 0, H)], nw=0, kind="r", extra=("af%d" % t, t))
             else:
-                quant(V(ZQ, 0, H), V(ZS, 0, H), V("Y", 0, 640))
-        if last:
-            tt(V("lg", 128, 160), row(PKL + 6), V("lg", 96, 128), A.subtract)
-            ts(O(OMF, 20, "of2"), V("lg", 128, 148), -0.75, A.add)
+                quant(ZQ, ZS, ("Y", 0), 0, H)
         for hf in range(2):
             a = H * hf
             if hf:
                 rec("n", "arrive", [V(ZQ, H, C), V(ZS, H, C)], nw=2, kind="a", extra=("aq%d" % t, t, 2))
-                rec("n", "arrive", [V(Fn, 192, 352)], kind="a", extra=("af%d" % t, t, 1))
+                rec("n", "arrive", [V(Fn, 224, 384)], kind="a", extra=("af%d" % t, t, 1))
             else:
-                act(V(Fn, 32, 192), IND(V("NW", 0, 688), O(OL, 10, "of2")))
+                act(V(Fn, 32, 192), IND(V("NW", 0, 688), HO(OL, 0)))
             for b in range(4):
                 mm("P%d" % (4 + b), "WQ", "WS", b, ZQ, ZS, a, H)
-                mm("P%d" % b, "EQ", "ES", b, ZQ, ZS, a, H)
-            for b in range(4):
                 act(V("RL", C * b + a, C * b + a + H), V("P%d" % (4 + b), 0, H), AF.Relu, scale=0.015625)
+            for b in range(4):
+                mm("P%d" % b, "EQ", "ES", b, ZQ, ZS, a, H)
                 tt(V(Xn, 4 * a + b, 4 * a + 640, 4), V("P%d" % b, 0, H), V("RL", C * b + a, C * b + a + H), A.add)
-                if hf == 0 and b == 0:
-                    lin(V(Fn, 191), zb(1))
+            quant(XQn, XSn, (Xn, 4 * a), a, H)
             if not last:
-                lin(V("BD", a + hf, a + H + 1), V(Fn, 31 + a + hf, 32 + a + H), -2 * BIG, BIG)
-            quant(V(XQn, a, a + H), V(XSn, a, a + H), V(Xn, 4 * a, 4 * a + 640))
-            if not last:
-                mm("P4", "UL", "ULS", 0, XQn, XSn, a, H)
-                mm("P5", "UR", "URS", 0, XQn, XSn, a, H)
-                if hf == 0 and t == 0:
-                    quant(V("VQ", 0, 128), V("VS", 0, 128), V("VB", 0, 512))
-                tt(V("S", 2 * a, 2 * a + C, 2), V("P4", 0, H), V("BD", a, a + H), A.min)
-                tt(V("S", 2 * a + 1, 2 * a + C, 2), V("P5", 0, H), V("BD", a + 1, a + H + 1), A.min)
-                if hf == 0:
-                    gfill(V("W", 0, C), 1)
-                    gfill(V("EW", 0, C))
+                f0, w = fa_(hf), 352 * hf
+                fr = V(Fn, f0 + H - 2, f0 - 1, -1)
+                kw = V("cf", KW + 10 * hf, KW + 10 * hf + 16)
+                lg = lambda i, n=16: V("lg", 128 * hf + 16 * i, 128 * hf + 16 * i + n)
+                for nm, co in (("RB", "AR"), ("RA", "AL")):
+                    scan(V(nm, a + H + 14, a + 15, -1), V(co, 0, H - 1), fr, 0.0, A.add, A.mult)
+                conv(Fn, H, "TE", f0 - 1, w)
+                conv(Fn, H, "TF", f0, w)
+                conv("RB", H, "TQ", a + 16, w)
+                ts(lg(0), pick("TE", H, 0, w), 1024.0, A.mult)
+                tt(lg(0), lg(0), kw, A.add)
+                ts(HO(OSA, hf), lg(0, 10), 640.0, A.min)
+                tt(lg(1), pick("TQ", H, 7, w), lg(0), A.add)
+                ts(HO(OSB, hf), lg(1, 10), float(C), A.add, 640.0, A.min)
+                ts(lg(2), pick("TE", H, 0, w), C - 1.0, A.mult)
+                tt(lg(2), lg(2), kw, A.add)
+                cp(O(OMB + 10 * hf, 10), lg(2, 10))
+                tt(lg(3), pick("TF", H, 0, w), kw, A.add)
+                ts(O(OMF + 10 * hf, 10), lg(3, 10), a + H - 1.0, A.min)
+                pl, pr = ("P4", "P5") if hf else ("P2", "P3")
+                mm(pl, "UL", "ULS", 0, XQn, XSn, a, H)
+                mm(pr, "UR", "URS", 0, XQn, XSn, a, H)
+                act(V("SW", a, a + H), V(pl, 0, H))
+                cp(V("SW", C + a, C + a + H), V(pr, 0, H))
+                act(V("SM", a, a + H), IND(V("SW", 0, 656), HO(OSA, hf)))
+                tt(V("M", 16 + a, 16 + a + H), IND(V("SW", 0, 656), HO(OSB, hf)), V("SM", a, a + H), A.max)
+                act(V("SC", a, a + H), IND(V("SW", 0, 656), HO(OSB, hf)))
+                conv("M", H, "TM", 16 + a, w)
+                cp(V("MW", 16 * hf, 16 * hf + 16), pick("TM", H, 0, w))
             else:
-                mm("P4", "VQ", "VS", 0, XQn, XSn, a, H)
+                py = "P4" if hf else "P3"
+                mm(py, "VQ", "VS", 0, XQn, XSn, a, H)
                 dma("y", ("raw", T.oc[:, 4 * a:4 * a + 640]), U8V(V(XQn, a, a + H)))
                 if hf:
                     for k in range(4):
                         dma("s" if k % 2 else "y", ("raw", T.osc[4 * k:4 * k + 4, :]), ("rows", slice(32 * k, 32 * k + 4), V("XS3", 0, C)))
-                    cp(V("OLT", C, 640), V("F3", 32, 352))
-                    dma("y", ("raw", T.ol[:, C:640]), ("rows", slice(0, 128, 16), V("OLT", C, 640)))
-                act(V("YO", a, a + H), V("P4", 0, H))
+                act(V("YO", a, a + H), V(py, 0, H))
                 dma("s", ("raw", T.y[:, a:a + H]), V("YO", a, a + H))
-                if hf == 0:
-                    cp(V("OLT", 0, C), IND(V("PW", 0, 688), O(OMF, 20, "of2")))
-                    dma("y", ("raw", T.ol[:, 0:C]), ("rows", slice(0, 128, 16), V("OLT", 0, C)))
+                cp(V("OLT", a, a + H), IND(V("PW", 0, 688), HO(OPL, hf)))
+                act(V("OLT", C + a, C + a + H - 1), V("F3", fa_(hf), fa_(hf) + H - 1))
+                if hf:
+                    dma("y", ("raw", T.ol[:, :]), ("rows", slice(0, 128, 16), V("OLT", 0, 640)))
     emit(g, core, rank, T, topo, ops)
+
+
+PLAN = {}
+WAIT, DMA, FAR, SLOW = 210.0, 2500.0, 3200.0, 1.15
+PASSES, MIX = 4, 1.0
+
+
+def link(ops):
+    hist = {}
+    for i, o in enumerate(ops):
+        dep, after = set(), set()
+        rd = o["rd"] if o["kind"] != "r" else touched(o["a"][1])
+        for nm, m in rd:
+            psum = SCRATCH[nm][0] == "psum"
+            dep.update(j for j, w, m2 in hist.get(nm, []) if m2 & m and (w or psum and ops[j]["e"] != o["e"]))
+        for nm, m in o["wr"]:
+            (after if o["x"] == "acc" else dep).update(j for j, w, m2 in hist.get(nm, []) if m2 & m)
+        if o["kind"] == "a":
+            after.update(j for j in range(i) if ops[j]["kind"] == "r" and ops[j]["x"][0] == o["x"][0])
+        o["dep"], o["after"] = dep, after
+        for nm, m in o["wr"]:
+            hist[nm] = [(j, w, m2 & ~m) for j, w, m2 in hist.get(nm, []) if m2 & ~m] + [(i, True, m)]
+        if o["kind"] != "r":
+            for nm, m in rd:
+                hist.setdefault(nm, []).append((i, False, m))
+
+
+def cost(o):
+    if o["kind"] != "c":
+        return {"a": 0.0, "d": 60.0, "r": 300.0}[o["kind"]]
+
+    def width(x):
+        if x[0] == "ind":
+            return 16 * width(x[2])
+        return len(range(x[2], x[3] if x[3] != "end" else -1, x[4])) if x[0] == "ap" else width(x[-1])
+
+    a = [x for x in o["a"] if isinstance(x, tuple)]
+    n = max(width(x) for x in a)
+    if a[0][0] == "ind":
+        return 50 + 2.9 * n
+    if any(x[0] == "ind" for x in a):
+        return 60 + 1.25 * width(a[0])
+    if o["m"] == "quantize_mx":
+        return 12 + 0.22 * n
+    if o["m"] == "iota":
+        return 130 + 1.66 * n
+    if o["m"] == "matmul_mx":
+        return 0.83 * (width(a[0]) + 16)
+    if o["m"] == "tensor_tensor":
+        n *= 1 + all(SCRATCH[x[1]][0] != "psum" for x in a)
+    elif o["m"] not in ("activation", "tensor_reduce") and all(SCRATCH[x[1]][2] == BF for x in a if width(x) > 1):
+        n /= 2
+    return 0.83 * max(n, 64)
+
+
+def sweep(eng, c, nxt, rank):
+    n = len(c)
+    left, ready, end, pool, order = [0] * n, [0.0] * n, [0.0] * n, {e: [] for e in eng}, []
+    for i in range(n):
+        for k, w in nxt[i]:
+            left[k] += 1
+    for i in range(n):
+        if not left[i]:
+            pool[eng[i]].append(i)
+    free = {e: 0.0 for e in pool}
+    while len(order) < n:
+        now, e = min((max(free[e], min(ready[i] for i in p)), e) for e, p in pool.items() if p)
+        p = sorted(pool[e], key=lambda i: -rank[i])
+        best = None
+        for x, i in enumerate(p):
+            if ready[i] <= now and all(now + c[i] + rank[k] <= max(ready[k] + rank[k], ready[k] + c[k] + rank[i]) for k in p[:x] if ready[k] > now):
+                best = i
+                break
+        if best is None:
+            best = min((i for i in p if ready[i] > now), key=lambda i: (ready[i], -rank[i]))
+        pool[e].remove(best)
+        order.append(best)
+        free[e] = end[best] = max(now, ready[best]) + c[best]
+        for k, w in nxt[best]:
+            ready[k] = max(ready[k], free[e] + w)
+            left[k] -= 1
+            if not left[k]:
+                pool[eng[k]].append(k)
+    return order, end
+
+
+def schedule(ops):
+    link(ops)
+    n = len(ops)
+    eng = [o["e"] for o in ops]
+    c = [SLOW * cost(o) for o in ops]
+    lag = [{"d": DMA, "r": FAR}.get(o["kind"], 0.0) for o in ops]
+    nxt, prv = [[] for o in ops], [[] for o in ops]
+    for i, o in enumerate(ops):
+        for j, w in [(j, lag[j] + WAIT) for j in o["dep"]] + [(j, lag[j]) for j in o["after"]]:
+            nxt[j].append((i, w))
+            prv[i].append((j, w))
+    rank = [0.0] * n
+    for i in range(n - 1, -1, -1):
+        rank[i] = c[i] + max([w + rank[k] for k, w in nxt[i]] + [lag[i]])
+    chain, best = rank, None
+
+    def span(order, k, far):
+        free, end = {}, [0.0] * n
+        for i in order:
+            at = max([free.get(eng[i], 0.0)] + [end[j] + w + (far - FAR) * (ops[j]["kind"] == "r") for j, w in prv[i]])
+            free[eng[i]] = end[i] = at + k * c[i]
+        return max(end) / (1 + k)
+
+    for _ in range(PASSES):
+        order, end = sweep(eng, c, nxt, rank)
+        s = span(order, 0.9, FAR / 2) + span(order, 1.0, FAR) + span(order, 1.3, 1.5 * FAR)
+        if best is None or s < best[0]:
+            best = (s, order)
+        back = sweep(eng, c, prv, end)[1]
+        rank = [MIX * back[i] + (1 - MIX) * chain[i] * max(back) / max(chain) for i in range(n)]
+    return best[1]
 
 
 def emit(g, core, rank, T, topo, ops):
@@ -715,20 +771,10 @@ def emit(g, core, rank, T, topo, ops):
         es = [topo.engines(src, T.cores[T.rank_of(src) ^ s]) for s in STEP]
         return [e for e in es[0] if all(e in x for x in es)]
 
-    hist = {}
-    for i, o in enumerate(ops):
-        dep = set()
-        rd = o["rd"] if o["kind"] != "r" else touched(o["a"][1])
-        for nm, m in rd:
-            dep.update(j for j, w, m2 in hist.get(nm, []) if w and m2 & m)
-        for nm, m in o["wr"]:
-            dep.update(j for j, w, m2 in hist.get(nm, []) if m2 & m)
-        o["dep"] = dep
-        for nm, m in o["wr"]:
-            hist[nm] = [(j, w, m2 & ~m) for j, w, m2 in hist.get(nm, []) if m2 & ~m] + [(i, True, m)]
-        if o["kind"] != "r":
-            for nm, m in rd:
-                hist.setdefault(nm, []).append((i, False, m))
+    if "order" not in PLAN:
+        PLAN["order"] = schedule(ops)
+    ops = [ops[i] for i in PLAN["order"]]
+    link(ops)
     known = {e: {} for e in qs}
     for o in ops:
         o["clock"] = {}

@@ -4,7 +4,9 @@ C, H, K2, R = 320, 160, 88, 3
 STEP = [1, 2, 4]
 BIG = 2.0 ** 90
 U = 1.0 / 1024
-NA = (13, 16, 16)
+NA = (13, 15, 15)
+NB = (3, 4, 5)
+RADIX = ((4, 4, 3), (3, 3, 3, 2))
 F32, BF, I32, U16, X4, U8 = "float32", "bfloat16", "int32", "uint16", "float8_e4m3fn_x4", "uint8"
 SCRATCH = {}
 SLOT = {}
@@ -22,12 +24,14 @@ def _slots(buf, names, n, more=0, d=F32):
 
 
 _buf("P0 P1 P2 P3 P4 P5 P6 P7", 512, F32, "psum")
-_buf("X0 X1 X2 X3 Y DH DG", 1280, BF)
+EARLY = (0,)
+_buf("X0 X1 X2 X3 Y DH DG DP", 1280, BF)
 _buf("XQ0 XQ1 XQ2 XQ3 ZQ0 ZQ1 ZQ2", C, X4)
 _buf("XS0 XS1 XS2 XS3 ZS0 ZS1 ZS2", C, U8)
-_buf("YQ0 YQ1 YQ2", H, X4)
-_buf("YS0 YS1 YS2", H, U8)
-_buf("NS0 NS1 NS2", H, BF)
+for _t in range(R):
+    _buf(("PQ%d" if _t in EARLY else "YQ%d") % _t, C, X4)
+    _buf(("PS%d" if _t in EARLY else "YS%d") % _t, C, U8)
+_buf("NS0 NS1 NS2", 336, BF)
 _buf("F1 F2 F3", 416, BF)
 _buf("UB VB", 512, BF)
 _buf("UQ VQ UL UR", 128, X4)
@@ -59,31 +63,37 @@ _buf("MK GT GE CAP PP ZB", C, BF)
 _buf("JK", 1280, BF)
 _buf("YV KZ KT", C, F32)
 _buf("RL", 1280, F32)
-_buf("WIN", 4 * 1008, BF)
+_buf("WIN0 WIN1", 4 * 1008, BF)
+_buf("L0 L1 L2", 72, U16)
 _buf("NW", 688, BF)
 _buf("PW", 688, F32)
 _buf("W1 W2", 432, F32)
 _buf("TK", 704, F32)
-_buf("EW", 1536, F32)
-_buf("TF TE TQ", 704, BF)
+_buf("EW", 4096, F32)
+_buf("TE TQ", 704, BF)
+_buf("SG", 768, BF)
+_buf("SH", 576, BF)
+_buf("AB", C, BF)
 _buf("OLT", 640, F32)
 _buf("YO", C, F32)
 _buf("ci HI", 96, I32)
 _buf("cf", 96, F32)
 _buf("sm", 32, F32)
 _buf("lg", 256, F32)
-_buf("off", 448, U16)
+_buf("off", 592, U16)
 _buf("lw SB", 288, F32)
-_buf("GJ", 384, F32)
-_slots("PB", "FJ FA FB FC RW RS", 112, 16)
-_slots("QA", "LA LB DW VM WV VR VC TN XX UA UC N1 N2 N3", 96)
-_slots("QB", "TS TJ TP TX D0 D4 D16 D1 XO CJ MT FS FR DA VA", 224)
+_buf("GJ", 768, F32)
+_slots("PB", "RW RS", 112, 16)
+_slots("PC", "FJ FA FB FC", 224, 40)
+_slots("PD", "LA LB LC D00 D01 D02 D03 D1 XO", 232)
+_slots("QA", "DW VM WV VR VC TN XX N1 N2 N3", 96)
+_slots("QB", "TS TJ TP TX CJ MT FS FR DA VA", 224)
 _slots("QC", "CEL CER KE CS FI EV", 352)
 _slots("QE", "RA RB AL AR", 352, 0, BF)
 
 ENG = ["v", "s", "t", "g"]
 SEMAPHORES = ["e" + e for e in ENG] + ["d%d" % i for i in range(20)] + \
-             ["aq%d" % t for t in range(R)] + ["af%d" % t for t in range(R)] + ["sent"]
+             [s + str(t) for t in range(R) for s in ("aq", "af", "ax", "ap")] + ["sent"]
 
 
 def V(n, a, b=None, s=1):
@@ -126,7 +136,7 @@ def touched(x):
 ROWS = {1: (0, -U, -U, 0, -U, -U), 2: (U, U, U / 2, U, 0, 0), 4: (-1, 0, 0, -1, 0, 0),
         5: (0, U, U, 0, U, U), 6: (1, 0, 0, 1, 1, 0), 7: (1, 1, 1, 1, 1, 1), 8: (0, 0, 0, 0, 0, 1),
         9: (-1, -1, 689, 1, 0, 2), 10: (2, 1, -687, -2, -1, 687), 11: (0, -U, 0, 0, -U, 0)}
-SINK = {0: (K2, 0), 1: (-1000 - 331 * U, U), 2: (-1000, 0), 3: (-1000, 0), 4: (-330, 0), 8: (1, 0), 9: (2, 0)}
+SINK = {0: (K2, 0), 1: (-1000 - 378 * U, U), 2: (-1000, 0), 3: (-1000, 0), 4: (-330, 0), 8: (1, 0), 9: (2, 0)}
 
 
 def rank_program(g, core, T, topo):
@@ -205,12 +215,20 @@ def rank_program(g, core, T, topo):
     for n, r in ((160, 0), (192, 0), (96, 0), (96, 6), (96, 3), (160, 7), (160, 1), (160, 2)):
         PKS[n, r] = 2 * len(PKS)
     PKA, PKE, OU, OREP = 16, 18, 20, 36
-    OI, OR, O1, O4, O4D, O16, O16D, O1D, OP, OA, OMM, OK_, OL, OPL, OMF, OMB, OSA, OSB = \
-        48, 64, 80, 96, 112, 128, 144, 160, 176, 192, 224, 240, 272, 304, 336, 368, 400, 416
+    OI, OR, OW, OP, OA, OMM, OK_, OL, OPL, OMF, OMB, OSA, OSB = \
+        48, 64, 80, 176, 192, 224, 240, 272, 304, 336, 356, 400, 416
     HO = lambda base, h: O(base + 16 * h, 10)
 
     def pick(tbuf, n, row=0, at=0):
         return IND(V(tbuf, at, at + 2 * n + 32), O(PKS[n, row], 1))
+
+    def dv(buf, n=96):
+        return V(buf, 40, 40 + 2 * n, 2)
+
+    def conv2(src, tbuf, o):
+        tr(V(tbuf, 0, 96), dv(src))
+        tr(V(tbuf, 96, 224), V(src, 8, 264, 2))
+        ts(O(o, 16), pick(tbuf, 96), float(K2), A.min, 2.0, A.mult)
 
     QF, HF, P32, G16, PF = [V("cf", i) for i in range(5)]
     KB, KW, RJ, J2, PR, CC = 8, 16, 48, 64, 68, 80
@@ -237,9 +255,11 @@ def rank_program(g, core, T, topo):
     iota(rj, [[32, 3], [0, 2]], 0)
     iota(V("ci", 24, 36), [[1, 12]], -1)
     ms(zb(C), 0.0)
+    ops[-1]["soon"] = True
     ms(V("KZ", 0, C), 0.0)
-    for a in range(0, 2048, 256):
-        act(V("EB", a, a + 256), zb(256))
+    ops[-1]["soon"] = True
+    for a in range(0, 2048, 512):
+        gfill(V("EB", a, a + 512))
     for nm, a, n, c in (("M", 0, 16, 0.0), ("M", 336, 352, 0.0), ("SM", C, 336, -BIG),
                         ("SC", C, 336, -BIG), ("CV", 0, 16, -BIG), ("SW", 640, 656, -BIG)):
         ms(V(nm, a, n), c)
@@ -256,8 +276,8 @@ def rank_program(g, core, T, topo):
     ts(V("cf", J2 + 2, J2 + 4), V("cf", J2, J2 + 2), 16.0, A.mult)
     pn = {160: 0, 192: 1, 96: 2, 288: 3}
     for n, i in pn.items():
-        ts(V("cf", PR + 2 * i, PR + 2 * i + 2), V("ci", 18, 20), n + 16.0, A.mult)
-        tt(V("cf", PR + 2 * i, PR + 2 * i + 2), V("cf", PR + 2 * i, PR + 2 * i + 2), V("cf", J2 + 2, J2 + 4), A.add)
+        for j in range(1 + (n == 288)):
+            ts(V("cf", PR + 2 * i + j), V("ci", 18 + j), n + 16.0, A.mult, V("cf", J2 + 2 + j), A.add)
     for (n, r), o in PKS.items():
         ts(O(o, 1), V("cf", PR + 2 * pn[n]), float(r), A.add, 2 * n + 31.0, A.min)
     ts(O(PKE, 2), V("cf", PR + 6, PR + 8), 607.0, A.min)
@@ -265,53 +285,61 @@ def rank_program(g, core, T, topo):
         ts(O(PKA + r, 1), V("cf", PR + 4), float(r), A.add, 223.0, A.min)
     ts(O(OREP, 12), V("ci", 24, 36), 0.0, A.max)
     for k in range(2):
-        ts(V("CB", 512 * k, 512 * k + 512), V("CI", 512 * k, 512 * k + 512), G16, A.is_equal)
+        ts(V("CB", 512 * k, 512 * k + 512), V("CI", 512 * k, 512 * k + 512), G16, A.is_equal, 1.0 - k / 2, A.mult)
         quant("CQ", "CP", ("CB", 512 * k), 128 * k, 128)
     ts(V("ID", 0, 128), V("IO", 0, 128), PF, A.is_equal)
     for b in range(4):
         cp(V("EB", 513 * b, 512 * (b + 1), 4), V("ID", 0, 128))
-    quant("EQ", "ES", ("EB", 0), 0, 512)
+        quant("EQ", "ES", ("EB", 512 * b), 128 * b, 128)
     ts(V("cf", KW, KW + 32), V("cf", KW, KW + 32), QF, A.add)
     ts(V("cf", KB, KB + 6), V("cf", KW, KW + 6), 0.5, A.add)
-    ts(V("MSK", 0, 16), V("IO", 0, 16), QF, A.is_gt)
+    ts(V("MSK", 0, 16), V("IO", 0, 16), QF, A.is_gt, 2.0, A.mult)
     table = {}
     for q, co in ROWS.items():
         for k, c in enumerate(co):
-            table[q, k] = c
+            table[q, 2 * (k % 3) + k // 3] = c
+    for q in range(4):
+        for k in (4, 5):
+            table[q, k] = table.get((q, k), 0) + 8 * len(NB)
     for q, co in SINK.items():
         table[q, 6], table[q, 7] = co
     table[0, 8], table[1, 9] = U, 1
     for (q, k), c in table.items():
-        if c:
-            iota(V("KZ", 32 * k + q, 32 * k + 32, 16), [[0, 2]], int(c * 2048))
+        twin = table.get((q, k ^ 1)) == c
+        if c and not (twin and k % 2):
+            lin(V("KZ", 32 * k + q, 32 * k + 32 + 32 * twin, 16), zb(2 + 2 * twin), 1.0, float(c))
+            ops[-1]["soon"] = True
     tr(V("KT", 0, C), V("KZ", 0, C))
-    ts(V("KT", 0, C, 32), V("KT", 0, C, 32), 1.0 / 2048, A.mult)
     ts(rj, rj, P32, A.add)
     ts(V("ci", 40, 46), rj, 0.5, A.mult, -0.25, A.add)
-    ts(V("XO", 184, 200, 2), V("IO", 0, 8), kt(7), A.mult, kt(6), A.add)
+    for o in (V("FJ", 216, 232, 2), V("XO", 216, 232, 2)):
+        ts(o, V("IO", 0, 8), kt(7), A.mult, kt(6), A.add)
     for i, (a, b, s) in enumerate(((1, 4, 1), (4, 13, 4), (16, 49, 16))):
         ts(V("cf", CC + 3 * i, CC + 3 * i + 3), V("IO", a, b, s), kt(9), A.mult, U, A.mult)
     ts(V("cf", CC + 9), kt(9), -47 * U, A.mult)
-    ts(V("FJ", 104, 112), V("XO", 184, 200, 2), V("cf", CC + 9), A.add)
     ts(tmp(22), rj, 336.0, A.add)
     ts(tmp(23), V("ci", 40, 46), 322.0, A.add)
-    lin(V("CEL", 0, 336), V("IO", 0, 336), kt(0), kt(2))
-    lin(V("CER", 0, 336), V("IO", 0, 336), kt(3), kt(5))
-    lin(V("AL", 0, H), zb(H), 1.0, kt(1))
-    lin(V("AR", 0, H), zb(H), 1.0, kt(4))
-    act(V("PW", 0, C), V("IO", 0, C))
-    lin(V("PW", 368, 688), V("IO", 0, C), -1.0, C - 1.0)
-    for nm, a, n, c in (("CAP", C - 1, C, K2), ("CV", 208, 224, 0), ("FJ", 0, 16, 0), ("PB", 112, 688, 0), ("D0", 0, 192, -(2 ** 23)),
-                        ("D4", 0, 192, -(2 ** 23)), ("D16", 0, 192, -(2 ** 23)),
-                        ("SB", 0, 288, 0), ("DW", 0, 96, 0), ("DA", 0, 192, 0), ("W1", 0, 432, 0), ("W2", C, 432, 0),
-                        ("CS", 0, 352, 0), ("EV", 0, 352, 0), ("EW", 0, C, 1), ("FI", 0, 16, 0), ("FI", 336, 352, 0), ("NW", 0, C, 0),
-                        ("NW", C, 368, 1), ("NW", 368, 688, 0), ("RA", 0, 352, 0), ("RB", 0, 352, 0), ("SW", 0, 640, 0), ("PW", C, 368, 0)):
+    lin(V("CEL", 0, 336), V("IO", 0, 336), kt(0), kt(4))
+    lin(V("CER", 0, 336), V("IO", 0, 336), kt(1), kt(5))
+    lin(V("AL", 0, H), zb(H), 1.0, kt(2))
+    lin(V("AR", 0, H), zb(H), 1.0, kt(3))
+    iota(V("PW", 0, 368), [[1, 368]], 0)
+    iota(V("PW", 368, 688), [[-1, C]], C - 1)
+    for nm, a, n, c in (("CAP", C - 1, C, K2), ("CV", 208, 224, 0), ("PB", 0, 16, 0), ("PB", 112, 128, 0), ("PB", 224, 240, 0),
+                        ("SB", 0, 288, 0), ("DW", 0, 96, 0), ("DA", 0, 192, 0), ("W1", 0, C, 0), ("W2", C, 432, 0),
+                        ("CS", 0, 1, 0), ("CS", C + 1, 352, 0), ("EV", 0, 16, 0), ("EV", 208, 352, 0), ("EW", 0, C, 1),
+                        ("FI", 0, 16, 0), ("FI", 336, 352, 0), ("NW", 0, C, 0),
+                        ("NW", C, 368, 1), ("RA", 0, 352, 0), ("RB", 0, 352, 0), ("SW", 0, 640, 0)):
         gfill(V(nm, a, n), c)
     gfill(V("OLT", C + H - 1, 640, H))
+    for a in range(8, 936, 224):
+        gfill(V("PC", a, a + 32, 2))
+    for st in range(4):
+        gfill(V("D0%d" % st, 39, 215, 2), -(2 ** 23))
     for nm in ("F1", "F2"):
         for a in (0, 192, 384):
             gfill(V(nm, a, a + 32))
-    ts(V("SB", 192, 288, 16), rj, 1200.0, A.add, U, A.mult)
+    ts(V("SB", 192, 288, 16), rj, 4000.0, A.add, U, A.mult)
     cp(V("DA", 97, 192, 16), tmp(23))
 
     quant("UQ", "US", ("UB", 0), 0, 128)
@@ -330,24 +358,36 @@ def rank_program(g, core, T, topo):
         cp(V("MW", 16 * h, 16 * h + 16), pick("TM", H, 0, 352 * h))
     quant("VQ", "VS", ("VB", 0), 0, 128)
 
-    win = lambda b, a, n=C: V("WIN", 1008 * b + a, 1008 * b + a + n)
-    winr = lambda b: V("WIN", 1008 * b + 1007, 1008 * b + 687, -1)
+    win = lambda h, b, a, n=C: V("WIN%d" % h, 1008 * b + a, 1008 * b + a + n)
 
     for t in range(R):
         XQ, XS, F, ZQ, ZS = "XQ%d" % t, "XS%d" % t, "F%d" % t, "ZQ%d" % t, "ZS%d" % t
         Fn, Xn, XQn, XSn = "F%d" % (t + 1), "X%d" % (t + 1), "XQ%d" % (t + 1), "XS%d" % (t + 1)
         last = t == R - 1
+        OP, OL = 448 + 48 * t, 464 + 48 * t
+
+        def send(dst, src, sem):
+            rec("g", "remote", [dst, src], nw=0, kind="r", extra=(sem + str(t), t))
+
+        def arrive(dst, sem):
+            rec("n", "arrive", dst, nw=len(dst), kind="a", extra=(sem + str(t), t, len(dst)))
+
+        if t in EARLY:
+            send(U8V(V("PQ%d" % t, 0, C)), U8V(V(XQ, 0, C)), "ax")
+            send(V("PS%d" % t, 0, C), V(XS, 0, C), "ax")
+            if t:
+                send(V("L%d" % t, 0, 40), O(OMF, 40), "ax")
+        order = (0, 1, 4, 2, 3) if t else (4, 0, 1, 3, 2)
         for i in range(20):
             s = V("MW", i + 6 * (i // 10))
-            for a, n in ((0, H), (H, H)) if t and i < 10 else ((0, C),):
+            for a, n in ((0, H), (H, H)) if t and i < 10 or i // 4 == order[4] else ((0, C),):
                 o = V("TA", 1280 * (i // 4) + 4 * a + i % 4, 1280 * (i // 4) + 4 * (a + n), 4)
                 if i < NA[t]:
                     act(o, V("M", 16 + a, 16 + a + n), AF.Sign, scale=-1.0, bias=s)
                 else:
                     ts(o, V("M", 16 + a, 16 + a + n), s, A.is_lt, 2.0, A.mult)
-        order = (0, 1, 4, 2, 3) if t else (4, 0, 1, 3, 2)
         for k in order:
-            for a, n in ((0, H), (H, H)) if t and k < 2 else ((0, C),):
+            for a, n in ((0, H), (H, H)) if t and k < 2 or k == order[4] else ((0, C),):
                 quant("AQ", "AP", ("TA", 4 * (C * k + a)), C * k + a, n)
             mm("P7", "CQ", "CP", 0, "AQ", "AP", C * k, C, k == order[0], k == order[4])
         s0, sg, a1, a2, a3, tau = [V("sm", i) for i in range(6)]
@@ -359,20 +399,21 @@ def rank_program(g, core, T, topo):
         red(a1, V("YV", 0, C), A.max)
         lin(a3, a2, 1.0, 1024.0)
         ts(tau, a1, sg, A.max, a3, A.min)
-        ts(V("GT", 0, C), V("P7", 0, C), tau, A.is_lt)
-        ts(V("GE", 0, C), V("P7", 0, C), tau, A.is_le)
+        act(V("AB", 0, C), V("P7", 0, C))
+        ts(V("GT", 0, C), V("AB", 0, C), tau, A.is_lt)
+        ts(V("GE", 0, C), V("AB", 0, C), tau, A.is_le)
         scan(V("CAP", C - 2, "end", -1), zb(C - 1), V("GT", C - 1, 0, -1), float(K2), A.add, A.subtract)
         scan(V("PP", 0, C), V("GE", 0, C), V("CAP", 0, C), 0.0, A.add, A.min)
         for c in range(6):
             a, n = 16 * c, min(C - K2 + 16, C - 16 * c)
-            if c < 4:
+            if c < 3:
                 act(V("JK", C * c, C * c + n), V("PP", a, a + n), AF.Sign, scale=-1.0, bias=V("cf", KB + c), accum_out=V("sm", 8 + c))
                 ts(O(OI + c, 1), V("sm", 8 + c), 0.5, A.mult, a + n / 2, A.add)
             else:
-                j = "GT" if c == 4 else "GE"
-                ts(V(j, 0, n), V("PP", a, a + n), V("cf", KB + c), A.is_lt)
-                red(V("sm", 8 + c), V(j, 0, n), A.add)
-                ts(O(OI + c, 1), V("sm", 8 + c), float(a), A.add)
+                j, k = V(("GT", "GE", "MK")[c - 3], 0, n), 256 * (c - 3)
+                ts(j, V("PP", a, a + n), V("cf", KB + c), A.is_lt)
+                scan(V("SG", k, k + n), j, zb(n), 0.0, A.add, A.add)
+                ts(O(OI + c, 1), V("SG", k + n - 1), float(a), A.add)
         cp(V("CV", 16, 208, 2), IND(V("SM", 0, 336), O(OI)))
         act(V("CV", 17, 208, 2), IND(V("SC", 0, 336), O(OI)))
         act(V("CJ", 0, 192, 2), IND(V("CEL", 0, 336), O(OI)))
@@ -389,37 +430,58 @@ def rank_program(g, core, T, topo):
             lin(V("TB", 768 * 2 + 3 + 4 * q, 768 * 3, 64), V("EQV", q, 192, 16), V("MSK", q))
         for c in range(11):
             a, m = 768 * (c // 4) + c % 4, 16 * c + 32
-            ts(V("TB", a, a + 4 * m - c % 4, 4), V("CV", 0, m), V("CW", c), A.is_lt)
+            lo, hi = V("TB", a, a + 4 * m - c % 4, 4), V("TB", a + 4 * m, 768 * (c // 4 + 1), 4)
+            if c in NB:
+                s = 192 * NB.index(c)
+                act(V("SH", s, s + 192), V("CV", 0, 192), AF.Sign, scale=-1.0, bias=V("CW", c))
+                act(lo, V("SH", s, s + m), AF.Sign, bias=-0.5)
+                act(hi, V("SH", s + m, s + 192), AF.Sign, bias=0.5)
+                continue
+            ts(lo, V("CV", 0, m), V("CW", c), A.is_lt, 2.0, A.mult)
             if m < 192:
-                ts(V("TB", a + 4 * m, 768 * (c // 4 + 1), 4), V("CV", m, 192), V("CW", c), A.is_le)
+                ts(hi, V("CV", m, 192), V("CW", c), A.is_le, 2.0, A.mult)
         for k in range(3):
             quant("BQ", "BP", ("TB", 768 * k), 192 * k, 192)
             mm("P7", "CQ", "CP", 1, "BQ", "BP", 192 * k, 192, k == 0, k == 2)
         conv("P7", 192, "TR")
         for e in range(2):
             tt(V("FS", e, 176, 2), V("P7", 17 - e, 192, 2), V("MT", e, 176, 2), A.add)
-        cp(O(OR, 16), pick("TR", 192))
+        ts(O(OR, 16), pick("TR", 192), 8.0 * len(NB), A.add)
         cp(IND(V("FR", 0, 192), O(OR, 11)), V("FS", 0, 176))
-        cp(V("FJ", 16, 104, 2), V("FR", 1, K2, 2))
-        act(V("FJ", 17, 104, 2), V("FR", 0, K2, 2))
-        conv("FJ", 96, "TJ")
-        ts(O(O1, 16), pick("TJ", 96), float(K2), A.min)
+        cp(V("FJ", 40, 216, 4), V("FR", 1, K2, 2))
+        act(V("FJ", 42, 216, 4), V("FR", 0, K2, 2))
+        conv2("FJ", "TJ", OW)
         cp(O(OP, 16), pick("TJ", 96, 6))
         z = lambda r: V("TJ", r, 96, 16)
-        for b in range(4):
-            dh = V("DH", C * b, C * b + C)
-            mm("P%d" % b, "EQ", "ES", b, XQ, XS, 0, C)
-            act(dh, V("P%d" % b, 0, C))
-            if t:
-                lin(win(b, 0), dh, 2.0)
-                act(V("DG", C * b, C * b + C), IND(dh, O(OMF, 20)))
-                tt(win(b, C), V("P%d" % b, 0, C), V("DG", C * b, C * b + C), A.add)
-                act(winr(b), IND(win(b, 0, 2 * C), O(OMB, 20)))
-            else:
-                lin(win(b, C), dh, 2.0)
-                lin(winr(b), dh, 2.0)
-            act(V("GJ", 96 * b, 96 * b + 96), IND(dh, O(OP)))
-            tt(win(b, 2 * C, 48), V("GJ", 96 * b, 96 * b + 96, 2), V("GJ", 96 * b + 1, 96 * b + 96, 2), A.add)
+        far = t in EARLY
+        LA_, PQ, PS = "L%d" % t, "PQ%d" % t, "PS%d" % t
+        if far:
+            send(V(LA_, 64, 70), O(OP), "ap")
+            arrive([U8V(V(PQ, 0, C)), V(PS, 0, C)] + [V(LA_, 0, 40)] * (t > 0), "ax")
+            arrive([V(LA_, 64, 70)], "ap")
+        for h in range(1 + far):
+            omf, omb, op = (V(LA_, 0, 20), V(LA_, 20, 40), V(LA_, 64, 70)) if h else (O(OMF, 20), O(OMB, 20), O(OP))
+            for b in range(4):
+                dh, dg, p = V("DH", C * b, C * b + C), V("DG", C * b, C * b + C), V("P%d" % ((b + 4 * h) % 7), 0, C)
+                gj = 384 * h + 96 * b
+                mm(p[1], "EQ", "ES", b, PQ if h else XQ, PS if h else XS, 0, C)
+                if t:
+                    if h:
+                        dh = V("DP", C * b, C * b + C)
+                    act(dh, p)
+                    lin(win(h, b, 0), dh, 2.0)
+                    part = lambda o, k: (o[0], o[1], o[2] + 20 // SPLIT * k, o[2] + 20 // SPLIT * (k + 1), 1)
+                    n = C // SPLIT
+                    for k in range(SPLIT):
+                        act(V("DG", C * b + n * k, C * b + n * k + n), IND(dh, part(omf, k)))
+                    tt(win(h, b, C), p, dg, A.add)
+                    for k in range(SPLIT):
+                        act(V("WIN%d" % h, 1008 * b + 1007 - n * k, 1008 * b + 1007 - n * k - n, -1), IND(win(h, b, 0, 2 * C), part(omb, k)))
+                    act(V("GJ", gj, gj + 96), IND(dh, op))
+                else:
+                    lin(win(h, b, C), p, 2.0)
+                    lin(V("GJ", gj, gj + 96), IND(win(h, b, C), op), 0.5)
+                tt(win(h, b, 2 * C, 48), V("GJ", gj, gj + 96, 2), V("GJ", gj + 1, gj + 96, 2), A.add)
         if t:
             for h in range(2):
                 act(V("NW", H * h, H * h + H - 1), V(F, fa_(h), fa_(h) + H - 1))
@@ -444,58 +506,55 @@ def rank_program(g, core, T, topo):
         ts(V("TN", 0, 96), IND(V("W2", 0, 432), O(OA + 16)), 0.0, A.is_le)
         tt(V("VC", 0, 96), V("TN", 0, 96), V("VR", 0, 96), A.mult)
         if t:
-            lin(tmp(20), tmp(0), 0.5)
+            lin(tmp(20), tmp(0), 1600.0 * U)
             tt(tmp(20), tmp(20), z(5), A.subtract)
+            ts(tmp(21), z(5), U, A.is_equal, 2000.0 * U, A.mult)
         else:
             tt(tmp(20), z(4), tmp(23), A.add)
         if last:
             lin(V("DA", 98, 192, 16), z(6), 1.0, 2.0)
-        fb = "FJ"
+        fb = cur = "FJ"
         if t:
-            ts(O(O1D, 16), pick("TJ", 96), float(K2), A.min, 2.0, A.mult)
-            act(V("D1", 1, 176, 2), V("FJ", 16, 104))
-            ts(V("VM", 0, 96), V("FJ", 16, 112), kt(9), A.mult)
-            ts(V("HI", 0, 96), V("FJ", 16, 112), kt(9), A.mult)
-            tt(V("D0", 1, 192, 2), V("VM", 0, 96), V("HI", 0, 96), A.subtract)
-            act(V("LA", 0, 96), V("D0", 1, 192, 2))
-        cur = V("FJ", 16, 112)
-        la = "LA"
-        for st, (o, o2, on, on2, d0, dn) in enumerate(((O1, O1D, O4, O4D, "D0", "D4"), (O4, O4D, O16, O16D, "D4", "D16"), (O16, O16D, None, None, "D16", None))):
-            steps = 3 if on else 2
-            if on:
+            act(dv("D1", K2), dv("FJ", K2))
+            lin(V("VM", 0, 96), dv("FJ"), kt(9))
+            ts(V("HI", 0, 96), dv("FJ"), kt(9), A.mult)
+            tt(dv("D00"), V("VM", 0, 96), V("HI", 0, 96), A.subtract)
+        radix = RADIX[min(t, 1)]
+        for st, rx in enumerate(radix):
+            o, more = O(OW + 16 * st), st + 1 < len(radix)
+            if more:
                 fa = fb
-                for k in range(3):
+                for k in range(rx - 1):
                     fo = [x for x in ("FA", "FB", "FC") if x != fa and x != fb][0]
-                    act(V(fo, 16, 112), IND(V(fa, 16, 112), O(o)))
+                    (cp if t and k < PV else act)(dv(fo), IND(V(fa, 40, 232), o))
                     fa = fo
                 fb = fa
             if t:
-                for k in range(steps):
-                    act(V("D1", 0, 192, 2), IND(V("XO", 8, 200), O(o2)) if st + k else IND(cur, O(o)))
-                    scan(V("XO", 7, 183), V(d0, 0, 176), V("D1", 0, 176), 0.0, A.add, A.max)
-                    if on:
-                        lo_ = "LB" if la == "LA" else "LA"
-                        for out in [V(dn, 1, 192, 2)] * (k == 2) + [V(lo_, 0, 96)] * (k < 2 or st == 0):
-                            tt(out, IND(V(la, 0, 96), O(o)), V(d0, 1, 192, 2), A.add)
-                        la = lo_
-                if on:
-                    cp(V("D1", 1, 176, 2), V("XO", 8, 184, 2))
+                d0, la = "D0%d" % st, "LC"
+                if more:
+                    act(dv(la), dv(d0))
+                for k in range(rx - 1):
+                    act(V("D1", 39, 231, 2), IND(V(cur, 40, 232), o))
+                    scan(V("XO", 39, 215), V(d0, 39, 215), V("D1", 39, 215), 0.0, A.add, A.max)
+                    cur = "XO"
+                    if more:
+                        nx = "D0%d" % (st + 1) if k == rx - 2 else "LB" if la == "LA" else "LA"
+                        tt(dv(nx), IND(V(la, 40, 232), o), dv(d0), A.add)
+                        la = nx
+                if more:
+                    cp(dv("D1", K2), dv("XO", K2))
             else:
-                for k in range(steps):
-                    lin(V("N%d" % (k + 1), 0, 96), cur, 1.0, V("cf", CC + 3 * st + k))
-                for k in range(steps):
-                    nx = V("UC" if cur == V("UA", 0, 96) else "UA", 0, 96)
-                    tt(nx, IND(cur, O(o)), V("N%d" % (k + 1), 0, 96), A.max)
+                for k in range(rx - 1):
+                    lin(V("N%d" % (k + 1), 0, 96), dv(cur), 1.0, V("cf", CC + 3 * st + k))
+                for k in range(rx - 1):
+                    nx = "LB" if cur == "LA" else "LA"
+                    tt(dv(nx), IND(V(cur, 40, 232), o), V("N%d" % (k + 1), 0, 96), A.max)
                     cur = nx
-            if on:
-                conv(fb, 96, "TS")
-                ts(O(on, 16), pick("TS", 96), float(K2), A.min)
-                if t:
-                    ts(O(on2, 16), pick("TS", 96), float(K2), A.min, 2.0, A.mult)
-        nm, a, s = ("XO", 8, 2) if t else ("QA", cur[2], 1)
-        cp(V("XX", 0, 96, 2), V(nm, a + s, a + 96 * s, 2 * s))
-        act(V("XX", 1, 96, 2), V(nm, a, a + 96 * s, 2 * s))
-        tr(V("TX", 0, 96), V(nm, a, a + 96 * s, s))
+            if more:
+                conv2(fb, "TS", OW + 16 * st + 16)
+        cp(V("XX", 0, 96, 2), V(cur, 42, 232, 4))
+        act(V("XX", 1, 96, 2), V(cur, 40, 232, 4))
+        tr(V("TX", 0, 96), dv(cur))
         tr(V("TX", 96, 192), V("XX", 0, 96))
         x1 = lambda r: V("TX", r, 96, 16)
         x2 = lambda r: V("TX", 96 + r, 192, 16)
@@ -512,8 +571,14 @@ def rank_program(g, core, T, topo):
         lin(tmp(14), tmp(6), -800.0 * U, 799.0 * U)
         tt(tmp(14), tmp(14), d1, A.add)
         if t:
-            tt(tmp(11), d1, tmp(20), A.add)
+            tt(tmp(17), d1, z(5), A.is_gt)
+            tt(tmp(18), tmp(6), tmp(21), A.mult)
+            tt(tmp(17), tmp(17), tmp(6), A.subtract)
+            tt(tmp(18), tmp(18), tmp(20), A.add)
+            tt(tmp(17), tmp(17), tmp(21), A.mult)
+            tt(tmp(11), d1, tmp(18), A.add)
             tt(tmp(13), d1, z(5), A.subtract)
+            tt(tmp(13), tmp(13), tmp(17), A.subtract)
             lin(tmp(16), tmp(12), 400.0 * U)
             tt(tmp(13), tmp(8), tmp(13), A.subtract)
             tt(tmp(15), tmp(12), z(10), A.mult)
@@ -547,9 +612,7 @@ def rank_program(g, core, T, topo):
             ts(O(OK_, 32), IND(V("TK", 0, 608), O(PKE, 2)), 1024.0, A.mult)
         else:
             ts(O(OK_, 16), pick("TK", 192), 1024.0, A.mult)
-        cp(IND(V("EW", 0, 1536), O(OK_, 12)), V("EV", 16, 208))
-        if t:
-            cp(IND(V("EW", 0, 1536), O(OK_ + 12)), V("EV", 208, 304))
+        cp(IND(V("EW", 0, 4096), O(OK_, ne // 16)), V("EV", 16, 16 + ne))
         ts(V("KE", 0, C), V("EW", 0, C), 1.0, A.is_equal)
         scan(V("FI", 16, 336), V("KE", 0, C), V("EW", 0, C), 1.0, A.mult, A.add)
         for h in (1, 0):
@@ -561,26 +624,34 @@ def rank_program(g, core, T, topo):
             gfill(V("W1", 0, C))
             gfill(V("EW", 0, C), 1)
         YQ, YS, NS = "YQ%d" % t, "YS%d" % t, "NS%d" % t
-        for hf in (1, 0):
-            o = HO(OL, hf)
+        if far:
+            send(V(LA_, 48, 58), HO(OL, 1), "aq")
+            arrive([V(LA_, 48, 58)], "aq")
+        act(V(NS, 0, H), IND(V("NW", 0, 688 if t else 368), HO(OL, 1)))
+        for hf in (0, 1) if far else (1, 0):
+            h = int(far and hf)
             for b in range(4):
-                y, w = V("Y", 640 * hf + b, 640 * hf + 640, 4), IND(win(b, C, 688), o)
+                y, w = V("Y", 640 * hf + b, 640 * hf + 640, 4), IND(win(h, b, C, 688 if t else 368), V(LA_, 48, 58) if h else HO(OL, hf))
                 ts(y, w, 0.5, A.mult) if b < 2 else lin(y, w, 0.5)
-            if hf:
+            if hf and not far:
                 quant(YQ, YS, ("Y", 640), 0, H)
-                rec("g", "remote", [U8V(V(ZQ, H, C)), U8V(V(YQ, 0, H))], nw=0, kind="r", extra=("aq%d" % t, t))
-                rec("g", "remote", [V(ZS, H, C), V(YS, 0, H)], nw=0, kind="r", extra=("aq%d" % t, t))
-                act(V(NS, 0, H), IND(V("NW", 0, 688), o))
-                rec("g", "remote", [V(Fn, 224, 384), V(NS, 0, H)], nw=0, kind="r", extra=("af%d" % t, t))
+                send(U8V(V(ZQ, H, C)), U8V(V(YQ, 0, H)), "aq")
+                send(V(ZS, H, C), V(YS, 0, H), "aq")
+                arrive([V(ZQ, H, C), V(ZS, H, C)], "aq")
             else:
-                quant(ZQ, ZS, ("Y", 0), 0, H)
+                quant(ZQ, ZS, ("Y", 640 * hf), H * hf, H)
+        if last and far:
+            ts(V(NS, H, H + 80), V(NS, 1, H, 2), 2.0, A.mult)
+            tt(V(NS, 256, 336), V(NS, H, H + 80), V(NS, 0, H, 2), A.add)
+            send(V(Fn, 224, 304), V(NS, 256, 336), "af")
+            arrive([V(Fn, 224, 304)], "af")
+        else:
+            send(V(Fn, 224, 384), V(NS, 0, H), "af")
+            arrive([V(Fn, 224, 384)], "af")
         for hf in range(2):
             a = H * hf
-            if hf:
-                rec("n", "arrive", [V(ZQ, H, C), V(ZS, H, C)], nw=2, kind="a", extra=("aq%d" % t, t, 2))
-                rec("n", "arrive", [V(Fn, 224, 384)], kind="a", extra=("af%d" % t, t, 1))
-            else:
-                act(V(Fn, 32, 192), IND(V("NW", 0, 688), HO(OL, 0)))
+            if not hf:
+                act(V(Fn, 32, 192), IND(V("NW", 0, 688 if t else 368), HO(OL, 0)))
             for b in range(4):
                 mm("P%d" % (4 + b), "WQ", "WS", b, ZQ, ZS, a, H)
                 act(V("RL", C * b + a, C * b + a + H), V("P%d" % (4 + b), 0, H), AF.Relu, scale=0.015625)
@@ -596,18 +667,18 @@ def rank_program(g, core, T, topo):
                 for nm, co in (("RB", "AR"), ("RA", "AL")):
                     scan(V(nm, a + H + 14, a + 15, -1), V(co, 0, H - 1), fr, 0.0, A.add, A.mult)
                 conv(Fn, H, "TE", f0 - 1, w)
-                conv(Fn, H, "TF", f0, w)
                 conv("RB", H, "TQ", a + 16, w)
-                ts(lg(0), pick("TE", H, 0, w), 1024.0, A.mult)
+                lin(lg(0), pick("TE", H, 0, w), 1024.0)
                 tt(lg(0), lg(0), kw, A.add)
                 ts(HO(OSA, hf), lg(0, 10), 640.0, A.min)
                 tt(lg(1), pick("TQ", H, 7, w), lg(0), A.add)
                 ts(HO(OSB, hf), lg(1, 10), float(C), A.add, 640.0, A.min)
-                ts(lg(2), pick("TE", H, 0, w), C - 1.0, A.mult)
+                lin(lg(2), pick("TE", H, 0, w), C - 1.0)
                 tt(lg(2), lg(2), kw, A.add)
                 cp(O(OMB + 10 * hf, 10), lg(2, 10))
-                tt(lg(3), pick("TF", H, 0, w), kw, A.add)
-                ts(O(OMF + 10 * hf, 10), lg(3, 10), a + H - 1.0, A.min)
+                act(lg(3), pick("TQ", H, 7, w), AF.Sign)
+                tt(lg(3), lg(3), kw, A.add)
+                cp(O(OMF + 10 * hf, 10), lg(3, 10))
                 pl, pr = ("P4", "P5") if hf else ("P2", "P3")
                 mm(pl, "UL", "ULS", 0, XQn, XSn, a, H)
                 mm(pr, "UR", "URS", 0, XQn, XSn, a, H)
@@ -627,16 +698,23 @@ def rank_program(g, core, T, topo):
                         dma("s" if k % 2 else "y", ("raw", T.osc[4 * k:4 * k + 4, :]), ("rows", slice(32 * k, 32 * k + 4), V("XS3", 0, C)))
                 act(V("YO", a, a + H), V(py, 0, H))
                 dma("s", ("raw", T.y[:, a:a + H]), V("YO", a, a + H))
-                cp(V("OLT", a, a + H), IND(V("PW", 0, 688), HO(OPL, hf)))
-                act(V("OLT", C + a, C + a + H - 1), V("F3", fa_(hf), fa_(hf) + H - 1))
+                act(V("OLT", a, a + H), IND(V("PW", 0, 688), HO(OPL, hf)))
+                if hf and far:
+                    ts(V("OLT", C + H + 1, 640, 2), V("F3", 224, 304), 2.0, A.is_ge)
+                    ts(V("F3", 304, 384), V("F3", 224, 304), 2.0, A.is_ge, -2.0, A.mult)
+                    tt(V("OLT", C + H, 640, 2), V("F3", 224, 304), V("F3", 304, 384), A.add)
+                else:
+                    act(V("OLT", C + a, C + a + H - 1), V("F3", fa_(hf), fa_(hf) + H - 1))
                 if hf:
                     dma("y", ("raw", T.ol[:, :]), ("rows", slice(0, 128, 16), V("OLT", 0, 640)))
     emit(g, core, rank, T, topo, ops)
 
 
 PLAN = {}
-WAIT, DMA, FAR, SLOW = 210.0, 2500.0, 3200.0, 1.15
-PASSES, MIX = 4, 1.0
+WAIT, DMA, FAR, SLOW = 210.0, 2500.0, 2000.0, 1.2
+PASSES, MOVES, TOL = 5, 900, 60.0
+PV, SPLIT = 0, 2
+GATH, SCAT, PE = 1.45, 3.7, 1.1
 
 
 def link(ops):
@@ -660,26 +738,30 @@ def link(ops):
 
 
 def cost(o):
-    if o["kind"] != "c":
-        return {"a": 0.0, "d": 60.0, "r": 300.0}[o["kind"]]
+    if o["kind"] in "ad":
+        return {"a": 0.0, "d": 60.0}[o["kind"]]
 
     def width(x):
         if x[0] == "ind":
             return 16 * width(x[2])
         return len(range(x[2], x[3] if x[3] != "end" else -1, x[4])) if x[0] == "ap" else width(x[-1])
 
+    if o["kind"] == "r":
+        x = o["a"][1]
+        return 16 * (50 + width(x) * (4 if x[0] == "u8" else 1 if SCRATCH[x[1]][2] == U8 else 2) / 16)
+
     a = [x for x in o["a"] if isinstance(x, tuple)]
     n = max(width(x) for x in a)
     if a[0][0] == "ind":
-        return 50 + 2.9 * n
+        return 50 + SCAT * n
     if any(x[0] == "ind" for x in a):
-        return 60 + 1.25 * width(a[0])
+        return 60 + GATH * width(a[0])
     if o["m"] == "quantize_mx":
         return 12 + 0.22 * n
     if o["m"] == "iota":
         return 130 + 1.66 * n
     if o["m"] == "matmul_mx":
-        return 0.83 * (width(a[0]) + 16)
+        return PE * (width(a[0]) + 16)
     if o["m"] == "tensor_tensor":
         n *= 1 + all(SCRATCH[x[1]][0] != "psum" for x in a)
     elif o["m"] not in ("activation", "tensor_reduce") and all(SCRATCH[x[1]][2] == BF for x in a if width(x) > 1):
@@ -702,7 +784,7 @@ def sweep(eng, c, nxt, rank):
         p = sorted(pool[e], key=lambda i: -rank[i])
         best = None
         for x, i in enumerate(p):
-            if ready[i] <= now and all(now + c[i] + rank[k] <= max(ready[k] + rank[k], ready[k] + c[k] + rank[i]) for k in p[:x] if ready[k] > now):
+            if ready[i] <= now and all(now + c[i] + rank[k] <= TOL + max(ready[k] + rank[k], ready[k] + c[k] + rank[i]) for k in p[:x] if ready[k] > now):
                 best = i
                 break
         if best is None:
@@ -732,23 +814,43 @@ def schedule(ops):
     rank = [0.0] * n
     for i in range(n - 1, -1, -1):
         rank[i] = c[i] + max([w + rank[k] for k, w in nxt[i]] + [lag[i]])
-    chain, best = rank, None
+    best, soon = None, [1e6 * bool(o.get("soon") or o["kind"] == "d" and not o["dep"]) for o in ops]
 
-    def span(order, k, far):
-        free, end = {}, [0.0] * n
-        for i in order:
-            at = max([free.get(eng[i], 0.0)] + [end[j] + w + (far - FAR) * (ops[j]["kind"] == "r") for j, w in prv[i]])
-            free[eng[i]] = end[i] = at + k * c[i]
-        return max(end) / (1 + k)
+    def play(rank):
+        order, first = sweep(eng, c, nxt, [r + s for r, s in zip(rank, soon)])
+        total, held = 0.0, []
+        for k in (0.85, 1.25):
+            free, end, by = {}, [0.0] * n, [-1] * n
+            for i in order:
+                at, by[i] = max([free.get(eng[i], (0.0, -1))] + [(end[j] + w, j) for j, w in prv[i]])
+                end[i] = at + k * c[i]
+                free[eng[i]] = (end[i], i)
+            i = max(range(n), key=lambda q: end[q])
+            total += end[i] / k ** 0.6
+            while by[i] >= 0:
+                if all(by[i] != j for j, w in prv[i]):
+                    held.append((by[i], i))
+                i = by[i]
+        return total, held, order, rank, first
 
     for _ in range(PASSES):
-        order, end = sweep(eng, c, nxt, rank)
-        s = span(order, 0.9, FAR / 2) + span(order, 1.0, FAR) + span(order, 1.3, 1.5 * FAR)
-        if best is None or s < best[0]:
-            best = (s, order)
-        back = sweep(eng, c, prv, end)[1]
-        rank = [MIX * back[i] + (1 - MIX) * chain[i] * max(back) / max(chain) for i in range(n)]
-    return best[1]
+        now = play(rank)
+        if best is None or now[0] < best[0]:
+            best = now
+        rank = sweep(eng, c, prv, now[4])[1]
+    tried = set()
+    for _ in range(MOVES):
+        left = [(j, i, d) for j, i in best[1] for d in (0, 1) if (j, i, d) not in tried and (d or best[3][j] <= best[3][i])]
+        if not left:
+            break
+        j, i, d = left[0]
+        tried.add(left[0])
+        rank = list(best[3])
+        rank[j] = min(rank[j], rank[i]) - 300 if d else rank[j] + 1500
+        now = play(rank)
+        if now[0] < best[0] - 1:
+            best = now
+    return best[2]
 
 
 def emit(g, core, rank, T, topo, ops):

@@ -4,7 +4,8 @@ C, H, K2, R = 320, 160, 88, 3
 STEP = [1, 2, 4]
 BIG = 2.0 ** 90
 U = 1.0 / 1024
-NA = (13, 15, 15)
+NV = ((0, 1, 2, 3, 16, 17, 18),) * 2
+ORD = ((0, 1, 4, 2, 3), (0, 1, 2, 4, 3))
 NB = (3, 4, 5)
 RADIX = ((4, 4, 3), (3, 3, 3, 2))
 F32, BF, I32, U16, X4, U8 = "float32", "bfloat16", "int32", "uint16", "float8_e4m3fn_x4", "uint8"
@@ -24,14 +25,12 @@ def _slots(buf, names, n, more=0, d=F32):
 
 
 _buf("P0 P1 P2 P3 P4 P5 P6 P7", 512, F32, "psum")
-EARLY = (0,)
-_buf("X0 X1 X2 X3 Y DH DG DP", 1280, BF)
-_buf("XQ0 XQ1 XQ2 XQ3 ZQ0 ZQ1 ZQ2", C, X4)
-_buf("XS0 XS1 XS2 XS3 ZS0 ZS1 ZS2", C, U8)
-for _t in range(R):
-    _buf(("PQ%d" if _t in EARLY else "YQ%d") % _t, C, X4)
-    _buf(("PS%d" if _t in EARLY else "YS%d") % _t, C, U8)
-_buf("NS0 NS1 NS2", 336, BF)
+_buf("X0 X1 X2 X3 Y DH DG", 1280, BF)
+_buf("XQ0 XQ1 XQ2 XQ3 ZQ0 ZQ1 ZQ2 PQ0", C, X4)
+_buf("XS0 XS1 XS2 XS3 ZS0 ZS1 ZS2 PS0", C, U8)
+_buf("YQ1 YQ2", H, X4)
+_buf("YS1 YS2", H, U8)
+_buf("NS1 NS2", H, BF)
 _buf("F1 F2 F3", 416, BF)
 _buf("UB VB", 512, BF)
 _buf("UQ VQ UL UR", 128, X4)
@@ -61,10 +60,10 @@ _buf("EQV", 192, BF)
 _buf("MSK", 16, F32)
 _buf("MK GT GE CAP PP ZB", C, BF)
 _buf("JK", 1280, BF)
-_buf("YV KZ KT", C, F32)
+_buf("YV KZ KT", 324, F32)
 _buf("RL", 1280, F32)
 _buf("WIN0 WIN1", 4 * 1008, BF)
-_buf("L0 L1 L2", 72, U16)
+_buf("L0", 72, U16)
 _buf("NW", 688, BF)
 _buf("PW", 688, F32)
 _buf("W1 W2", 432, F32)
@@ -72,7 +71,7 @@ _buf("TK", 704, F32)
 _buf("EW", 4096, F32)
 _buf("TE TQ", 704, BF)
 _buf("SG", 768, BF)
-_buf("SH", 576, BF)
+_buf("SH", 768, BF)
 _buf("AB", C, BF)
 _buf("OLT", 640, F32)
 _buf("YO", C, F32)
@@ -81,19 +80,20 @@ _buf("cf", 96, F32)
 _buf("sm", 32, F32)
 _buf("lg", 256, F32)
 _buf("off", 592, U16)
-_buf("lw SB", 288, F32)
+_buf("lw SB", 384, F32)
 _buf("GJ", 768, F32)
-_slots("PB", "RW RS", 112, 16)
-_slots("PC", "FJ FA FB FC", 224, 40)
-_slots("PD", "LA LB LC D00 D01 D02 D03 D1 XO", 232)
-_slots("QA", "DW VM WV VR VC TN XX N1 N2 N3", 96)
-_slots("QB", "TS TJ TP TX CJ MT FS FR DA VA", 224)
-_slots("QC", "CEL CER KE CS FI EV", 352)
+_slots("PB", "EA EB2", 112, 16)
+_slots("PE", "RW RS", 144)
+_slots("PC", "FA FB FC FJ", 224, 72)
+_slots("PD", "LA LB LC D00 D01 D02 D03 D1 XO", 296)
+_slots("QA", "DW VM WV VR VC TN TZ N1 N2 N3", 128)
+_slots("QB", "TS TJ TP TX CJ MT FS FR VA DA", 224, 32)
+_slots("QC", "CEL CER KE CS FI YW YC EV", 352, 32)
 _slots("QE", "RA RB AL AR", 352, 0, BF)
 
 ENG = ["v", "s", "t", "g"]
 SEMAPHORES = ["e" + e for e in ENG] + ["d%d" % i for i in range(20)] + \
-             [s + str(t) for t in range(R) for s in ("aq", "af", "ax", "ap")] + ["sent"]
+             ["ax0", "ap0", "aq0", "aq1", "af1", "aq2", "af2", "sent"]
 
 
 def V(n, a, b=None, s=1):
@@ -207,9 +207,9 @@ def rank_program(g, core, T, topo):
     def dma(e, o, i, behind=None):
         rec(e, "dma_start", [o, i], kind="d", behind=behind)
 
-    def conv(src, n, tbuf, a=16, at=0):
+    def conv(src, n, tbuf, a=16, at=0, more=32):
         tr(V(tbuf, at, at + n), V(src, a, a + n))
-        tr(V(tbuf, at + n, at + 2 * n + 32), V(src, a - 16, a + n + 16))
+        tr(V(tbuf, at + n, at + 2 * n + more), V(src, a - 16, a + n - 16 + more))
 
     PKS = {}
     for n, r in ((160, 0), (192, 0), (96, 0), (96, 6), (96, 3), (160, 7), (160, 1), (160, 2)):
@@ -230,13 +230,17 @@ def rank_program(g, core, T, topo):
         tr(V(tbuf, 96, 224), V(src, 8, 264, 2))
         ts(O(o, 16), pick(tbuf, 96), float(K2), A.min, 2.0, A.mult)
 
+    def back(dst, a, src, b):
+        for k in range(2):
+            tr(V(dst, a + k, a + 128, 2), V(src, b + 64 * k, b + 64 * k + 64))
+
     QF, HF, P32, G16, PF = [V("cf", i) for i in range(5)]
     KB, KW, RJ, J2, PR, CC = 8, 16, 48, 64, 68, 80
-    tmp = lambda i, n=6: V("lw", 12 * i, 12 * i + n)
+    tmp = lambda i, n=8: V("lw", 12 * i, 12 * i + n)
     zb = lambda n: V("ZB", 0, n)
     kt = lambda i: V("KT", 32 * i)
     fa_ = lambda h: 32 + 192 * h
-    rj = V("cf", RJ, RJ + 6)
+    rj = V("cf", RJ, RJ + 8)
 
     dma("s", V("UB", 0, 512), ("raw", T.u[:]))
     dma("y", V("X0", 0, 640), ("raw", T.x[:, 0:640]))
@@ -252,14 +256,13 @@ def rank_program(g, core, T, topo):
     iota(V("IO", 0, 336), [[1, 336]], 0)
     iota(V("CI", 512, 1024), [[4, 32], [0, 16]], 0)
     iota(V("cf", KW, KW + 32), [[16, 32]], 0)
-    iota(rj, [[32, 3], [0, 2]], 0)
+    iota(rj, [[1, 2], [64, 2], [0, 2]], 0)
     iota(V("ci", 24, 36), [[1, 12]], -1)
     ms(zb(C), 0.0)
-    ops[-1]["soon"] = True
     ms(V("KZ", 0, C), 0.0)
-    ops[-1]["soon"] = True
-    for a in range(0, 2048, 512):
-        gfill(V("EB", a, a + 512))
+    ops[-2]["soon"] = ops[-1]["soon"] = 1e6
+    for a in range(0, 2048, 256):
+        act(V("EB", a, a + 256), zb(256))
     for nm, a, n, c in (("M", 0, 16, 0.0), ("M", 336, 352, 0.0), ("SM", C, 336, -BIG),
                         ("SC", C, 336, -BIG), ("CV", 0, 16, -BIG), ("SW", 640, 656, -BIG)):
         ms(V(nm, a, n), c)
@@ -274,13 +277,14 @@ def rank_program(g, core, T, topo):
     ts(V("ci", 16, 18), V("cf", J2, J2 + 2), HF, A.add)
     ts(V("ci", 18, 20), V("ci", 16, 18), 1, A.bitwise_and)
     ts(V("cf", J2 + 2, J2 + 4), V("cf", J2, J2 + 2), 16.0, A.mult)
-    pn = {160: 0, 192: 1, 96: 2, 288: 3}
+    pn = {160: 0, 192: 1, 96: 2}
     for n, i in pn.items():
-        for j in range(1 + (n == 288)):
-            ts(V("cf", PR + 2 * i + j), V("ci", 18 + j), n + 16.0, A.mult, V("cf", J2 + 2 + j), A.add)
+        ts(V("cf", PR + 2 * i), V("ci", 18), n + 16.0, A.mult, V("cf", J2 + 2), A.add)
     for (n, r), o in PKS.items():
         ts(O(o, 1), V("cf", PR + 2 * pn[n]), float(r), A.add, 2 * n + 31.0, A.min)
-    ts(O(PKE, 2), V("cf", PR + 6, PR + 8), 607.0, A.min)
+    ts(V("cf", 5), QF, 6.0, A.is_ge, -100.0, A.mult)
+    ts(V("cf", 6), V("cf", PR + 4), 4.0, A.add)
+    ts(O(PKE, 1), V("cf", 5), V("cf", 6), A.add, 223.0, A.min)
     for r in range(2):
         ts(O(PKA + r, 1), V("cf", PR + 4), float(r), A.add, 223.0, A.min)
     ts(O(OREP, 12), V("ci", 24, 36), 0.0, A.max)
@@ -303,44 +307,51 @@ def rank_program(g, core, T, topo):
             table[q, k] = table.get((q, k), 0) + 8 * len(NB)
     for q, co in SINK.items():
         table[q, 6], table[q, 7] = co
-    table[0, 8], table[1, 9] = U, 1
+    table[0, 8], table[4, 8], table[1, 9] = U, U, 1
     for (q, k), c in table.items():
         twin = table.get((q, k ^ 1)) == c
         if c and not (twin and k % 2):
             lin(V("KZ", 32 * k + q, 32 * k + 32 + 32 * twin, 16), zb(2 + 2 * twin), 1.0, float(c))
-            ops[-1]["soon"] = True
+            ops[-1]["soon"] = 1e6
     tr(V("KT", 0, C), V("KZ", 0, C))
-    ts(rj, rj, P32, A.add)
-    ts(V("ci", 40, 46), rj, 0.5, A.mult, -0.25, A.add)
+    ts(rj, rj, P32, A.add, P32, A.add)
+    ts(V("ci", 40, 48), rj, 0.5, A.mult, -0.25, A.add)
     for o in (V("FJ", 216, 232, 2), V("XO", 216, 232, 2)):
         ts(o, V("IO", 0, 8), kt(7), A.mult, kt(6), A.add)
     for i, (a, b, s) in enumerate(((1, 4, 1), (4, 13, 4), (16, 49, 16))):
         ts(V("cf", CC + 3 * i, CC + 3 * i + 3), V("IO", a, b, s), kt(9), A.mult, U, A.mult)
     ts(V("cf", CC + 9), kt(9), -47 * U, A.mult)
+    ts(V("cf", 92), QF, -1.5, A.add)
+    ts(V("cf", 92), V("cf", 92), V("cf", 92), A.mult)
+    ts(V("cf", 90), V("cf", 92), 1.0, A.is_lt, -1.0, A.mult)
+    ts(V("cf", 91), V("cf", 92), 1.0, A.is_lt, 2.0, A.mult)
+    lin(V("cf", 93), kt(9), -1.0)
+    lin(V("cf", 94), kt(9), 2.0)
     ts(tmp(22), rj, 336.0, A.add)
-    ts(tmp(23), V("ci", 40, 46), 322.0, A.add)
+    ts(tmp(23), V("ci", 40, 48), 322.0, A.add)
     lin(V("CEL", 0, 336), V("IO", 0, 336), kt(0), kt(4))
     lin(V("CER", 0, 336), V("IO", 0, 336), kt(1), kt(5))
     lin(V("AL", 0, H), zb(H), 1.0, kt(2))
     lin(V("AR", 0, H), zb(H), 1.0, kt(3))
     iota(V("PW", 0, 368), [[1, 368]], 0)
     iota(V("PW", 368, 688), [[-1, C]], C - 1)
-    for nm, a, n, c in (("CAP", C - 1, C, K2), ("CV", 208, 224, 0), ("PB", 0, 16, 0), ("PB", 112, 128, 0), ("PB", 224, 240, 0),
-                        ("SB", 0, 288, 0), ("DW", 0, 96, 0), ("DA", 0, 192, 0), ("W1", 0, C, 0), ("W2", C, 432, 0),
-                        ("CS", 0, 1, 0), ("CS", C + 1, 352, 0), ("EV", 0, 16, 0), ("EV", 208, 352, 0), ("EW", 0, C, 1),
+    for nm, a, n, c in (("CAP", C - 1, C, K2), ("YC", 0, 161, 0), ("YC", 161, 162, 1024), ("TC", 384, 416, 0), ("TR", 384, 416, 0), ("PB", 0, 16, 0), ("PB", 112, 128, 0), ("PB", 224, 240, 0), ("RW", 0, 16, 0), ("RS", 0, 16, 0),
+                        ("SB", 0, 384, 0), ("DW", 0, 128, 0), ("DA", 0, 256, 0), ("FJ", 232, 296, 0), ("XO", 232, 296, 0),
+                        ("LA", 232, 296, 0), ("LB", 232, 296, 0), ("W1", 0, C, 0), ("W2", C, 432, 0),
+                        ("CS", 0, 1, 0), ("CS", C + 1, 352, 0), ("EW", 0, C, 1),
                         ("FI", 0, 16, 0), ("FI", 336, 352, 0), ("NW", 0, C, 0),
                         ("NW", C, 368, 1), ("RA", 0, 352, 0), ("RB", 0, 352, 0), ("SW", 0, 640, 0)):
         gfill(V(nm, a, n), c)
     gfill(V("OLT", C + H - 1, 640, H))
-    for a in range(8, 936, 224):
+    for a in range(8, 896, 224):
         gfill(V("PC", a, a + 32, 2))
     for st in range(4):
         gfill(V("D0%d" % st, 39, 215, 2), -(2 ** 23))
     for nm in ("F1", "F2"):
         for a in (0, 192, 384):
             gfill(V(nm, a, a + 32))
-    ts(V("SB", 192, 288, 16), rj, 4000.0, A.add, U, A.mult)
-    cp(V("DA", 97, 192, 16), tmp(23))
+    ts(V("SB", 256, 384, 16), rj, 4000.0, A.add, U, A.mult)
+    cp(V("DA", 129, 256, 16), tmp(23))
 
     quant("UQ", "US", ("UB", 0), 0, 128)
     for nm, o in (("UL", OU), ("UR", OU + 8)):
@@ -372,34 +383,37 @@ def rank_program(g, core, T, topo):
         def arrive(dst, sem):
             rec("n", "arrive", dst, nw=len(dst), kind="a", extra=(sem + str(t), t, len(dst)))
 
-        if t in EARLY:
-            send(U8V(V("PQ%d" % t, 0, C)), U8V(V(XQ, 0, C)), "ax")
-            send(V("PS%d" % t, 0, C), V(XS, 0, C), "ax")
-            if t:
-                send(V("L%d" % t, 0, 40), O(OMF, 40), "ax")
-        order = (0, 1, 4, 2, 3) if t else (4, 0, 1, 3, 2)
+        far = t == 0
+        if far:
+            send(U8V(V("PQ0", 0, C)), U8V(V(XQ, 0, C)), "ax")
+            send(V("PS0", 0, C), V(XS, 0, C), "ax")
+            ops[-2]["soon"] = ops[-1]["soon"] = 1e6
+        order = ORD[min(t, 1)]
         for i in range(20):
             s = V("MW", i + 6 * (i // 10))
-            for a, n in ((0, H), (H, H)) if t and i < 10 or i // 4 == order[4] else ((0, C),):
-                o = V("TA", 1280 * (i // 4) + 4 * a + i % 4, 1280 * (i // 4) + 4 * (a + n), 4)
-                if i < NA[t]:
-                    act(o, V("M", 16 + a, 16 + a + n), AF.Sign, scale=-1.0, bias=s)
+            for a in (0, H):
+                o = V("TA", 1280 * (i // 4) + 4 * a + i % 4, 1280 * (i // 4) + 4 * (a + H), 4)
+                if i not in NV[min(t, 1)]:
+                    act(o, V("M", 16 + a, 16 + a + H), AF.Sign, scale=-1.0, bias=s)
                 else:
-                    ts(o, V("M", 16 + a, 16 + a + n), s, A.is_lt, 2.0, A.mult)
-        for k in order:
-            for a, n in ((0, H), (H, H)) if t and k < 2 or k == order[4] else ((0, C),):
-                quant("AQ", "AP", ("TA", 4 * (C * k + a)), C * k + a, n)
-            mm("P7", "CQ", "CP", 0, "AQ", "AP", C * k, C, k == order[0], k == order[4])
-        s0, sg, a1, a2, a3, tau = [V("sm", i) for i in range(6)]
-        ts(V("MK", 0, C), V("P7", 0, C), 2 * K2 - 0.5 - 16 * NA[t], A.is_gt, -1024.0, A.mult)
-        act(V("JK", 0, C), V("MK", 0, C), accum_out=s0)
-        lin(sg, s0, -4.0, -4096.0 * (C - K2 + 0.5))
-        tt(V("YV", 0, C), V("P7", 0, C), V("MK", 0, C), A.add)
-        red(a2, V("YV", 0, C), A.min)
-        red(a1, V("YV", 0, C), A.max)
-        lin(a3, a2, 1.0, 1024.0)
-        ts(tau, a1, sg, A.max, a3, A.min)
-        act(V("AB", 0, C), V("P7", 0, C))
+                    ts(o, V("M", 16 + a, 16 + a + H), s, A.is_lt, 2.0, A.mult)
+        s0, s1, sg, a1, a2, a3, tau = [V("sm", i) for i in range(7)]
+        for h in range(2):
+            a, p, y = H * h, V("P%d" % (6 + h), 0, H), V("YV", 162 * h, 162 * h + H)
+            for k in order:
+                quant("AQ", "AP", ("TA", 4 * (C * k + a)), C * k + a, H)
+                mm(p[1], "CQ", "CP", 0, "AQ", "AP", C * k + a, H, k == order[0], k == order[4])
+            ts(V("MK", a, a + H), p, 2 * K2 - 0.5 - 16 * (20 - len(NV[min(t, 1)])), A.is_gt, -1024.0, A.mult)
+            act(V("JK", a, a + H), V("MK", a, a + H), accum_out=s0)
+            lin(sg if h else s1, s0, -4.0, s1 if h else -4096.0 * (C - K2 + 0.5))
+            tt(y, p, V("MK", a, a + H), A.add)
+            if h:
+                scan(V("YW", 0, 162), V("YV", 161, 323), V("YC", 0, 162), BIG, A.min, A.add)
+            else:
+                red(V("YV", 161), y, A.min)
+            red(a1 if h else V("YV", 322), V("YV", 161, 323) if h else y, A.max)
+            act(V("AB", a, a + H), p)
+        ts(tau, a1, sg, A.max, V("YW", 161), A.min)
         ts(V("GT", 0, C), V("AB", 0, C), tau, A.is_lt)
         ts(V("GE", 0, C), V("AB", 0, C), tau, A.is_le)
         scan(V("CAP", C - 2, "end", -1), zb(C - 1), V("GT", C - 1, 0, -1), float(K2), A.add, A.subtract)
@@ -423,60 +437,58 @@ def rank_program(g, core, T, topo):
             tt(V("MT", 1, 192, 2), IND(V("RB", 16, 352), O(OI)), V("CJ", 1, 192, 2), A.add)
         else:
             lin(V("MT", 0, 192), V("CJ", 0, 192), 1.0, V("cf", CC + 9))
-        conv("CV", 192, "TC")
+        conv("CV", 192, "TC", more=0)
         cp(V("CW", 0, 16), pick("TC", 192))
         tt(V("EQV", 0, 192), IND(V("CW", 0, 16), O(OREP, 12)), V("CV", 0, 192), A.is_equal)
         for q in range(16):
             lin(V("TB", 768 * 2 + 3 + 4 * q, 768 * 3, 64), V("EQV", q, 192, 16), V("MSK", q))
         for c in range(11):
             a, m = 768 * (c // 4) + c % 4, 16 * c + 32
-            lo, hi = V("TB", a, a + 4 * m - c % 4, 4), V("TB", a + 4 * m, 768 * (c // 4 + 1), 4)
+            f = 16 * (t > 0)
+            lo, hi = V("TB", a + 4 * f, a + 4 * m - c % 4, 4), V("TB", a + 4 * m, 768 * (c // 4 + 1), 4)
             if c in NB:
                 s = 192 * NB.index(c)
                 act(V("SH", s, s + 192), V("CV", 0, 192), AF.Sign, scale=-1.0, bias=V("CW", c))
-                act(lo, V("SH", s, s + m), AF.Sign, bias=-0.5)
+                act(lo, V("SH", s + f, s + m), AF.Sign, bias=-0.5)
                 act(hi, V("SH", s + m, s + 192), AF.Sign, bias=0.5)
                 continue
-            ts(lo, V("CV", 0, m), V("CW", c), A.is_lt, 2.0, A.mult)
+            ts(lo, V("CV", f, m), V("CW", c), A.is_lt, 2.0, A.mult)
             if m < 192:
                 ts(hi, V("CV", m, 192), V("CW", c), A.is_le, 2.0, A.mult)
         for k in range(3):
             quant("BQ", "BP", ("TB", 768 * k), 192 * k, 192)
-            mm("P7", "CQ", "CP", 1, "BQ", "BP", 192 * k, 192, k == 0, k == 2)
-        conv("P7", 192, "TR")
+            mm("P5", "CQ", "CP", 1, "BQ", "BP", 192 * k, 192, k == 0, k == 2)
+        conv("P5", 192, "TR", more=0)
         for e in range(2):
-            tt(V("FS", e, 176, 2), V("P7", 17 - e, 192, 2), V("MT", e, 176, 2), A.add)
+            tt(V("FS", e, 176, 2), V("P5", 17 - e, 192, 2), V("MT", e, 176, 2), A.add)
         ts(O(OR, 16), pick("TR", 192), 8.0 * len(NB), A.add)
         cp(IND(V("FR", 0, 192), O(OR, 11)), V("FS", 0, 176))
         cp(V("FJ", 40, 216, 4), V("FR", 1, K2, 2))
         act(V("FJ", 42, 216, 4), V("FR", 0, K2, 2))
         conv2("FJ", "TJ", OW)
         cp(O(OP, 16), pick("TJ", 96, 6))
-        z = lambda r: V("TJ", r, 96, 16)
-        far = t in EARLY
-        LA_, PQ, PS = "L%d" % t, "PQ%d" % t, "PS%d" % t
+        for k in range(2):
+            tr(V("TZ", 64 * k, 64 * k + 64), V("FJ", 40 + 2 * k, 296, 4))
+        z = lambda r: V("TZ", r, 128, 16)
+        LA_ = "L0"
         if far:
             send(V(LA_, 64, 70), O(OP), "ap")
-            arrive([U8V(V(PQ, 0, C)), V(PS, 0, C)] + [V(LA_, 0, 40)] * (t > 0), "ax")
+            arrive([U8V(V("PQ0", 0, C)), V("PS0", 0, C)], "ax")
             arrive([V(LA_, 64, 70)], "ap")
         for h in range(1 + far):
-            omf, omb, op = (V(LA_, 0, 20), V(LA_, 20, 40), V(LA_, 64, 70)) if h else (O(OMF, 20), O(OMB, 20), O(OP))
+            op = V(LA_, 64, 70) if h else O(OP)
             for b in range(4):
-                dh, dg, p = V("DH", C * b, C * b + C), V("DG", C * b, C * b + C), V("P%d" % ((b + 4 * h) % 7), 0, C)
+                dh, p = V("DH", C * b, C * b + C), V("P%d" % ((4, 6, 7, 0)[b] if h else b), 0, C)
                 gj = 384 * h + 96 * b
-                mm(p[1], "EQ", "ES", b, PQ if h else XQ, PS if h else XS, 0, C)
+                mm(p[1], "EQ", "ES", b, "PQ0" if h else XQ, "PS0" if h else XS, 0, C)
                 if t:
-                    if h:
-                        dh = V("DP", C * b, C * b + C)
                     act(dh, p)
                     lin(win(h, b, 0), dh, 2.0)
-                    part = lambda o, k: (o[0], o[1], o[2] + 20 // SPLIT * k, o[2] + 20 // SPLIT * (k + 1), 1)
-                    n = C // SPLIT
-                    for k in range(SPLIT):
-                        act(V("DG", C * b + n * k, C * b + n * k + n), IND(dh, part(omf, k)))
-                    tt(win(h, b, C), p, dg, A.add)
-                    for k in range(SPLIT):
-                        act(V("WIN%d" % h, 1008 * b + 1007 - n * k, 1008 * b + 1007 - n * k - n, -1), IND(win(h, b, 0, 2 * C), part(omb, k)))
+                    for a in (0, H):
+                        act(V("DG", C * b + a, C * b + a + H), IND(dh, O(OMF + a // 16, 10)))
+                        tt(win(h, b, C + a, H), V(p[1], a, a + H), V("DG", C * b + a, C * b + a + H), A.add)
+                    for a in (0, H):
+                        act(V("WIN0", 1008 * b + 1007 - a, 1008 * b + 1007 - a - H, -1), IND(win(h, b, 0, 2 * C), O(OMB + a // 16, 10)))
                     act(V("GJ", gj, gj + 96), IND(dh, op))
                 else:
                     lin(win(h, b, C), p, 2.0)
@@ -486,25 +498,30 @@ def rank_program(g, core, T, topo):
             for h in range(2):
                 act(V("NW", H * h, H * h + H - 1), V(F, fa_(h), fa_(h) + H - 1))
                 act(V("NW", 687 - H * h, 687 - H * h - H, -1), V(F, fa_(h) - 1, fa_(h) + H - 1))
+        first = len(ops)
         ts(tmp(0), z(3), float(K2), A.is_lt)
         tt(tmp(2), tmp(22), z(4), A.add)
         lin(tmp(3), z(7), -1.0, float(C))
         tt(tmp(0), tmp(0), z(8), A.mult)
         tt(tmp(2), tmp(2), tmp(0), A.mult)
         tt(tmp(3), tmp(3), tmp(0), A.mult)
-        tt(V("SB", 0, 96, 16), tmp(2), z(4), A.subtract)
-        tt(V("SB", 1, 96, 16), tmp(3), z(7), A.add)
-        lin(V("SB", 96, 192, 16), z(11))
+        tt(V("SB", 0, 128, 16), tmp(2), z(4), A.subtract)
+        tt(V("SB", 1, 128, 16), tmp(3), z(7), A.add)
+        for r in (0, 4):
+            lin(V("SB", 128 + r, 256, 16), z(11))
         for r in (1, 2) if last else (1,):
-            lin(V("SB", 192 + r, 288, 16), z(7), 1.0, 2.0)
-        tr(V("RS", 16, 112), V("SB", 0, 96))
-        tr(V("WV", 0, 192), V("SB", 96, 288))
+            lin(V("SB", 256 + r, 384, 16), z(7), 1.0, 2.0)
+        back("RS", 16, "SB", 0)
+        back("WV", 0, "SB", 128)
+        back("VR", 0, "SB", 256)
         conv("RS", 96, "TP")
         cp(O(OA, 32), IND(V("TP", 0, 224), O(PKA, 2)))
         lin(V("W2", 0, C), zb(C), 1.0, kt(8))
         cp(IND(V("W2", 0, 432), O(OA)), V("WV", 0, 96))
         ts(V("TN", 0, 96), IND(V("W2", 0, 432), O(OA + 16)), 0.0, A.is_le)
         tt(V("VC", 0, 96), V("TN", 0, 96), V("VR", 0, 96), A.mult)
+        for o in ops[first:]:
+            o["soon"] = 0.0 if t else 1500.0
         if t:
             lin(tmp(20), tmp(0), 1600.0 * U)
             tt(tmp(20), tmp(20), z(5), A.subtract)
@@ -512,7 +529,9 @@ def rank_program(g, core, T, topo):
         else:
             tt(tmp(20), z(4), tmp(23), A.add)
         if last:
-            lin(V("DA", 98, 192, 16), z(6), 1.0, 2.0)
+            lin(V("DA", 130, 256, 16), z(6), 1.0, 2.0)
+        if t:
+            back("EV", 0, "DA", 128)
         fb = cur = "FJ"
         if t:
             act(dv("D1", K2), dv("FJ", K2))
@@ -526,7 +545,8 @@ def rank_program(g, core, T, topo):
                 fa = fb
                 for k in range(rx - 1):
                     fo = [x for x in ("FA", "FB", "FC") if x != fa and x != fb][0]
-                    (cp if t and k < PV else act)(dv(fo), IND(V(fa, 40, 232), o))
+                    act(dv(fo), IND(V(fa, 40, 232), o))
+                    ops[-1]["soon"] = 300.0
                     fa = fo
                 fb = fa
             if t:
@@ -552,68 +572,67 @@ def rank_program(g, core, T, topo):
                     cur = nx
             if more:
                 conv2(fb, "TS", OW + 16 * st + 16)
-        cp(V("XX", 0, 96, 2), V(cur, 42, 232, 4))
-        act(V("XX", 1, 96, 2), V(cur, 40, 232, 4))
-        tr(V("TX", 0, 96), dv(cur))
-        tr(V("TX", 96, 192), V("XX", 0, 96))
-        x1 = lambda r: V("TX", r, 96, 16)
-        x2 = lambda r: V("TX", 96 + r, 192, 16)
-        d1, d2 = V("lw", 60, 66), V("lw", 66, 72)
+        for k in range(3):
+            tr(V("TX", 64 * k, 64 * k + 64), V(cur, 40 + 2 * (k % 2), 296, 4))
+        x1 = lambda r: V("TX", r, 128, 16)
+        x2 = lambda r: V("TX", 64 + r, 192, 16)
+        d1, d2 = V("lw", 60, 68), V("lw", 64, 72)
         tt(tmp(6), x1(3), rj, A.not_equal)
         tt(tmp(5, 12), V("TX", 3, 192, 16), V("TX", 1, 192, 16), A.subtract)
-        tt(V("DW", 3, 96, 16), x1(4), x2(4), A.max)
+        tt(V("DW", 3, 128, 16), x1(4), x2(4), A.max)
         tt(tmp(7, 12), V("TX", 2, 192, 16), V("TX", 3, 192, 16), A.subtract)
         tt(tmp(8), tmp(6), d2, A.mult)
-        tt(tmp(9), V("DW", 3, 96, 16), z(4), A.is_equal)
-        tt(tmp(12), tmp(7), V("lw", 90, 96), A.is_ge)
+        tt(tmp(9), V("DW", 3, 128, 16), z(4), A.is_equal)
+        tt(tmp(12), tmp(7), V("lw", 88, 96), A.is_ge)
         tt(tmp(10), tmp(8), d1, A.add)
-        tt(V("DW", 0, 96, 16), tmp(10), tmp(9), A.mult)
+        tt(V("DW", 0, 128, 16), tmp(10), tmp(9), A.mult)
+        if t:
+            tt(V("DW", 4, 128, 16), tmp(10), tmp(9), A.mult)
         lin(tmp(14), tmp(6), -800.0 * U, 799.0 * U)
         tt(tmp(14), tmp(14), d1, A.add)
         if t:
-            tt(tmp(17), d1, z(5), A.is_gt)
+            tt(tmp(17), x1(3), z(3), A.not_equal)
             tt(tmp(18), tmp(6), tmp(21), A.mult)
-            tt(tmp(17), tmp(17), tmp(6), A.subtract)
-            tt(tmp(18), tmp(18), tmp(20), A.add)
             tt(tmp(17), tmp(17), tmp(21), A.mult)
-            tt(tmp(11), d1, tmp(18), A.add)
             tt(tmp(13), d1, z(5), A.subtract)
-            tt(tmp(13), tmp(13), tmp(17), A.subtract)
+            tt(tmp(19), tmp(18), tmp(20), A.add)
+            tt(tmp(17), tmp(17), tmp(8), A.add)
+            tt(tmp(13), tmp(13), tmp(18), A.add)
+            tt(tmp(11), d1, tmp(19), A.add)
             lin(tmp(16), tmp(12), 400.0 * U)
-            tt(tmp(13), tmp(8), tmp(13), A.subtract)
+            tt(tmp(13), tmp(17), tmp(13), A.subtract)
             tt(tmp(15), tmp(12), z(10), A.mult)
             tt(tmp(13), tmp(13), tmp(12), A.mult)
             for r in (1, 2) if last else (1,):
-                tt(V("DA", r, 96, 16), tmp(15), z(9), A.add)
-            tt(V("DA", 96, 192, 16), tmp(14), tmp(16), A.add)
-            tt(V("DA", 0, 96, 16), tmp(13), tmp(11), A.add)
+                tt(V("DA", r, 128, 16), tmp(15), z(9), A.add)
+            tt(V("DA", 4, 128, 16), tmp(14), tmp(16), A.add)
+            tt(V("DA", 0, 128, 16), tmp(13), tmp(11), A.add)
         else:
             ts(tmp(16), d1, 1.5 * U, A.is_gt, 400.0 * U, A.mult)
             lin(tmp(20), tmp(20), -1.0, 2.0)
             tt(tmp(16), tmp(16), tmp(8), A.add)
             tt(tmp(15), tmp(12), tmp(20), A.mult)
             tt(tmp(13), tmp(16), tmp(14), A.subtract)
-            tt(V("DA", 1, 96, 16), tmp(15), tmp(23), A.add)
+            tt(V("DA", 1, 128, 16), tmp(15), tmp(23), A.add)
             tt(tmp(13), tmp(13), tmp(12), A.mult)
-            tt(V("DA", 0, 96, 16), tmp(13), tmp(14), A.add)
+            tt(V("DA", 0, 128, 16), tmp(13), tmp(14), A.add)
         ne = 288 if t else 192
-        tr(V("RW", 16, 112), V("DW", 0, 96))
+        back("RW", 16, "DW", 0)
         cp(IND(V("W1", 0, 432), O(OA)), V("RW", 16, 112))
         conv("RW", 96, "TP")
         scan(V("CS", 1, C + 1), V("W1", 0, C), V("W2", 0, C), 0.0, A.add, A.add)
         ts(O(OMM, 16), pick("TP", 96, 3), -1.0, A.mult)
-        tr(V("VA", 0, ne - 96), V("DA", 0, ne - 96))
-        tt(V("EV", 112, 208), IND(V("CS", 0, 352), O(OA + 16)), V("VC", 0, 96), A.max)
-        tt(V("EV", 16, 112), IND(V("CS", 0, 352), O(OMM)), V("VA", 0, 96), A.add)
-        if t:
-            tt(V("EV", 208, 304), IND(V("CS", 0, 352), O(OMM)), V("VA", 96, 192), A.add)
-        conv("EV", ne, "TK")
-        if t:
-            ts(O(OK_, 32), IND(V("TK", 0, 608), O(PKE, 2)), 1024.0, A.mult)
-        else:
-            ts(O(OK_, 16), pick("TK", 192), 1024.0, A.mult)
-        cp(IND(V("EW", 0, 4096), O(OK_, ne // 16)), V("EV", 16, 16 + ne))
-        ts(V("KE", 0, C), V("EW", 0, C), 1.0, A.is_equal)
+        back("EV", 96, "DA", 0)
+        tt(V("EB2", 16, 112), IND(V("CS", 0, 352), O(OA + 16)), V("VC", 0, 96), A.max)
+        tt(V("EA", 16, 112), IND(V("CS", 0, 352), O(OMM)), V("EV", 96, 192), A.add)
+        conv("EB2", 96, "TS")
+        ts(O(OK_, 16), pick("TS", 96), 1024.0, A.mult)
+        conv("EA", 96, "VA")
+        ts(O(OK_ + 16, 16), IND(V("VA", 0, 224), O(PKE, 1)) if t else pick("VA", 96), 1024.0, A.mult)
+        cp(IND(V("EW", 0, 4096), O(OK_)), V("VR", 0, 96))
+        cp(IND(V("EW", 0, 4096), O(OK_ + 16, ne // 16 - 6)), V("EV", 288 - ne, 192))
+        ts(V("KE", 0, H), V("EW", 0, H), 1.0, A.is_equal)
+        act(V("KE", H, C), V("EW", H, C), AF.Relu, scale=V("cf", 90 if last else 93), bias=V("cf", 91 if last else 94))
         scan(V("FI", 16, 336), V("KE", 0, C), V("EW", 0, C), 1.0, A.mult, A.add)
         for h in (1, 0):
             conv("FI", H, "TK", 16 + H * h, 352 * h)
@@ -627,7 +646,7 @@ def rank_program(g, core, T, topo):
         if far:
             send(V(LA_, 48, 58), HO(OL, 1), "aq")
             arrive([V(LA_, 48, 58)], "aq")
-        act(V(NS, 0, H), IND(V("NW", 0, 688 if t else 368), HO(OL, 1)))
+            act(V(Fn, 224, 384), IND(V("NW", 0, 368), V(LA_, 48, 58)))
         for hf in (0, 1) if far else (1, 0):
             h = int(far and hf)
             for b in range(4):
@@ -640,12 +659,8 @@ def rank_program(g, core, T, topo):
                 arrive([V(ZQ, H, C), V(ZS, H, C)], "aq")
             else:
                 quant(ZQ, ZS, ("Y", 640 * hf), H * hf, H)
-        if last and far:
-            ts(V(NS, H, H + 80), V(NS, 1, H, 2), 2.0, A.mult)
-            tt(V(NS, 256, 336), V(NS, H, H + 80), V(NS, 0, H, 2), A.add)
-            send(V(Fn, 224, 304), V(NS, 256, 336), "af")
-            arrive([V(Fn, 224, 304)], "af")
-        else:
+        if not far:
+            act(V(NS, 0, H), IND(V("NW", 0, 688), HO(OL, 1)))
             send(V(Fn, 224, 384), V(NS, 0, H), "af")
             arrive([V(Fn, 224, 384)], "af")
         for hf in range(2):
@@ -684,7 +699,9 @@ def rank_program(g, core, T, topo):
                 mm(pr, "UR", "URS", 0, XQn, XSn, a, H)
                 act(V("SW", a, a + H), V(pl, 0, H))
                 cp(V("SW", C + a, C + a + H), V(pr, 0, H))
-                act(V("SM", a, a + H), IND(V("SW", 0, 656), HO(OSA, hf)))
+                act(V("SM", a, a + 64 + 96 * (1 - hf)), IND(V("SW", 0, 656), O(OSA + 16 * hf, 10 - 6 * hf)))
+                if hf:
+                    cp(V("SM", a + 64, a + H), IND(V("SW", 0, 656), O(OSA + 20, 6)))
                 tt(V("M", 16 + a, 16 + a + H), IND(V("SW", 0, 656), HO(OSB, hf)), V("SM", a, a + H), A.max)
                 act(V("SC", a, a + H), IND(V("SW", 0, 656), HO(OSB, hf)))
                 conv("M", H, "TM", 16 + a, w)
@@ -699,21 +716,16 @@ def rank_program(g, core, T, topo):
                 act(V("YO", a, a + H), V(py, 0, H))
                 dma("s", ("raw", T.y[:, a:a + H]), V("YO", a, a + H))
                 act(V("OLT", a, a + H), IND(V("PW", 0, 688), HO(OPL, hf)))
-                if hf and far:
-                    ts(V("OLT", C + H + 1, 640, 2), V("F3", 224, 304), 2.0, A.is_ge)
-                    ts(V("F3", 304, 384), V("F3", 224, 304), 2.0, A.is_ge, -2.0, A.mult)
-                    tt(V("OLT", C + H, 640, 2), V("F3", 224, 304), V("F3", 304, 384), A.add)
-                else:
-                    act(V("OLT", C + a, C + a + H - 1), V("F3", fa_(hf), fa_(hf) + H - 1))
+                act(V("OLT", C + a, C + a + H - 1), V("F3", fa_(hf), fa_(hf) + H - 1))
                 if hf:
                     dma("y", ("raw", T.ol[:, :]), ("rows", slice(0, 128, 16), V("OLT", 0, 640)))
     emit(g, core, rank, T, topo, ops)
 
 
 PLAN = {}
-WAIT, DMA, FAR, SLOW = 210.0, 2500.0, 2000.0, 1.2
-PASSES, MOVES, TOL = 5, 900, 60.0
-PV, SPLIT = 0, 2
+WAIT, DMA, FAR, SLOW = 225.0, 2500.0, 2000.0, 1.2
+START, LONG, TOL = 1500.0, 450.0, 45.0
+PASSES, MOVES = 5, 1200
 GATH, SCAT, PE = 1.45, 3.7, 1.1
 
 
@@ -737,7 +749,7 @@ def link(ops):
                 hist.setdefault(nm, []).append((i, False, m))
 
 
-def cost(o):
+def cost(o, GATH=GATH, SCAT=SCAT, PE=PE):
     if o["kind"] in "ad":
         return {"a": 0.0, "d": 60.0}[o["kind"]]
 
@@ -814,19 +826,26 @@ def schedule(ops):
     rank = [0.0] * n
     for i in range(n - 1, -1, -1):
         rank[i] = c[i] + max([w + rank[k] for k, w in nxt[i]] + [lag[i]])
-    best, soon = None, [1e6 * bool(o.get("soon") or o["kind"] == "d" and not o["dep"]) for o in ops]
+    best, soon = None, [1e6 if o["kind"] == "d" and not o["dep"] else o.get("soon", 0.0) for o in ops]
+
+    near = [[(j, w - FAR * (ops[j]["kind"] == "r")) for j, w in p] for p in prv]
+    ends = [([cost(o, 1.25, 2.9, 0.9) for o in ops], 1.0), ([1.4 * cost(o, 1.66, 4.5, 1.1) for o in ops], 0.75)]
 
     def play(rank):
         order, first = sweep(eng, c, nxt, [r + s for r, s in zip(rank, soon)])
         total, held = 0.0, []
-        for k in (0.85, 1.25):
-            free, end, by = {}, [0.0] * n, [-1] * n
+        for ck, weight in ends:
+            free, end, by, dma = {}, [0.0] * n, [-1] * n, 0.0
             for i in order:
-                at, by[i] = max([free.get(eng[i], (0.0, -1))] + [(end[j] + w, j) for j, w in prv[i]])
-                end[i] = at + k * c[i]
-                free[eng[i]] = (end[i], i)
+                at, by[i] = max([free.get(eng[i], (0.0, -1))] + [(end[j] + w, j) for j, w in near[i]])
+                if ops[i]["kind"] == "r":
+                    end[i] = dma = max(at + START, dma) + ck[i]
+                    free[eng[i]] = (at + 300.0, i)
+                else:
+                    end[i] = at + ck[i]
+                    free[eng[i]] = (end[i], i)
             i = max(range(n), key=lambda q: end[q])
-            total += end[i] / k ** 0.6
+            total += end[i] * weight
             while by[i] >= 0:
                 if all(by[i] != j for j, w in prv[i]):
                     held.append((by[i], i))
@@ -850,6 +869,7 @@ def schedule(ops):
         now = play(rank)
         if now[0] < best[0] - 1:
             best = now
+    PLAN["end"] = best[4]
     return best[2]
 
 
@@ -876,7 +896,12 @@ def emit(g, core, rank, T, topo, ops):
     if "order" not in PLAN:
         PLAN["order"] = schedule(ops)
     ops = [ops[i] for i in PLAN["order"]]
+    end = [PLAN["end"][i] for i in PLAN["order"]]
     link(ops)
+    line = {}
+    for i, o in enumerate(ops):
+        o["i"], o["at"] = i, len(line.setdefault(o["e"], []))
+        line[o["e"]].append(o)
     known = {e: {} for e in qs}
     for o in ops:
         o["clock"] = {}
@@ -889,6 +914,10 @@ def emit(g, core, rank, T, topo, ops):
             key = p["e"] if p["kind"] == "c" else ("x", j)
             if kn.get(key, -1) >= j:
                 continue
+            if p["kind"] == "c":
+                j = max([j] + [k for q in line[o["e"]][o["at"] + 1:o["at"] + 60] for k in q["dep"]
+                               if k < o["i"] and ops[k]["kind"] == "c" and ops[k]["e"] == key and end[k] + LONG <= end[o["i"]] - SLOW * cost(o)])
+                p = ops[j]
             o["need"].append(j)
             p["sig"] = True
             kn[key] = j

from concourse.mybir import dt, AluOpType as A, AxisListType, ActivationFunctionType as AF

C, H, K2, R = 320, 160, 88, 3
STEP = [1, 2, 4]
BIG = 2.0 ** 90
U = 1.0 / 1024
NV = ((0, 1, 2, 3, 16, 17, 18),) * 2
ORD = ((0, 1, 4, 2, 3), (0, 1, 2, 4, 3))
NB = (3, 4, 5)
RADIX = ((4, 4, 3), (3, 3, 3, 2))
F32, BF, I32, U16, X4, U8 = "float32", "bfloat16", "int32", "uint16", "float8_e4m3fn_x4", "uint8"
SCRATCH = {}
SLOT = {}


def _buf(names, n, d, where="sbuf"):
    for s in names.split():
        SCRATCH[s] = (where, [128, n], d)


def _slots(buf, names, n, more=0, d=F32):
    for i, s in enumerate(names.split()):
        SLOT[s] = (buf, n * i)
    _buf(buf, n * len(names.split()) + more, d)


_buf("P0 P1 P2 P3 P4 P5 P6 P7", 512, F32, "psum")
_buf("X0 X1 X2 X3 Y DH DG", 1280, BF)
_buf("XQ0 XQ1 XQ2 XQ3 ZQ0 ZQ1 ZQ2 PQ0", C, X4)
_buf("XS0 XS1 XS2 XS3 ZS0 ZS1 ZS2 PS0", C, U8)
_buf("YQ1 YQ2", H, X4)
_buf("YS1 YS2", H, U8)
_buf("NS1 NS2", H, BF)
_buf("F1 F2 F3", 416, BF)
_buf("UB VB", 512, BF)
_buf("UQ VQ UL UR", 128, X4)
_buf("US VS ULS URS", 128, U8)
_buf("WQ EQ", 512, X4)
_buf("WS ES", 512, U8)
_buf("EB", 2048, BF)
_buf("ID", 128, BF)
_buf("CB", 1024, BF)
_buf("CI", 1024, BF)
_buf("CQ", 256, X4)
_buf("CP", 256, U8)
_buf("TA", 5 * 1280, BF)
_buf("AQ", 5 * C, X4)
_buf("AP", 5 * C, U8)
_buf("TB", 3 * 768, BF)
_buf("BQ", 3 * 192, X4)
_buf("BP", 3 * 192, U8)
_buf("SW", 656, F32)
_buf("IO SM SC", 336, F32)
_buf("M", 352, F32)
_buf("TM", 704, F32)
_buf("MW CW", 32, F32)
_buf("CV", 224, F32)
_buf("TC TR", 416, F32)
_buf("EQV", 192, BF)
_buf("MSK", 16, F32)
_buf("MK GT GE CAP PP ZB", C, BF)
_buf("JK", 1280, BF)
_buf("YV KZ KT", 324, F32)
_buf("RL", 1280, F32)
_buf("WIN0 WIN1", 4 * 1008, BF)
_buf("L0", 72, U16)
_buf("NW", 688, BF)
_buf("PW", 688, F32)
_buf("W1 W2", 432, F32)
_buf("TK", 704, F32)
_buf("EW", 4096, F32)
_buf("TE TQ", 704, BF)
_buf("SG", 768, BF)
_buf("SH", 768, BF)
_buf("AB", C, BF)
_buf("OLT", 640, F32)
_buf("YO", C, F32)
_buf("ci HI", 96, I32)
_buf("cf", 96, F32)
_buf("sm", 32, F32)
_buf("lg", 256, F32)
_buf("off", 592, U16)
_buf("lw SB", 384, F32)
_buf("GJ", 768, F32)
_slots("PB", "EA EB2", 112, 16)
_slots("PE", "RW RS", 144)
_slots("PC", "FA FB FC FJ", 224, 72)
_slots("PD", "LA LB LC D00 D01 D02 D03 D1 XO", 296)
_slots("QA", "DW VM WV VR VC TN TZ N1 N2 N3", 128)
_slots("QB", "TS TJ TP TX CJ MT FS FR VA DA", 224, 32)
_slots("QC", "CEL CER KE CS FI YW YC EV", 352, 32)
_slots("QE", "RA RB AL AR", 352, 0, BF)

ENG = ["v", "s", "t", "g"]
SEMAPHORES = ["e" + e for e in ENG] + ["d%d" % i for i in range(20)] + \
             ["ax0", "ap0", "aq0", "aq1", "af1", "aq2", "af2", "sent"]


def V(n, a, b=None, s=1):
    b = a + 1 if b is None else b
    if n in SLOT:
        return ("ap", SLOT[n][0], a + SLOT[n][1], b + SLOT[n][1], s)
    return ("ap", n, a, b, s)


def IND(w, o):
    return ("ind", w, o)


def U8V(w):
    return ("u8", w)


def U32V(w):
    return ("u32", w)


def O(a, n=6):
    return V("off", a, a + n)


def touched(x):
    if not isinstance(x, tuple) or x[0] == "raw":
        return []
    if x[0] == "ap":
        if SCRATCH[x[1]][0] == "psum":
            return [(x[1], 1)]
        if x[4] == 1:
            return [(x[1], ((1 << (x[3] - x[2])) - 1) << x[2])]
        return [(x[1], sum(1 << i for i in range(x[2], x[3] if x[3] != "end" else -1, x[4])))]
    if x[0] == "ind":
        return touched(x[1]) + touched(x[2])
    return touched(x[-1])


ROWS = {1: (0, -U, -U, 0, -U, -U), 2: (U, U, U / 2, U, 0, 0), 4: (-1, 0, 0, -1, 0, 0),
        5: (0, U, U, 0, U, U), 6: (1, 0, 0, 1, 1, 0), 7: (1, 1, 1, 1, 1, 1), 8: (0, 0, 0, 0, 0, 1),
        9: (-1, -1, 689, 1, 0, 2), 10: (2, 1, -687, -2, -1, 687), 11: (0, -U, 0, 0, -U, 0)}
SINK = {0: (K2, 0), 1: (-1000 - 378 * U, U), 2: (-1000, 0), 3: (-1000, 0), 4: (-330, 0), 8: (1, 0), 9: (2, 0)}


def rank_program(g, core, T, topo):
    rank = T.rank_of(core)
    if rank is None:
        return
    ops = []

    def rec(e, meth, args, nw=1, kw=None, kind="c", extra=None, behind=None):
        kw = kw or {}
        wr, rd = [], touched(behind)
        for i, a in enumerate(args):
            if i < nw and isinstance(a, tuple) and a[0] == "ind":
                wr += touched(a[1])
                rd += touched(a[2])
            elif i < nw:
                wr += touched(a)
            else:
                rd += touched(a)
        for k, a in kw.items():
            if k == "accum_out":
                wr += touched(a)
            else:
                rd += touched(a)
        ops.append({"e": e, "m": meth, "a": args, "kw": kw, "wr": wr, "rd": rd, "kind": kind, "x": extra})

    def ts(o, i, s1, op0, s2=None, op1=None):
        rec("v", "tensor_scalar", [o, i, s1, s2, op0] + ([op1] if op1 is not None else []))

    def tt(o, a, b, op):
        rec("v", "tensor_tensor", [o, a, b, op])

    def cp(o, i):
        rec("v", "tensor_copy", [o, i])

    def ms(o, c):
        rec("v", "memset", [o, c])

    def tr(o, i):
        rec("v", "transpose", [o, i])

    def red(o, i, op):
        rec("v", "tensor_reduce", [o, i, AxisListType.X, op])

    def scan(o, d0, d1, init, op0, op1):
        rec("v", "tensor_tensor_scan", [o, d0, d1, init, op0, op1])

    def act(o, i, f=AF.Copy, **kw):
        rec("s", "activation", [o, i, f], kw=kw)

    def lin(o, i, scale=1.0, bias=0.0):
        act(o, i, AF.Identity if isinstance(bias, tuple) or isinstance(scale, tuple) else AF.Copy, scale=scale, bias=bias)

    def iota(o, pat, base, cm=0):
        kw = {} if SCRATCH[o[1]][2] == I32 else {"allow_small_or_imprecise_dtypes": True}
        rec("g", "iota", [o, pat, base, cm], kw=kw)

    def gfill(o, c=0):
        iota(o, [[0, len(range(o[2], o[3], o[4]))]], c)

    def quant(q, s, x, a, n):
        rec("v", "quantize_mx", [V(q, a, a + n), V(s, a, a + n), V(x[0], x[1], x[1] + 4 * n)], nw=2)

    def mm(p, w, ws, k, x, xs, a, n, start=True, stop=True):
        rec("t", "matmul_mx", [V(p, 0, n), V(w, 128 * k, 128 * k + 128), V(ws, 128 * k, 128 * k + 128), V(x, a, a + n), V(xs, a, a + n), start, stop],
            extra=None if start else "acc")

    def dma(e, o, i, behind=None):
        rec(e, "dma_start", [o, i], kind="d", behind=behind)

    def conv(src, n, tbuf, a=16, at=0, more=32):
        tr(V(tbuf, at, at + n), V(src, a, a + n))
        tr(V(tbuf, at + n, at + 2 * n + more), V(src, a - 16, a + n - 16 + more))

    PKS = {}
    for n, r in ((160, 0), (192, 0), (96, 0), (96, 6), (96, 3), (160, 7), (160, 1), (160, 2)):
        PKS[n, r] = 2 * len(PKS)
    PKA, PKE, OU, OREP = 16, 18, 20, 36
    OI, OR, OW, OP, OA, OMM, OK_, OL, OPL, OMF, OMB, OSA, OSB = \
        48, 64, 80, 176, 192, 224, 240, 272, 304, 336, 356, 400, 416
    HO = lambda base, h: O(base + 16 * h, 10)

    def pick(tbuf, n, row=0, at=0):
        return IND(V(tbuf, at, at + 2 * n + 32), O(PKS[n, row], 1))

    def dv(buf, n=96):
        return V(buf, 40, 40 + 2 * n, 2)

    def conv2(src, tbuf, o):
        tr(V(tbuf, 0, 96), dv(src))
        tr(V(tbuf, 96, 224), V(src, 8, 264, 2))
        ts(O(o, 16), pick(tbuf, 96), float(K2), A.min, 2.0, A.mult)

    def back(dst, a, src, b):
        for k in range(2):
            tr(V(dst, a + k, a + 128, 2), V(src, b + 64 * k, b + 64 * k + 64))

    QF, HF, P32, G16, PF = [V("cf", i) for i in range(5)]
    KB, KW, RJ, J2, PR, CC = 8, 16, 48, 64, 68, 80
    tmp = lambda i, n=8: V("lw", 12 * i, 12 * i + n)
    zb = lambda n: V("ZB", 0, n)
    kt = lambda i: V("KT", 32 * i)
    fa_ = lambda h: 32 + 192 * h
    rj = V("cf", RJ, RJ + 8)

    dma("s", V("UB", 0, 512), ("raw", T.u[:]))
    dma("y", V("X0", 0, 640), ("raw", T.x[:, 0:640]))
    dma("s", V("X0", 640, 1280), ("raw", T.x[:, 640:1280]))
    dma("y", U8V(V("WQ", 0, 512)), ("raw", T.wc[:]), V("X0", 0, 1280))
    dma("y", V("WS", 0, 512), ("raw", T.ws[:]), V("X0", 0, 1280))
    dma("y", V("VB", 0, 512), ("raw", T.v[:]), V("X0", 0, 1280))
    iota(V("ci", 0), [[0, 1]], 0, 1)
    iota(V("ci", 8, 16), [[16, 8]], 0)
    iota(V("cf", J2, J2 + 2), [[16, 2]], 0)
    iota(PF, [[0, 1]], 0, 1)
    iota(V("CI", 0, 512), [[16, 8], [0, 64]], 0)
    iota(V("IO", 0, 336), [[1, 336]], 0)
    iota(V("CI", 512, 1024), [[4, 32], [0, 16]], 0)
    iota(V("cf", KW, KW + 32), [[16, 32]], 0)
    iota(rj, [[1, 2], [64, 2], [0, 2]], 0)
    iota(V("ci", 24, 36), [[1, 12]], -1)
    ms(zb(C), 0.0)
    ms(V("KZ", 0, C), 0.0)
    ops[-2]["soon"] = ops[-1]["soon"] = 1e6
    for a in range(0, 2048, 256):
        act(V("EB", a, a + 256), zb(256))
    for nm, a, n, c in (("M", 0, 16, 0.0), ("M", 336, 352, 0.0), ("SM", C, 336, -BIG),
                        ("SC", C, 336, -BIG), ("CV", 0, 16, -BIG), ("SW", 640, 656, -BIG)):
        ms(V(nm, a, n), c)
    ts(V("ci", 1), V("ci", 0), 15, A.bitwise_and)
    ts(V("ci", 2), V("ci", 0), 4, A.arith_shift_right, 1, A.bitwise_and)
    ts(V("ci", 3), V("ci", 0), 31, A.bitwise_and)
    ts(V("ci", 4), V("ci", 0), 112, A.bitwise_and)
    cp(O(OU, 8), V("ci", 8, 16))
    ts(O(OU + 8, 8), V("ci", 8, 16), 1.0, A.add)
    cp(V("cf", 0, 4), V("ci", 1, 5))
    ts(V("cf", J2, J2 + 2), V("cf", J2, J2 + 2), QF, A.add)
    ts(V("ci", 16, 18), V("cf", J2, J2 + 2), HF, A.add)
    ts(V("ci", 18, 20), V("ci", 16, 18), 1, A.bitwise_and)
    ts(V("cf", J2 + 2, J2 + 4), V("cf", J2, J2 + 2), 16.0, A.mult)
    pn = {160: 0, 192: 1, 96: 2}
    for n, i in pn.items():
        ts(V("cf", PR + 2 * i), V("ci", 18), n + 16.0, A.mult, V("cf", J2 + 2), A.add)
    for (n, r), o in PKS.items():
        ts(O(o, 1), V("cf", PR + 2 * pn[n]), float(r), A.add, 2 * n + 31.0, A.min)
    ts(V("cf", 5), QF, 6.0, A.is_ge, -100.0, A.mult)
    ts(V("cf", 6), V("cf", PR + 4), 4.0, A.add)
    ts(O(PKE, 1), V("cf", 5), V("cf", 6), A.add, 223.0, A.min)
    for r in range(2):
        ts(O(PKA + r, 1), V("cf", PR + 4), float(r), A.add, 223.0, A.min)
    ts(O(OREP, 12), V("ci", 24, 36), 0.0, A.max)
    for k in range(2):
        ts(V("CB", 512 * k, 512 * k + 512), V("CI", 512 * k, 512 * k + 512), G16, A.is_equal, 1.0 - k / 2, A.mult)
        quant("CQ", "CP", ("CB", 512 * k), 128 * k, 128)
    ts(V("ID", 0, 128), V("IO", 0, 128), PF, A.is_equal)
    for b in range(4):
        cp(V("EB", 513 * b, 512 * (b + 1), 4), V("ID", 0, 128))
        quant("EQ", "ES", ("EB", 512 * b), 128 * b, 128)
    ts(V("cf", KW, KW + 32), V("cf", KW, KW + 32), QF, A.add)
    ts(V("cf", KB, KB + 6), V("cf", KW, KW + 6), 0.5, A.add)
    ts(V("MSK", 0, 16), V("IO", 0, 16), QF, A.is_gt, 2.0, A.mult)
    table = {}
    for q, co in ROWS.items():
        for k, c in enumerate(co):
            table[q, 2 * (k % 3) + k // 3] = c
    for q in range(4):
        for k in (4, 5):
            table[q, k] = table.get((q, k), 0) + 8 * len(NB)
    for q, co in SINK.items():
        table[q, 6], table[q, 7] = co
    table[0, 8], table[4, 8], table[1, 9] = U, U, 1
    for (q, k), c in table.items():
        twin = table.get((q, k ^ 1)) == c
        if c and not (twin and k % 2):
            lin(V("KZ", 32 * k + q, 32 * k + 32 + 32 * twin, 16), zb(2 + 2 * twin), 1.0, float(c))
            ops[-1]["soon"] = 1e6
    tr(V("KT", 0, C), V("KZ", 0, C))
    ts(rj, rj, P32, A.add, P32, A.add)
    ts(V("ci", 40, 48), rj, 0.5, A.mult, -0.25, A.add)
    for o in (V("FJ", 216, 232, 2), V("XO", 216, 232, 2)):
        ts(o, V("IO", 0, 8), kt(7), A.mult, kt(6), A.add)
    for i, (a, b, s) in enumerate(((1, 4, 1), (4, 13, 4), (16, 49, 16))):
        ts(V("cf", CC + 3 * i, CC + 3 * i + 3), V("IO", a, b, s), kt(9), A.mult, U, A.mult)
    ts(V("cf", CC + 9), kt(9), -47 * U, A.mult)
    ts(V("cf", 92), QF, -1.5, A.add)
    ts(V("cf", 92), V("cf", 92), V("cf", 92), A.mult)
    ts(V("cf", 90), V("cf", 92), 1.0, A.is_lt, -1.0, A.mult)
    ts(V("cf", 91), V("cf", 92), 1.0, A.is_lt, 2.0, A.mult)
    lin(V("cf", 93), kt(9), -1.0)
    lin(V("cf", 94), kt(9), 2.0)
    ts(tmp(22), rj, 336.0, A.add)
    ts(tmp(23), V("ci", 40, 48), 322.0, A.add)
    lin(V("CEL", 0, 336), V("IO", 0, 336), kt(0), kt(4))
    lin(V("CER", 0, 336), V("IO", 0, 336), kt(1), kt(5))
    lin(V("AL", 0, H), zb(H), 1.0, kt(2))
    lin(V("AR", 0, H), zb(H), 1.0, kt(3))
    iota(V("PW", 0, 368), [[1, 368]], 0)
    iota(V("PW", 368, 688), [[-1, C]], C - 1)
    for nm, a, n, c in (("CAP", C - 1, C, K2), ("YC", 0, 161, 0), ("YC", 161, 162, 1024), ("TC", 384, 416, 0), ("TR", 384, 416, 0), ("PB", 0, 16, 0), ("PB", 112, 128, 0), ("PB", 224, 240, 0), ("RW", 0, 16, 0), ("RS", 0, 16, 0),
                        ("SB", 0, 384, 0), ("DW", 0, 128, 0), ("DA", 0, 256, 0), ("FJ", 232, 296, 0), ("XO", 232, 296, 0),
                        ("LA", 232, 296, 0), ("LB", 232, 296, 0), ("W1", 0, C, 0), ("W2", C, 432, 0),
                        ("CS", 0, 1, 0), ("CS", C + 1, 352, 0), ("EW", 0, C, 1),
                        ("FI", 0, 16, 0), ("FI", 336, 352, 0), ("NW", 0, C, 0),
                        ("NW", C, 368, 1), ("RA", 0, 352, 0), ("RB", 0, 352, 0), ("SW", 0, 640, 0)):
        gfill(V(nm, a, n), c)
    gfill(V("OLT", C + H - 1, 640, H))
    for a in range(8, 896, 224):
        gfill(V("PC", a, a + 32, 2))
    for st in range(4):
        gfill(V("D0%d" % st, 39, 215, 2), -(2 ** 23))
    for nm in ("F1", "F2"):
        for a in (0, 192, 384):
            gfill(V(nm, a, a + 32))
    ts(V("SB", 256, 384, 16), rj, 4000.0, A.add, U, A.mult)
    cp(V("DA", 129, 256, 16), tmp(23))

    quant("UQ", "US", ("UB", 0), 0, 128)
    for nm, o in (("UL", OU), ("UR", OU + 8)):
        cp(U32V(V(nm, 0, 128)), IND(U32V(V("UQ", 0, 128)), O(o, 8)))
        act(V(nm + "S", 0, 128), IND(V("US", 0, 128), O(o, 8)))
    for h in range(2):
        quant("XQ0", "XS0", ("X0", 640 * h), H * h, H)
    mm("P5", "UR", "URS", 0, "XQ0", "XS0", 0, C)
    mm("P4", "UL", "ULS", 0, "XQ0", "XS0", 0, C)
    act(V("SC", 0, C), V("P5", 0, C))
    tt(V("M", 16, 16 + C), V("P4", 0, C), V("SC", 0, C), A.max)
    act(V("SM", 0, C), V("P4", 0, C))
    for h in range(2):
        conv("M", H, "TM", 16 + H * h, 352 * h)
        cp(V("MW", 16 * h, 16 * h + 16), pick("TM", H, 0, 352 * h))
    quant("VQ", "VS", ("VB", 0), 0, 128)

    win = lambda h, b, a, n=C: V("WIN%d" % h, 1008 * b + a, 1008 * b + a + n)

    for t in range(R):
        XQ, XS, F, ZQ, ZS = "XQ%d" % t, "XS%d" % t, "F%d" % t, "ZQ%d" % t, "ZS%d" % t
        Fn, Xn, XQn, XSn = "F%d" % (t + 1), "X%d" % (t + 1), "XQ%d" % (t + 1), "XS%d" % (t + 1)
        last = t == R - 1
        OP, OL = 448 + 48 * t, 464 + 48 * t

        def send(dst, src, sem):
            rec("g", "remote", [dst, src], nw=0, kind="r", extra=(sem + str(t), t))

        def arrive(dst, sem):
            rec("n", "arrive", dst, nw=len(dst), kind="a", extra=(sem + str(t), t, len(dst)))

        far = t == 0
        if far:
            send(U8V(V("PQ0", 0, C)), U8V(V(XQ, 0, C)), "ax")
            send(V("PS0", 0, C), V(XS, 0, C), "ax")
            ops[-2]["soon"] = ops[-1]["soon"] = 1e6
        order = ORD[min(t, 1)]
        for i in range(20):
            s = V("MW", i + 6 * (i // 10))
            for a in (0, H):
                o = V("TA", 1280 * (i // 4) + 4 * a + i % 4, 1280 * (i // 4) + 4 * (a + H), 4)
                if i not in NV[min(t, 1)]:
                    act(o, V("M", 16 + a, 16 + a + H), AF.Sign, scale=-1.0, bias=s)
                else:
                    ts(o, V("M", 16 + a, 16 + a + H), s, A.is_lt, 2.0, A.mult)
        s0, s1, sg, a1, a2, a3, tau = [V("sm", i) for i in range(7)]
        for h in range(2):
            a, p, y = H * h, V("P%d" % (6 + h), 0, H), V("YV", 162 * h, 162 * h + H)
            for k in order:
                quant("AQ", "AP", ("TA", 4 * (C * k + a)), C * k + a, H)
                mm(p[1], "CQ", "CP", 0, "AQ", "AP", C * k + a, H, k == order[0], k == order[4])
            ts(V("MK", a, a + H), p, 2 * K2 - 0.5 - 16 * (20 - len(NV[min(t, 1)])), A.is_gt, -1024.0, A.mult)
            act(V("JK", a, a + H), V("MK", a, a + H), accum_out=s0)
            lin(sg if h else s1, s0, -4.0, s1 if h else -4096.0 * (C - K2 + 0.5))
            tt(y, p, V("MK", a, a + H), A.add)
            if h:
                scan(V("YW", 0, 162), V("YV", 161, 323), V("YC", 0, 162), BIG, A.min, A.add)
            else:
                red(V("YV", 161), y, A.min)
            red(a1 if h else V("YV", 322), V("YV", 161, 323) if h else y, A.max)
            act(V("AB", a, a + H), p)
        ts(tau, a1, sg, A.max, V("YW", 161), A.min)
        ts(V("GT", 0, C), V("AB", 0, C), tau, A.is_lt)
        ts(V("GE", 0, C), V("AB", 0, C), tau, A.is_le)
        scan(V("CAP", C - 2, "end", -1), zb(C - 1), V("GT", C - 1, 0, -1), float(K2), A.add, A.subtract)
        scan(V("PP", 0, C), V("GE", 0, C), V("CAP", 0, C), 0.0, A.add, A.min)
        for c in range(6):
            a, n = 16 * c, min(C - K2 + 16, C - 16 * c)
            if c < 3:
                act(V("JK", C * c, C * c + n), V("PP", a, a + n), AF.Sign, scale=-1.0, bias=V("cf", KB + c), accum_out=V("sm", 8 + c))
                ts(O(OI + c, 1), V("sm", 8 + c), 0.5, A.mult, a + n / 2, A.add)
            else:
                j, k = V(("GT", "GE", "MK")[c - 3], 0, n), 256 * (c - 3)
                ts(j, V("PP", a, a + n), V("cf", KB + c), A.is_lt)
                scan(V("SG", k, k + n), j, zb(n), 0.0, A.add, A.add)
                ts(O(OI + c, 1), V("SG", k + n - 1), float(a), A.add)
        cp(V("CV", 16, 208, 2), IND(V("SM", 0, 336), O(OI)))
        act(V("CV", 17, 208, 2), IND(V("SC", 0, 336), O(OI)))
        act(V("CJ", 0, 192, 2), IND(V("CEL", 0, 336), O(OI)))
        act(V("CJ", 1, 192, 2), IND(V("CER", 0, 336), O(OI)))
        if t:
            tt(V("MT", 0, 192, 2), IND(V("RA", 16, 352), O(OI)), V("CJ", 0, 192, 2), A.add)
            tt(V("MT", 1, 192, 2), IND(V("RB", 16, 352), O(OI)), V("CJ", 1, 192, 2), A.add)
        else:
            lin(V("MT", 0, 192), V("CJ", 0, 192), 1.0, V("cf", CC + 9))
        conv("CV", 192, "TC", more=0)
        cp(V("CW", 0, 16), pick("TC", 192))
        tt(V("EQV", 0, 192), IND(V("CW", 0, 16), O(OREP, 12)), V("CV", 0, 192), A.is_equal)
        for q in range(16):
            lin(V("TB", 768 * 2 + 3 + 4 * q, 768 * 3, 64), V("EQV", q, 192, 16), V("MSK", q))
        for c in range(11):
            a, m = 768 * (c // 4) + c % 4, 16 * c + 32
            f = 16 * (t > 0)
            lo, hi = V("TB", a + 4 * f, a + 4 * m - c % 4, 4), V("TB", a + 4 * m, 768 * (c // 4 + 1), 4)
            if c in NB:
                s = 192 * NB.index(c)
                act(V("SH", s, s + 192), V("CV", 0, 192), AF.Sign, scale=-1.0, bias=V("CW", c))
                act(lo, V("SH", s + f, s + m), AF.Sign, bias=-0.5)
                act(hi, V("SH", s + m, s + 192), AF.Sign, bias=0.5)
                continue
            ts(lo, V("CV", f, m), V("CW", c), A.is_lt, 2.0, A.mult)
            if m < 192:
                ts(hi, V("CV", m, 192), V("CW", c), A.is_le, 2.0, A.mult)
        for k in range(3):
            quant("BQ", "BP", ("TB", 768 * k), 192 * k, 192)
            mm("P5", "CQ", "CP", 1, "BQ", "BP", 192 * k, 192, k == 0, k == 2)
        conv("P5", 192, "TR", more=0)
        for e in range(2):
            tt(V("FS", e, 176, 2), V("P5", 17 - e, 192, 2), V("MT", e, 176, 2), A.add)
        ts(O(OR, 16), pick("TR", 192), 8.0 * len(NB), A.add)
        cp(IND(V("FR", 0, 192), O(OR, 11)), V("FS", 0, 176))
        cp(V("FJ", 40, 216, 4), V("FR", 1, K2, 2))
        act(V("FJ", 42, 216, 4), V("FR", 0, K2, 2))
        conv2("FJ", "TJ", OW)
        cp(O(OP, 16), pick("TJ", 96, 6))
        for k in range(2):
            tr(V("TZ", 64 * k, 64 * k + 64), V("FJ", 40 + 2 * k, 296, 4))
        z = lambda r: V("TZ", r, 128, 16)
        LA_ = "L0"
        if far:
            send(V(LA_, 64, 70), O(OP), "ap")
            arrive([U8V(V("PQ0", 0, C)), V("PS0", 0, C)], "ax")
            arrive([V(LA_, 64, 70)], "ap")
        for h in range(1 + far):
            op = V(LA_, 64, 70) if h else O(OP)
            for b in range(4):
                dh, p = V("DH", C * b, C * b + C), V("P%d" % ((4, 6, 7, 0)[b] if h else b), 0, C)
                gj = 384 * h + 96 * b
                mm(p[1], "EQ", "ES", b, "PQ0" if h else XQ, "PS0" if h else XS, 0, C)
                if t:
                    act(dh, p)
                    lin(win(h, b, 0), dh, 2.0)
                    for a in (0, H):
                        act(V("DG", C * b + a, C * b + a + H), IND(dh, O(OMF + a // 16, 10)))
                        tt(win(h, b, C + a, H), V(p[1], a, a + H), V("DG", C * b + a, C * b + a + H), A.add)
                    for a in (0, H):
                        act(V("WIN0", 1008 * b + 1007 - a, 1008 * b + 1007 - a - H, -1), IND(win(h, b, 0, 2 * C), O(OMB + a // 16, 10)))
                    act(V("GJ", gj, gj + 96), IND(dh, op))
                else:
                    lin(win(h, b, C), p, 2.0)
                    lin(V("GJ", gj, gj + 96), IND(win(h, b, C), op), 0.5)
                tt(win(h, b, 2 * C, 48), V("GJ", gj, gj + 96, 2), V("GJ", gj + 1, gj + 96, 2), A.add)
        if t:
            for h in range(2):
                act(V("NW", H * h, H * h + H - 1), V(F, fa_(h), fa_(h) + H - 1))
                act(V("NW", 687 - H * h, 687 - H * h - H, -1), V(F, fa_(h) - 1, fa_(h) + H - 1))
        first = len(ops)
        ts(tmp(0), z(3), float(K2), A.is_lt)
        tt(tmp(2), tmp(22), z(4), A.add)
        lin(tmp(3), z(7), -1.0, float(C))
        tt(tmp(0), tmp(0), z(8), A.mult)
        tt(tmp(2), tmp(2), tmp(0), A.mult)
        tt(tmp(3), tmp(3), tmp(0), A.mult)
        tt(V("SB", 0, 128, 16), tmp(2), z(4), A.subtract)
        tt(V("SB", 1, 128, 16), tmp(3), z(7), A.add)
        for r in (0, 4):
            lin(V("SB", 128 + r, 256, 16), z(11))
        for r in (1, 2) if last else (1,):
            lin(V("SB", 256 + r, 384, 16), z(7), 1.0, 2.0)
        back("RS", 16, "SB", 0)
        back("WV", 0, "SB", 128)
        back("VR", 0, "SB", 256)
        conv("RS", 96, "TP")
        cp(O(OA, 32), IND(V("TP", 0, 224), O(PKA, 2)))
        lin(V("W2", 0, C), zb(C), 1.0, kt(8))
        cp(IND(V("W2", 0, 432), O(OA)), V("WV", 0, 96))
        ts(V("TN", 0, 96), IND(V("W2", 0, 432), O(OA + 16)), 0.0, A.is_le)
        tt(V("VC", 0, 96), V("TN", 0, 96), V("VR", 0, 96), A.mult)
        for o in ops[first:]:
            o["soon"] = 0.0 if t else 1500.0
        if t:
            lin(tmp(20), tmp(0), 1600.0 * U)
            tt(tmp(20), tmp(20), z(5), A.subtract)
            ts(tmp(21), z(5), U, A.is_equal, 2000.0 * U, A.mult)
        else:
            tt(tmp(20), z(4), tmp(23), A.add)
        if last:
            lin(V("DA", 130, 256, 16), z(6), 1.0, 2.0)
        if t:
            back("EV", 0, "DA", 128)
        fb = cur = "FJ"
        if t:
            act(dv("D1", K2), dv("FJ", K2))
            lin(V("VM", 0, 96), dv("FJ"), kt(9))
            ts(V("HI", 0, 96), dv("FJ"), kt(9), A.mult)
            tt(dv("D00"), V("VM", 0, 96), V("HI", 0, 96), A.subtract)
        radix = RADIX[min(t, 1)]
        for st, rx in enumerate(radix):
            o, more = O(OW + 16 * st), st + 1 < len(radix)
            if more:
                fa = fb
                for k in range(rx - 1):
                    fo = [x for x in ("FA", "FB", "FC") if x != fa and x != fb][0]
                    act(dv(fo), IND(V(fa, 40, 232), o))
                    ops[-1]["soon"] = 300.0
                    fa = fo
                fb = fa
            if t:
                d0, la = "D0%d" % st, "LC"
                if more:
                    act(dv(la), dv(d0))
                for k in range(rx - 1):
                    act(V("D1", 39, 231, 2), IND(V(cur, 40, 232), o))
                    scan(V("XO", 39, 215), V(d0, 39, 215), V("D1", 39, 215), 0.0, A.add, A.max)
                    cur = "XO"
                    if more:
                        nx = "D0%d" % (st + 1) if k == rx - 2 else "LB" if la == "LA" else "LA"
                        tt(dv(nx), IND(V(la, 40, 232), o), dv(d0), A.add)
                        la = nx
                if more:
                    cp(dv("D1", K2), dv("XO", K2))
            else:
                for k in range(rx - 1):
                    lin(V("N%d" % (k + 1), 0, 96), dv(cur), 1.0, V("cf", CC + 3 * st + k))
                for k in range(rx - 1):
                    nx = "LB" if cur == "LA" else "LA"
                    tt(dv(nx), IND(V(cur, 40, 232), o), V("N%d" % (k + 1), 0, 96), A.max)
                    cur = nx
            if more:
                conv2(fb, "TS", OW + 16 * st + 16)
        for k in range(3):
            tr(V("TX", 64 * k, 64 * k + 64), V(cur, 40 + 2 * (k % 2), 296, 4))
        x1 = lambda r: V("TX", r, 128, 16)
        x2 = lambda r: V("TX", 64 + r, 192, 16)
        d1, d2 = V("lw", 60, 68), V("lw", 64, 72)
        tt(tmp(6), x1(3), rj, A.not_equal)
        tt(tmp(5, 12), V("TX", 3, 192, 16), V("TX", 1, 192, 16), A.subtract)
        tt(V("DW", 3, 128, 16), x1(4), x2(4), A.max)
        tt(tmp(7, 12), V("TX", 2, 192, 16), V("TX", 3, 192, 16), A.subtract)
        tt(tmp(8), tmp(6), d2, A.mult)
        tt(tmp(9), V("DW", 3, 128, 16), z(4), A.is_equal)
        tt(tmp(12), tmp(7), V("lw", 88, 96), A.is_ge)
        tt(tmp(10), tmp(8), d1, A.add)
        tt(V("DW", 0, 128, 16), tmp(10), tmp(9), A.mult)
        if t:
            tt(V("DW", 4, 128, 16), tmp(10), tmp(9), A.mult)
        lin(tmp(14), tmp(6), -800.0 * U, 799.0 * U)
        tt(tmp(14), tmp(14), d1, A.add)
        if t:
            tt(tmp(17), x1(3), z(3), A.not_equal)
            tt(tmp(18), tmp(6), tmp(21), A.mult)
            tt(tmp(17), tmp(17), tmp(21), A.mult)
            tt(tmp(13), d1, z(5), A.subtract)
            tt(tmp(19), tmp(18), tmp(20), A.add)
            tt(tmp(17), tmp(17), tmp(8), A.add)
            tt(tmp(13), tmp(13), tmp(18), A.add)
            tt(tmp(11), d1, tmp(19), A.add)
            lin(tmp(16), tmp(12), 400.0 * U)
            tt(tmp(13), tmp(17), tmp(13), A.subtract)
            tt(tmp(15), tmp(12), z(10), A.mult)
            tt(tmp(13), tmp(13), tmp(12), A.mult)
            for r in (1, 2) if last else (1,):
                tt(V("DA", r, 128, 16), tmp(15), z(9), A.add)
            tt(V("DA", 4, 128, 16), tmp(14), tmp(16), A.add)
            tt(V("DA", 0, 128, 16), tmp(13), tmp(11), A.add)
        else:
            ts(tmp(16), d1, 1.5 * U, A.is_gt, 400.0 * U, A.mult)
            lin(tmp(20), tmp(20), -1.0, 2.0)
            tt(tmp(16), tmp(16), tmp(8), A.add)
            tt(tmp(15), tmp(12), tmp(20), A.mult)
            tt(tmp(13), tmp(16), tmp(14), A.subtract)
            tt(V("DA", 1, 128, 16), tmp(15), tmp(23), A.add)
            tt(tmp(13), tmp(13), tmp(12), A.mult)
            tt(V("DA", 0, 128, 16), tmp(13), tmp(14), A.add)
        ne = 288 if t else 192
        back("RW", 16, "DW", 0)
        cp(IND(V("W1", 0, 432), O(OA)), V("RW", 16, 112))
        conv("RW", 96, "TP")
        scan(V("CS", 1, C + 1), V("W1", 0, C), V("W2", 0, C), 0.0, A.add, A.add)
        ts(O(OMM, 16), pick("TP", 96, 3), -1.0, A.mult)
        back("EV", 96, "DA", 0)
        tt(V("EB2", 16, 112), IND(V("CS", 0, 352), O(OA + 16)), V("VC", 0, 96), A.max)
        tt(V("EA", 16, 112), IND(V("CS", 0, 352), O(OMM)), V("EV", 96, 192), A.add)
        conv("EB2", 96, "TS")
        ts(O(OK_, 16), pick("TS", 96), 1024.0, A.mult)
        conv("EA", 96, "VA")
        ts(O(OK_ + 16, 16), IND(V("VA", 0, 224), O(PKE, 1)) if t else pick("VA", 96), 1024.0, A.mult)
        cp(IND(V("EW", 0, 4096), O(OK_)), V("VR", 0, 96))
        cp(IND(V("EW", 0, 4096), O(OK_ + 16, ne // 16 - 6)), V("EV", 288 - ne, 192))
        ts(V("KE", 0, H), V("EW", 0, H), 1.0, A.is_equal)
        act(V("KE", H, C), V("EW", H, C), AF.Relu, scale=V("cf", 90 if last else 93), bias=V("cf", 91 if last else 94))
        scan(V("FI", 16, 336), V("KE", 0, C), V("EW", 0, C), 1.0, A.mult, A.add)
        for h in (1, 0):
            conv("FI", H, "TK", 16 + H * h, 352 * h)
            ts(O(OL + 16 * h, 16), pick("TK", H, 1, 352 * h), -2.0, A.add)
            if last:
                ts(O(OPL + 16 * h, 16), pick("TK", H, 2, 352 * h), -2.0, A.add)
        if not last:
            gfill(V("W1", 0, C))
            gfill(V("EW", 0, C), 1)
        YQ, YS, NS = "YQ%d" % t, "YS%d" % t, "NS%d" % t
        if far:
            send(V(LA_, 48, 58), HO(OL, 1), "aq")
            arrive([V(LA_, 48, 58)], "aq")
            act(V(Fn, 224, 384), IND(V("NW", 0, 368), V(LA_, 48, 58)))
        for hf in (0, 1) if far else (1, 0):
            h = int(far and hf)
            for b in range(4):
                y, w = V("Y", 640 * hf + b, 640 * hf + 640, 4), IND(win(h, b, C, 688 if t else 368), V(LA_, 48, 58) if h else HO(OL, hf))
                ts(y, w, 0.5, A.mult) if b < 2 else lin(y, w, 0.5)
            if hf and not far:
                quant(YQ, YS, ("Y", 640), 0, H)
                send(U8V(V(ZQ, H, C)), U8V(V(YQ, 0, H)), "aq")
                send(V(ZS, H, C), V(YS, 0, H), "aq")
                arrive([V(ZQ, H, C), V(ZS, H, C)], "aq")
            else:
                quant(ZQ, ZS, ("Y", 640 * hf), H * hf, H)
        if not far:
            act(V(NS, 0, H), IND(V("NW", 0, 688), HO(OL, 1)))
            send(V(Fn, 224, 384), V(NS, 0, H), "af")
            arrive([V(Fn, 224, 384)], "af")
        for hf in range(2):
            a = H * hf
            if not hf:
                act(V(Fn, 32, 192), IND(V("NW", 0, 688 if t else 368), HO(OL, 0)))
            for b in range(4):
                mm("P%d" % (4 + b), "WQ", "WS", b, ZQ, ZS, a, H)
                act(V("RL", C * b + a, C * b + a + H), V("P%d" % (4 + b), 0, H), AF.Relu, scale=0.015625)
            for b in range(4):
                mm("P%d" % b, "EQ", "ES", b, ZQ, ZS, a, H)
                tt(V(Xn, 4 * a + b, 4 * a + 640, 4), V("P%d" % b, 0, H), V("RL", C * b + a, C * b + a + H), A.add)
            quant(XQn, XSn, (Xn, 4 * a), a, H)
            if not last:
                f0, w = fa_(hf), 352 * hf
                fr = V(Fn, f0 + H - 2, f0 - 1, -1)
                kw = V("cf", KW + 10 * hf, KW + 10 * hf + 16)
                lg = lambda i, n=16: V("lg", 128 * hf + 16 * i, 128 * hf + 16 * i + n)
                for nm, co in (("RB", "AR"), ("RA", "AL")):
                    scan(V(nm, a + H + 14, a + 15, -1), V(co, 0, H - 1), fr, 0.0, A.add, A.mult)
                conv(Fn, H, "TE", f0 - 1, w)
                conv("RB", H, "TQ", a + 16, w)
                lin(lg(0), pick("TE", H, 0, w), 1024.0)
                tt(lg(0), lg(0), kw, A.add)
                ts(HO(OSA, hf), lg(0, 10), 640.0, A.min)
                tt(lg(1), pick("TQ", H, 7, w), lg(0), A.add)
                ts(HO(OSB, hf), lg(1, 10), float(C), A.add, 640.0, A.min)
                lin(lg(2), pick("TE", H, 0, w), C - 1.0)
                tt(lg(2), lg(2), kw, A.add)
                cp(O(OMB + 10 * hf, 10), lg(2, 10))
                act(lg(3), pick("TQ", H, 7, w), AF.Sign)
                tt(lg(3), lg(3), kw, A.add)
                cp(O(OMF + 10 * hf, 10), lg(3, 10))
                pl, pr = ("P4", "P5") if hf else ("P2", "P3")
                mm(pl, "UL", "ULS", 0, XQn, XSn, a, H)
                mm(pr, "UR", "URS", 0, XQn, XSn, a, H)
                act(V("SW", a, a + H), V(pl, 0, H))
                cp(V("SW", C + a, C + a + H), V(pr, 0, H))
                act(V("SM", a, a + 64 + 96 * (1 - hf)), IND(V("SW", 0, 656), O(OSA + 16 * hf, 10 - 6 * hf)))
                if hf:
                    cp(V("SM", a + 64, a + H), IND(V("SW", 0, 656), O(OSA + 20, 6)))
                tt(V("M", 16 + a, 16 + a + H), IND(V("SW", 0, 656), HO(OSB, hf)), V("SM", a, a + H), A.max)
                act(V("SC", a, a + H), IND(V("SW", 0, 656), HO(OSB, hf)))
                conv("M", H, "TM", 16 + a, w)
                cp(V("MW", 16 * hf, 16 * hf + 16), pick("TM", H, 0, w))
            else:
                py = "P4" if hf else "P3"
                mm(py, "VQ", "VS", 0, XQn, XSn, a, H)
                dma("y", ("raw", T.oc[:, 4 * a:4 * a + 640]), U8V(V(XQn, a, a + H)))
                if hf:
                    for k in range(4):
                        dma("s" if k % 2 else "y", ("raw", T.osc[4 * k:4 * k + 4, :]), ("rows", slice(32 * k, 32 * k + 4), V("XS3", 0, C)))
                act(V("YO", a, a + H), V(py, 0, H))
                dma("s", ("raw", T.y[:, a:a + H]), V("YO", a, a + H))
                act(V("OLT", a, a + H), IND(V("PW", 0, 688), HO(OPL, hf)))
                act(V("OLT", C + a, C + a + H - 1), V("F3", fa_(hf), fa_(hf) + H - 1))
                if hf:
                    dma("y", ("raw", T.ol[:, :]), ("rows", slice(0, 128, 16), V("OLT", 0, 640)))
    emit(g, core, rank, T, topo, ops)


PLAN = {}
WAIT, DMA, FAR, SLOW = 225.0, 2500.0, 2000.0, 1.2
START, LONG, TOL = 1500.0, 450.0, 45.0
PASSES, MOVES = 5, 1200
GATH, SCAT, PE = 1.45, 3.7, 1.1


def link(ops):
    hist = {}
    for i, o in enumerate(ops):
        dep, after = set(), set()
        rd = o["rd"] if o["kind"] != "r" else touched(o["a"][1])
        for nm, m in rd:
            psum = SCRATCH[nm][0] == "psum"
            dep.update(j for j, w, m2 in hist.get(nm, []) if m2 & m and (w or psum and ops[j]["e"] != o["e"]))
        for nm, m in o["wr"]:
            (after if o["x"] == "acc" else dep).update(j for j, w, m2 in hist.get(nm, []) if m2 & m)
        if o["kind"] == "a":
            after.update(j for j in range(i) if ops[j]["kind"] == "r" and ops[j]["x"][0] == o["x"][0])
        o["dep"], o["after"] = dep, after
        for nm, m in o["wr"]:
            hist[nm] = [(j, w, m2 & ~m) for j, w, m2 in hist.get(nm, []) if m2 & ~m] + [(i, True, m)]
        if o["kind"] != "r":
            for nm, m in rd:
                hist.setdefault(nm, []).append((i, False, m))


def cost(o, GATH=GATH, SCAT=SCAT, PE=PE):
    if o["kind"] in "ad":
        return {"a": 0.0, "d": 60.0}[o["kind"]]

    def width(x):
        if x[0] == "ind":
            return 16 * width(x[2])
        return len(range(x[2], x[3] if x[3] != "end" else -1, x[4])) if x[0] == "ap" else width(x[-1])

    if o["kind"] == "r":
        x = o["a"][1]
        return 16 * (50 + width(x) * (4 if x[0] == "u8" else 1 if SCRATCH[x[1]][2] == U8 else 2) / 16)

    a = [x for x in o["a"] if isinstance(x, tuple)]
    n = max(width(x) for x in a)
    if a[0][0] == "ind":
        return 50 + SCAT * n
    if any(x[0] == "ind" for x in a):
        return 60 + GATH * width(a[0])
    if o["m"] == "quantize_mx":
        return 12 + 0.22 * n
    if o["m"] == "iota":
        return 130 + 1.66 * n
    if o["m"] == "matmul_mx":
        return PE * (width(a[0]) + 16)
    if o["m"] == "tensor_tensor":
        n *= 1 + all(SCRATCH[x[1]][0] != "psum" for x in a)
    elif o["m"] not in ("activation", "tensor_reduce") and all(SCRATCH[x[1]][2] == BF for x in a if width(x) > 1):
        n /= 2
    return 0.83 * max(n, 64)


def sweep(eng, c, nxt, rank):
    n = len(c)
    left, ready, end, pool, order = [0] * n, [0.0] * n, [0.0] * n, {e: [] for e in eng}, []
    for i in range(n):
        for k, w in nxt[i]:
            left[k] += 1
    for i in range(n):
        if not left[i]:
            pool[eng[i]].append(i)
    free = {e: 0.0 for e in pool}
    while len(order) < n:
        now, e = min((max(free[e], min(ready[i] for i in p)), e) for e, p in pool.items() if p)
        p = sorted(pool[e], key=lambda i: -rank[i])
        best = None
        for x, i in enumerate(p):
            if ready[i] <= now and all(now + c[i] + rank[k] <= TOL + max(ready[k] + rank[k], ready[k] + c[k] + rank[i]) for k in p[:x] if ready[k] > now):
                best = i
                break
        if best is None:
            best = min((i for i in p if ready[i] > now), key=lambda i: (ready[i], -rank[i]))
        pool[e].remove(best)
        order.append(best)
        free[e] = end[best] = max(now, ready[best]) + c[best]
        for k, w in nxt[best]:
            ready[k] = max(ready[k], free[e] + w)
            left[k] -= 1
            if not left[k]:
                pool[eng[k]].append(k)
    return order, end


def schedule(ops):
    link(ops)
    n = len(ops)
    eng = [o["e"] for o in ops]
    c = [SLOW * cost(o) for o in ops]
    lag = [{"d": DMA, "r": FAR}.get(o["kind"], 0.0) for o in ops]
    nxt, prv = [[] for o in ops], [[] for o in ops]
    for i, o in enumerate(ops):
        for j, w in [(j, lag[j] + WAIT) for j in o["dep"]] + [(j, lag[j]) for j in o["after"]]:
            nxt[j].append((i, w))
            prv[i].append((j, w))
    rank = [0.0] * n
    for i in range(n - 1, -1, -1):
        rank[i] = c[i] + max([w + rank[k] for k, w in nxt[i]] + [lag[i]])
    best, soon = None, [1e6 if o["kind"] == "d" and not o["dep"] else o.get("soon", 0.0) for o in ops]

    near = [[(j, w - FAR * (ops[j]["kind"] == "r")) for j, w in p] for p in prv]
    ends = [([cost(o, 1.25, 2.9, 0.9) for o in ops], 1.0), ([1.4 * cost(o, 1.66, 4.5, 1.1) for o in ops], 0.75)]

    def play(rank):
        order, first = sweep(eng, c, nxt, [r + s for r, s in zip(rank, soon)])
        total, held = 0.0, []
        for ck, weight in ends:
            free, end, by, dma = {}, [0.0] * n, [-1] * n, 0.0
            for i in order:
                at, by[i] = max([free.get(eng[i], (0.0, -1))] + [(end[j] + w, j) for j, w in near[i]])
                if ops[i]["kind"] == "r":
                    end[i] = dma = max(at + START, dma) + ck[i]
                    free[eng[i]] = (at + 300.0, i)
                else:
                    end[i] = at + ck[i]
                    free[eng[i]] = (end[i], i)
            i = max(range(n), key=lambda q: end[q])
            total += end[i] * weight
            while by[i] >= 0:
                if all(by[i] != j for j, w in prv[i]):
                    held.append((by[i], i))
                i = by[i]
        return total, held, order, rank, first

    for _ in range(PASSES):
        now = play(rank)
        if best is None or now[0] < best[0]:
            best = now
        rank = sweep(eng, c, prv, now[4])[1]
    tried = set()
    for _ in range(MOVES):
        left = [(j, i, d) for j, i in best[1] for d in (0, 1) if (j, i, d) not in tried and (d or best[3][j] <= best[3][i])]
        if not left:
            break
        j, i, d = left[0]
        tried.add(left[0])
        rank = list(best[3])
        rank[j] = min(rank[j], rank[i]) - 300 if d else rank[j] + 1500
        now = play(rank)
        if now[0] < best[0] - 1:
            best = now
    PLAN["end"] = best[4]
    return best[2]


def emit(g, core, rank, T, topo, ops):
    qs = {"v": g.vector, "s": g.scalar, "t": g.tensor, "g": g, "y": g.sync}

    def ap(x, rows=slice(None)):
        if not isinstance(x, tuple):
            return x
        if x[0] == "raw":
            return x[1]
        if x[0] == "ap":
            return T[x[1]][rows, slice(x[2], None if x[3] == "end" else x[3], x[4] if x[4] != 1 else None)]
        if x[0] == "rows":
            return ap(x[2], x[1])
        if x[0] == "ind":
            return ap(x[1]).indirect(ap(x[2]))
        return ap(x[1]).bitcast(dt.uint8 if x[0] == "u8" else dt.uint32)

    def engines(src):
        es = [topo.engines(src, T.cores[T.rank_of(src) ^ s]) for s in STEP]
        return [e for e in es[0] if all(e in x for x in es)]

    if "order" not in PLAN:
        PLAN["order"] = schedule(ops)
    ops = [ops[i] for i in PLAN["order"]]
    end = [PLAN["end"][i] for i in PLAN["order"]]
    link(ops)
    line = {}
    for i, o in enumerate(ops):
        o["i"], o["at"] = i, len(line.setdefault(o["e"], []))
        line[o["e"]].append(o)
    known = {e: {} for e in qs}
    for o in ops:
        o["clock"] = {}
        if o["kind"] == "a":
            continue
        kn = known[o["e"]]
        o["need"] = []
        for j in sorted(o["dep"], reverse=True):
            p = ops[j]
            key = p["e"] if p["kind"] == "c" else ("x", j)
            if kn.get(key, -1) >= j:
                continue
            if p["kind"] == "c":
                j = max([j] + [k for q in line[o["e"]][o["at"] + 1:o["at"] + 60] for k in q["dep"]
                               if k < o["i"] and ops[k]["kind"] == "c" and ops[k]["e"] == key and end[k] + LONG <= end[o["i"]] - SLOW * cost(o)])
                p = ops[j]
            o["need"].append(j)
            p["sig"] = True
            kn[key] = j
            for k2, v2 in p["clock"].items():
                if kn.get(k2, -1) < v2:
                    kn[k2] = v2
        o["clock"] = dict(kn)
    count = {e: 0 for e in ENG}
    nd, sent, final = 0, 0, []
    v = g.vector
    calls = {"tensor_scalar": v.tensor_scalar, "tensor_tensor": v.tensor_tensor, "tensor_copy": v.tensor_copy, "memset": v.memset,
             "transpose": v.transpose, "tensor_tensor_scan": v.tensor_tensor_scan, "quantize_mx": v.quantize_mx,
             "tensor_reduce": v.tensor_reduce, "activation": g.scalar.activation, "matmul_mx": g.tensor.matmul_mx, "iota": g.iota}
    for o in ops:
        if o["kind"] == "a":
            nm, t, n = o["x"]
            o["wait"] = (nm, n * len(engines(T.cores[rank ^ STEP[t]])))
            final.append(o["wait"])
            continue
        q = qs[o["e"]]
        for j in o["need"]:
            q.wait_ge(T.sem[ops[j]["wait"][0]], ops[j]["wait"][1])
        a = [ap(x) for x in o["a"]]
        if o["kind"] == "r":
            dst = T.cores[rank ^ STEP[o["x"][1]]]
            rid, pid = topo.addr(dst, core)
            g.remote_dma(a[0], a[1], T.sem[o["x"][0]], T.sem.sent, pid, rid, sum(1 << e for e in engines(core)))
            sent += len(engines(core))
        elif o["kind"] == "d":
            o["wait"] = ("d%d" % nd, 16)
            nd += 1
            q.dma_start(a[0], a[1]).then_inc(T.sem[o["wait"][0]], 16)
            final.append(o["wait"])
        else:
            ins = calls[o["m"]](*a, **{k: ap(x) for k, x in o["kw"].items()})
            if o.get("sig"):
                count[o["e"]] += 1
                o["wait"] = ("e" + o["e"], count[o["e"]])
                ins.then_inc(T.sem[o["wait"][0]], 1)
    for nm, n in final + [("sent", sent)] + [("e" + e, count[e]) for e in ENG if count[e]]:
        g.wait_ge(T.sem[nm], n)
